import numpy as np, ml_dtypes
CORES = [6,15,38,47]
N = 4
import mx_ref
BF = ml_dtypes.bfloat16
def gcols(t, e):
    v = np.concatenate([t.reshape(8, 16, -1, 4), np.zeros((8, 16, 1, 4), BF)], axis=2)
    return np.ascontiguousarray(np.stack([v[g][:, e[g]] for g in range(8)])).reshape(128, -1)
def tile(rs):
    return np.stack(rs, axis=2).reshape(128, -1).astype(BF)
def pick(q, e):
    c = np.concatenate([q[0].reshape(128, -1, 4), np.zeros((128, 1, 4), np.uint8)], axis=1); s = np.concatenate([q[1], np.ones((16, 1), np.uint8)], axis=1)
    return (np.ascontiguousarray(c[:, e].reshape(128, -1)), np.ascontiguousarray(s[:, e]))
def join(*qs):
    return (np.concatenate([q[0] for q in qs], axis=1), np.concatenate([q[1] for q in qs], axis=1))
def put(q, e, v):
    c, s = q[0].reshape(128, -1, 4).copy(), q[1].copy(); c[:, e] = v[0].reshape(128, -1, 4); s[:, e] = v[1]
    return (c.reshape(128, -1), s)
def pk(c, s):
    return (np.ascontiguousarray(c), mx_ref.live(s))
def emit(q):
    return q[0], q[1]
def packed(v, rng):
    q = [mx_ref.quantize(np.ascontiguousarray(v[r])) for r in range(N)]
    return np.stack([a for a, b in q]), np.stack([mx_ref.plane(b, rng) for a, b in q])
def values_of_codes():
    e, c = np.zeros((128, 128, 4), np.float32), np.zeros((128, 2, 4), np.uint8)
    e[np.arange(128), np.arange(128), 0] = 1
    c[:127, :, 0] = np.arange(256).reshape(2, 128).T[:127]
    return mx_ref.matmul(mx_ref.quantize(e.reshape(128, 512).astype(BF)), (c.reshape(128, 8), np.full((16, 2), 127, np.uint8))).T.reshape(-1).astype(np.float64)
CODE_VALUE, SCALE_VALUE = values_of_codes(), 2.0 ** (np.arange(256) - 127.0)
def decode(q):
    return (CODE_VALUE[q[0]].reshape(16, 8, -1, 4) * SCALE_VALUE[q[1]][:, None, :, None] + 0.0).reshape(128, -1).astype(np.float32)
def f(rng, *shape):
    return mx_ref.flush((rng.standard_normal(shape, dtype=np.float32) * np.exp2(rng.integers(-2, 3, shape[:-1] + (1,)))).astype(BF))
def wide(rng, *shape, cols=0):
    v = rng.standard_normal(shape, dtype=np.float32) * np.exp2(rng.integers(-12, 13, shape)).astype(np.float32)
    if cols: v *= np.repeat(np.exp2(rng.integers(-cols, cols + 1, shape[:-2] + (1, shape[-1] // 4))) * (rng.random(shape[:-2] + (1, shape[-1] // 4)) > 0.0625), 4, axis=-1).astype(np.float32)
    return mx_ref.flush(v.astype(BF))
C, K, DEP, R = 320, 160, 40, 3
SOURCE = [7, 0, 1, 1, 2, 2, 3, 3]
LEVEL = [0, 1, 2, 2, 3, 3, 3, 3]
ITEM = 8 * (np.arange(C) % DEP) + np.arange(C) // DEP
def big(v):
    v = v.astype(np.float32)
    v[np.abs(v) < np.float32(2.0 ** -16)] = 0
    return v.astype(BF)
def numbers_of(rng):
    return {"x": big(f(rng, N, 128, 4 * C)), "u": np.array(f(rng, N, 128, 512)), "v": np.array(f(rng, N, 128, 512))}
def layers(rng):
    return big(f(rng, N, 128, 2048).astype(np.float32) * np.float32(0.5)).reshape(N, 8, 16, 4, 8, 16, 4)
def weights(rng, w):
    c, p = packed(np.ascontiguousarray(w).reshape(N, 128, 2048), rng)
    return {"wc": c, "ws": p}
def own_bits(u):
    for b in range(3): u[:, :, b::16] = 0
    for h in range(0, 128, 16):
        for b in range(3): u[:, h, h + b, b] = 1
def setup_inputs(rng):
    return {**numbers_of(rng), **weights(rng, layers(rng))}
def setup_inputs_ties(rng):
    d = numbers_of(rng)
    e = rng.permutation(N)
    k = rng.integers(-1, 2, (N, 8, C, 3)).astype(np.float32)
    k[e[0]] = 0
    k[e[1]] = 1
    for g in range(8): k[e[2], g, :, 0] = 2.0 * (LEVEL[g] % 2) - 1.0
    x = d["x"].reshape(N, 8, 16, C, 4)
    x[:, :, :8] = 0
    x[:, :, 0, :, :3] = k.astype(BF)
    u = d["u"].reshape(N, 128, 128, 4)
    own_bits(u)
    w = layers(rng)
    w[:, :, :, :, :, :8] = 0
    return {"x": x.reshape(N, 128, 4 * C), "u": u.reshape(N, 128, 512), "v": d["v"], **weights(rng, w)}
def setup_inputs_near(rng):
    d = numbers_of(rng)
    x = d["x"].reshape(N, 8, 16, C, 4)
    u = d["u"].reshape(N, 128, 128, 4)
    o = rng.permutation(N) % 4
    x[:, :, :8] = 0
    for b in range(3): u[:, :, b::16] = 0
    for r in range(N):
        a = rng.integers(-1, 2, (8, C, 3)).astype(np.float32)
        b = np.where(rng.random((8, C, 3)) < 0.75, -a, rng.integers(-1, 2, (8, C, 3))).astype(np.float32)
        k = np.float32(2.0 ** -27 if o[r] < 2 else 1.0)
        a, b = a * k, b * k
        for g in rng.permutation(8)[:4]: a[g, rng.integers(C)] = 2.0 ** 18 * rng.choice([-1.0, 1.0], 3)
        x[r, :, 0, :, :3] = a.astype(BF)
        x[r, :, 1, :, :3] = b.astype(BF)
        m = 2.0 ** -30 if o[r] % 2 == 0 else 1.0
        for h in range(0, 128, 16):
            for t in range(3):
                u[r, h, h + t, t] = 1.125 * m
                u[r, h + 1, h + t, t] = m
    w = layers(rng)
    w[:, :, :8] = 0
    w[:, :, :, :, :, :8] = 0
    return {"x": x.reshape(N, 128, 4 * C), "u": u.reshape(N, 128, 512), "v": d["v"], **weights(rng, w)}
def setup_inputs_late(rng):
    d = numbers_of(rng)
    s = rng.integers(6, 8, (N, 8, 8, DEP))
    for g in range(8):
        if g: s[:, g, :, 0] = LEVEL[g] - 1
        s[:, g, :, -1] = LEVEL[g]
    s[:, 7, 7] = 0
    s[:, 7, 7, -1] = 2
    e = int(rng.integers(N))
    s[e] = 7
    for g in range(8):
        if LEVEL[g] > 0: s[e, g, :, 0] = 7 - LEVEL[g]
        if LEVEL[g] < 3: s[e, g, :, -1] = 6 - LEVEL[g]
    s[e, 2:4, :7, -1] = 2
    for h in (0, 1, 6, 7):
        s[e, 4:, h, 0] = 2
        s[e, 4:, h, 1] = 3
    s[e, 4:, 5, 1] = 6
    s = s.reshape(N, 8, C)
    x = d["x"].reshape(N, 8, 16, C, 4)
    x[:, :, :8] = 0
    x[:, :, 0, :, :3] = (2.0 * ((s[..., None] >> np.array([2, 1, 0])) & 1) - 1.0).astype(np.float32).astype(BF)
    k = (1.0 + (2 * rng.integers(0, 64, (N, 8, 8, C, 4)) + 1) / 128.0) * np.exp2(-1.0 * rng.integers(8, 15, (N, 8, 8, C, 4))) * rng.choice([-1.0, 1.0], (N, 8, 8, C, 4))
    k[:, :, 0, :, 0] = 1.96875
    x[:, :, 8:] = k.astype(np.float32).astype(BF)
    u = d["u"].reshape(N, 128, 128, 4)
    own_bits(u)
    w = layers(rng)
    w[:, :, :, :, :, :8] = 0
    return {"x": x.reshape(N, 128, 4 * C), "u": u.reshape(N, 128, 512), "v": d["v"], **weights(rng, w)}
def setup_inputs_ends(rng):
    o = rng.permutation(N)
    x = rng.choice([-1.0, 1.0], (N, 8, 1, C, 1)) * np.ones((1, 1, 16, 1, 4))
    u, v = rng.choice([-1.0, 1.0], (N, 128, 512)), rng.choice([-1.0, 1.0], (N, 128, 512))
    w = np.zeros((N, 128, 2048), np.float32)
    for r in range(N):
        if o[r] == 0: x[r] = 1.0
        if o[r] == 3: x[r] = -1.0
        if o[r] in (0, 3): u[r] = 1.0
        x[r] *= 2.0 ** 19 if o[r] % 2 == 0 else 2.0 ** -27
        u[r] *= 2.0 ** 30 if o[r] % 4 < 2 else 2.0 ** -30
        v[r] *= 2.0 ** 30 if o[r] % 4 in (0, 3) else 2.0 ** -30
        w[r] = (2.0, -2.0, 0.0)[o[r] % 3]
    return {"x": x.astype(np.float32).reshape(N, 128, 4 * C).astype(BF), "u": u.astype(np.float32).astype(BF), "v": v.astype(np.float32).astype(BF), **weights(rng, w.astype(BF))}
def setup_inputs_spread(rng):
    d = setup_inputs(rng)
    d["x"] = big(wide(rng, N, 128, 4 * C, cols=3))
    return d
def check_inputs(d):
    b = []
    for k, m in (("x", 2.0 ** 19), ("u", 2.0 ** 30), ("v", 2.0 ** 30)):
        a = np.abs(d[k].astype(np.float32))
        if not (np.isfinite(a).all() and ((a == 0) | (a >= 2.0 ** -30) & (a <= m)).all()): b.append("a value of " + k)
    none, least, most = [emit(mx_ref.quantize(np.full((128, 16), k, np.float32).astype(BF)))[1][0, 0] for k in (0.0, 2.0 ** -30, 2.0 ** 30)]
    for r in range(N):
        if ((d["wc"][r] == 0x7F) | (d["wc"][r] == 0xFF)).any(): b.append("wc: a code that is no number")
        s = mx_ref.live(d["ws"][r])
        if ((s != none) & ((s < least) | (s > most))).any(): b.append("ws: a scale out of range")
        a = np.abs(decode(pk(d["wc"][r], d["ws"][r])).astype(np.float64)).reshape(128, 512, 4)
        if not (np.sum(a, axis=(0, 2)) <= 1024).all(): b.append("W: a column that adds up to more than 1024")
    return b
def times(sym, wait):
    sym, wait = sym.reshape(8, DEP), wait.reshape(8, DEP)
    t, last = np.zeros((8, DEP), np.int64), np.zeros(8, np.int64)
    for i in range(DEP):
        last = np.maximum(last, wait[:, i]) + (1 + sym[:, i])
        t[:, i] = last
    return t.reshape(C)
def orders(sym):
    o, b = np.zeros((8, C), np.int64), np.zeros((8, K), np.int64)
    first, least = np.full((8, 8), -1), np.zeros((8, 8), np.int64)
    for g in range(8):
        e = SOURCE[g]
        t = times(sym[g], least[e][sym[g]] if g > 0 else np.zeros(C, np.int64))
        o[g] = np.argsort(t, kind="stable")
        for s in range(8):
            p = np.flatnonzero(sym[g][o[g]] == s)
            if len(p) > 0:
                first[g, s] = o[g, p[0]]
                least[g, s] = t[o[g, p[0]]]
        l = o[g, :K]
        p = first[e][sym[g][l]] if g > 0 else l
        b[g] = np.where(p < 0, l, p)
    return o, b
def reference(x, u, v, wc, ws):
    qu = [mx_ref.quantize(u[r]) for r in range(N)]
    lay = [pk(wc[r], ws[r]) for r in range(N)]
    now = [x[r] for r in range(N)]
    order = np.zeros((N, 8, C), np.int64)
    for t in range(R):
        stay, sent = [], []
        for r in range(N):
            q = mx_ref.quantize(now[r])
            full = decode(q)
            s = mx_ref.matmul(qu[r], q)
            order[r], mate = orders(4 * (s[::16] > 0) + 2 * (s[1::16] > 0) + (s[2::16] > 0))
            a = full.reshape(8, 16, C, 4)
            z = np.stack([(a[g][:, order[r, g, :K]] + a[SOURCE[g]][:, mate[g]]) * np.float32(0.5) for g in range(8)])
            sent.append(mx_ref.quantize(np.ascontiguousarray(z.reshape(128, 4 * K).astype(BF))))
            stay.append(gcols(full.astype(BF), order[r][:, K:]))
        for r in range(N):
            q = sent[r - 1]
            d = decode(q)
            h = tile([mx_ref.matmul(pick(lay[r], np.arange(128 * b, 128 * b + 128)), q) * np.float32(0.0078125) + d[:, b::4] for b in range(4)])
            items = np.concatenate([stay[r], h], axis=1).reshape(128, C, 4)
            now[r] = np.ascontiguousarray(items[:, ITEM].reshape(128, 4 * C))
    y, op = np.zeros((N, 128, C), np.float32), np.zeros((N, 8, C), np.float32)
    oc, osc = np.zeros((N, 128, 4 * C), np.uint8), np.zeros((N, 16, C), np.uint8)
    for r in range(N):
        q = mx_ref.quantize(now[r])
        y[r] = mx_ref.matmul(mx_ref.quantize(v[r]), q)
        op[r] = order[r]
        oc[r], osc[r] = emit(q)
    return {"y": y, "op": op, "oc": oc, "osc": osc}

@@ -1,0 +1,549 @@
+from concourse.mybir import dt, AluOpType as O, AxisListType, ActivationFunctionType as AF
+
+NS = 10
+NV = 20 - NS
+HUGE = 1.0e25
+BIG = float(2 ** 20)
+F4 = "float8_e4m3fn_x4"
+
+
+def _decl():
+    d = {}
+
+    def sb(names, n, t):
+        for k in names.split():
+            d[k] = ("sbuf", [128, n], t)
+    sb("xt fp f2", 1280, "bfloat16")
+    sb("xk xh zt pz sj", 640, "bfloat16")
+    sb("uv", 1024, "bfloat16")
+    sb("zz", 512, "bfloat16")
+    sb("ct et", 2048, "bfloat16")
+    sb("fl", 1408, "bfloat16")
+    sb("fab", 960, "bfloat16")
+    sb("scn", 160 * NV, "bfloat16")
+    sb("idx ix", 256, "bfloat16")
+    sb("tg", 1536, "bfloat16")
+    for k, n in (("u", 128), ("up", 128), ("v", 128), ("w", 512), ("e", 512), ("h", 512), ("g", 512), ("a", 512), ("b", 512), ("c", 512), ("f", 352), ("n", 320)):
+        d["q" + k] = ("sbuf", [128, n], F4)
+        d["s" + k + "_p"] = ("sbuf", [128, n], "uint8")
+    for r in range(4):
+        d["q%d" % r] = ("sbuf", [128, 320], F4)
+        d["s%d_p" % r] = ("sbuf", [128, 320], "uint8")
+    for r in range(3):
+        for k in ("z", "l"):
+            d["q%s%d" % (k, r)] = ("sbuf", [128, 160], F4)
+            d["s%s%d_p" % (k, r)] = ("sbuf", [128, 160], "uint8")
+    sb("par th hrow si0 si1 ccol d0o dow vrow yo oprow tlo", 320, "float32")
+    sb("c0 d0h tt vv dst0 dst1 dst2 ast0 ast1 ast2 tl", 160, "float32")
+    sb("kap", 352, "float32")
+    sb("kt", 672, "float32")
+    sb("ex", 48, "float32")
+    sb("my acc", 20, "float32")
+    sb("win tw", 640, "float32")
+    sb("mcol", 8, "float32")
+    sb("top mb tb", 32, "float32")
+    sb("cf rf", 64, "float32")
+    sb("ci mi wt w8 ft ub", 16, "int32")
+    sb("fx lx", 128, "int32")
+    sb("rx", 32, "int32")
+    sb("nx", 64, "int32")
+    sb("off12 offd offs offo nat", 32, "uint16")
+    sb("ll bl kl ulist", 16, "uint16")
+    sb("ku", 320, "uint16")
+    for b in range(8):
+        d["pb%d" % b] = ("psum", [128, 512], "float32")
+    return d
+
+
+SCRATCH = _decl()
+SEMAPHORES = ["sV", "sS", "sP", "sG", "dx", "du", "dw", "dws", "dv", "arr0", "arr1", "arr2", "loc", "doy", "doa"]
+
+
+def rank_program(g, core, T, topo):
+    rank = T.rank_of(core)
+    if rank is None:
+        return
+    nxt = T.cores[(rank + 1) % len(T.cores)]
+    queue = {"V": g.vector, "S": g.scalar, "P": g.tensor, "G": g, "Y": g.sync}
+    own = {"V": "sV", "S": "sS", "P": "sP", "G": "sG"}
+    count = {}
+    clock = {}
+    known = {k: {} for k in queue}
+    hist = {}
+
+    def norm(a):
+        if isinstance(a, str):
+            a = (a, 0, 1 << 20)
+        if a[0][:2] == "pb":
+            return (a[0], 0, 1 << 20)
+        return a
+
+    def accesses(reads, writes):
+        r = [norm(a) for a in reads]
+        return [(a, "p" if a[0][:2] == "pb" else "r") for a in r] + [(norm(a), "w") for a in writes]
+
+    def waits(q, acc):
+        need = {}
+        for (b, lo, hi), kind in acc:
+            for e in hist.get(b, []):
+                if e[0] >= hi or e[1] <= lo or (kind == "r" and e[2] == "r"):
+                    continue
+                if b[:2] == "pb" and kind == ("w" if e[2] == "w" else "p") and own.get(q) == e[3]:
+                    continue
+                need[e[3]] = max(need.get(e[3], 0), e[4])
+        kn = known[q]
+        for s in sorted(need, key=lambda s: -need[s]):
+            if kn.get(s, 0) >= need[s]:
+                continue
+            queue[q].wait_ge(T.sem[s], need[s])
+            for k, v in clock.get((s, need[s]), {}).items():
+                kn[k] = max(kn.get(k, 0), v)
+            kn[s] = max(kn.get(s, 0), need[s])
+
+    def record(q, sem, n, acc):
+        count[sem] = count.get(sem, 0) + n
+        v = count[sem]
+        clock[(sem, v)] = dict(known[q])
+        for (b, lo, hi), kind in acc:
+            h = hist.setdefault(b, [])
+            if kind == "r":
+                h[:] = [e for e in h if not (e[2] == "r" and e[3] == sem and e[0] >= lo and e[1] <= hi)]
+            else:
+                h[:] = [e for e in h if not (e[0] >= lo and e[1] <= hi)]
+            h.append([lo, hi, kind, sem, v])
+
+    def op(q, call, reads, writes):
+        acc = accesses(reads, writes)
+        waits(q, acc)
+        call(queue[q]).then_inc(T.sem[own[q]], 1)
+        record(q, own[q], 1, acc)
+
+    def dma(q, out, in_, reads, writes, sem):
+        acc = accesses(reads, writes)
+        waits(q, acc)
+        queue[q].dma_start(out, in_).then_inc(T.sem[sem], 16)
+        record(q, sem, 16, acc)
+
+    def V(call, reads, writes):
+        op("V", call, reads, writes)
+
+    def ts(out, in0, s1, s2, o0, o1, reads, writes):
+        if o1 is None:
+            V(lambda v: v.tensor_scalar(out, in0, s1, None, o0), reads, writes)
+        else:
+            V(lambda v: v.tensor_scalar(out, in0, s1, s2, o0, o1), reads, writes)
+
+    def tt(out, a, b, o, reads, writes):
+        V(lambda v: v.tensor_tensor(out, a, b, o), reads, writes)
+
+    def fill(out, val, writes):
+        V(lambda v: v.memset(out, val), [], writes)
+
+    def act(out, in_, f, reads, writes, **kw):
+        op("S", lambda s: s.activation(out, in_, f, **kw), reads, writes)
+
+    def iota(out, pat, base, cm, writes, f=True):
+        if f:
+            op("G", lambda e: e.iota(out, pat, base, cm, allow_small_or_imprecise_dtypes=True), [], writes)
+        else:
+            op("G", lambda e: e.iota(out, pat, base, cm), [], writes)
+
+    def quant(k, a, b, tile, lo, hi):
+        qn, sn = "q" + k, "s" + k + "_p"
+        V(lambda v: v.quantize_mx(T[qn][:, a:b], T[sn][:, a:b], T[tile][:, lo:hi]), [(tile, lo, hi)], [(qn, a, b), (sn, a, b)])
+
+    def mm(bank, n, k, a, m, b, start=True, stop=True):
+        qa, sa, qb, sq = "q" + k, "s" + k + "_p", "q" + m, "s" + m + "_p"
+        op("P", lambda t: t.matmul_mx(T["pb%d" % bank][:, 0:n], T[qa][:, a:a + 128], T[sa][:, a:a + 128], T[qb][:, b:b + n], T[sq][:, b:b + n], start, stop),
+           [(qa, a, a + 128), (sa, a, a + 128), (qb, b, b + n), (sq, b, b + n)], ["pb%d" % bank])
+
+    def between(todo):
+        if todo:
+            todo.pop(0)()
+
+    dma("Y", T.xt[:], T.x[:], [], ["xt"], "dx")
+    dma("S", T.uv[:, 0:512], T.u[:], [], [("uv", 0, 512)], "du")
+    dma("Y", T.qw[:].bitcast(dt.uint8), T.wc[:], [], ["qw"], "dw")
+    dma("Y", T["sw_p"][:], T.ws[:], [], ["sw_p"], "dws")
+    dma("Y", T.uv[:, 512:1024], T.v[:], [], [("uv", 512, 1024)], "dv")
+
+    fill(T.zz[:], 0.0, ["zz"])
+    fill(T.tg[:, 256:512], -1.0, [("tg", 256, 512)])
+    iota(T.ci[:, 0:1], [[1, 1]], 0, 1, [("ci", 0, 1)], f=False)
+    iota(T.ub[:, 0:8], [[16, 8]], 0, 0, ["ub"], f=False)
+    iota(T.tg[:, 0:128], [[0, 4], [100, 2], [0, 16]], 0, 0, [("tg", 0, 128)])
+    iota(T.tg[:, 128:256], [[0, 4], [100, 2], [0, 16]], -100, 0, [("tg", 128, 256)])
+    for base, jj, code in ((256, 0, 8), (384, 1, 16)):
+        iota(T.tg[:, base + jj:base + 128:32], [[1, 2], [0, 2]], code, 0, [("tg", base, base + 64)])
+        iota(T.tg[:, base + jj + 2:base + 128:32], [[1, 4]], code, 0, [("tg", base + 64, base + 128)])
+    iota(T.par[:], [[0, 10], [1, 2], [0, 16]], 0, 0, ["par"])
+    iota(T.c0[:], [[64, 4], [1, 40]], -1, 0, ["c0"])
+    for h in range(2):
+        for k in range(2):
+            lo = 512 + 128 * h + 64 * k
+            iota(T.tg[:, lo:lo + 64], [[0, 2], [100, 2], [0, 16]], k - 100 * h, 0, [("tg", lo, lo + 64)])
+    for h in range(2):
+        lo = 768 + 128 * h
+        iota(T.tg[:, lo:lo + 128], [[1, 4], [100, 2], [0, 16]], -100 * h, 0, [("tg", lo, lo + 128)])
+    iota(T.tg[:, 1024:1152], [[1, 8], [0, 16]], 0, 0, [("tg", 1024, 1152)])
+    fill(T.tg[:, 1152:1536], -1.0, [("tg", 1152, 1536)])
+    for i, (base, jj, code) in enumerate(((1152, 0, 8), (1152, 1, 17), (1280, 0, 9), (1408, 1, 16))):
+        iota(T.tg[:, base + jj:base + 128:32], [[2, 4]], code, 0, [("tg", 1152 + 96 * i, 1248 + 96 * i)])
+    iota(T.ix[:, 0:128], [[1, 128]], 0, 0, [("ix", 0, 128)])
+    iota(T.ix[:, 128:256], [[16, 4], [0, 2], [1, 16]], 0, 0, [("ix", 128, 256)])
+    iota(T.ix[:, 128:144], [[1, 16]], 112, 0, [("ix", 128, 256)])
+    iota(T.hrow[:], [[1, 8], [0, 40]], 0, 0, ["hrow"])
+    iota(T.si0[:], [[1, 320]], 1, 0, ["si0"])
+    iota(T.si1[:], [[1, 8], [8, 40]], 1, 0, ["si1"])
+    iota(T.ccol[:], [[1, 320]], 0, 0, ["ccol"])
+    iota(T.nx[:, 0:20], [[16, 20]], 0, 0, [("nx", 0, 20)], f=False)
+    for n, w in (("ct", 512), ("fl", 352)):
+        for b in range(4):
+            act(T[n][:, w * b:w * b + w], T.zz[:, 0:w], AF.Copy, ["zz"], [(n, w * b, w * b + w)])
+
+    def ci(i):
+        return T.ci[:, i:i + 1]
+
+    def cf(i):
+        return T.cf[:, i:i + 1]
+
+    def C(i):
+        return ("ci", i, i + 1)
+
+    def K(i):
+        return ("cf", i, i + 1)
+    RK, SG, HF, BK, GR = 1, 2, 3, 4, 5
+    ts(ci(RK), ci(0), 15, None, O.bitwise_and, None, [C(0)], [C(RK)])
+    ts(ci(GR), ci(0), 4, None, O.arith_shift_right, None, [C(0)], [C(GR)])
+    ts(ci(SG), ci(0), 7, None, O.bitwise_and, None, [C(0)], [C(SG)])
+    ts(ci(HF), ci(0), 16, 4, O.bitwise_and, O.arith_shift_right, [C(0)], [C(HF)])
+    ts(ci(BK), ci(0), 5, None, O.arith_shift_right, None, [C(0)], [C(BK)])
+    ts(cf(0), ci(RK), 3.0, None, O.is_ge, None, [C(RK)], [K(0)])
+    ts(cf(1), ci(RK), 6.0, None, O.is_ge, None, [C(RK)], [K(1)])
+    ts(cf(9), ci(RK), 9.0, 100.0, O.is_ge, O.mult, [C(RK)], [K(9)])
+    tt(cf(2), cf(0), cf(1), O.add, [K(0), K(1)], [K(2)])
+    tt(cf(10), cf(9), ci(GR), O.add, [K(9), C(GR)], [K(10)])
+    ts(cf(3), cf(2), -3.0, None, O.mult, None, [K(2)], [K(3)])
+    ts(cf(8), cf(2), 8.0, None, O.mult, None, [K(2)], [K(8)])
+    ts(cf(13), cf(2), 2.0, HUGE, O.is_equal, O.mult, [K(2)], [K(13)])
+    ts(cf(12), cf(2), 1.0, HUGE, O.is_equal, O.mult, [K(2)], [K(12)])
+    tt(cf(4), cf(3), ci(RK), O.add, [K(3), C(RK)], [K(4)])
+    tt(cf(11), cf(8), cf(10), O.add, [K(8), K(10)], [K(11)])
+    tt(cf(14), cf(12), cf(13), O.subtract, [K(12), K(13)], [K(14)])
+    ts(cf(5), cf(4), 1.0, 1.0, O.is_equal, O.add, [K(4)], [K(5)])
+    ts(cf(6), cf(4), 0.0, 3.0, O.is_equal, O.mult, [K(4)], [K(6)])
+    ts(T.ulist[:, 0:8], T.ub[:, 0:8], cf(4), None, O.add, None, ["ub", K(4)], ["ulist"])
+    tt(cf(7), cf(5), cf(6), O.add, [K(5), K(6)], [K(7)])
+    act(T.th[:], T.par[:], AF.Identity, ["par", K(14), K(13)], ["th"], scale=cf(14), bias=cf(13))
+    for b in range(4):
+        act(T.et[:, 512 * b:512 * b + 512], T.zz[:], AF.Copy, ["zz"], [("et", 512 * b, 512 * b + 512)])
+
+    def conts(i, k):
+        lo, hi = 512 * i, 512 * i + 512
+        ts(T.ct[:, 0:2048:4], T.tg[:, lo:hi], cf(11), cf(7), O.is_equal, O.mult, [("tg", lo, hi), K(11), K(7)], ["ct"])
+        quant(k, 0, 512, "ct", 0, 2048)
+    conts(0, "a")
+    quant("u", 0, 128, "uv", 0, 512)
+    quant("0", 0, 320, "xt", 0, 1280)
+    V(lambda v: v.tensor_copy(T.qup[:, 0:128].bitcast(dt.uint32), T.qu[:, 0:128].bitcast(dt.uint32).indirect(T.ulist[:, 0:8])), ["qu", "ulist"], ["qup"])
+    V(lambda v: v.tensor_copy(T["sup_p"][:, 0:128], T["su_p"][:, 0:128].indirect(T.ulist[:, 0:8])), ["su_p", "ulist"], ["sup_p"])
+    ts(cf(20), ci(SG), -BIG, None, O.mult, None, [C(SG)], [K(20)])
+    ts(cf(21), ci(HF), 256.0, None, O.mult, None, [C(HF)], [K(21)])
+    ts(cf(22), ci(HF), 16.0, None, O.mult, None, [C(HF)], [K(22)])
+    ts(T.d0h[:], T.c0[:], cf(21), None, O.add, None, ["c0", K(21)], ["d0h"])
+    ts(cf(23), ci(HF), 0.0, None, O.is_equal, None, [C(HF)], [K(23)])
+    ts(cf(24), ci(HF), 1.0, None, O.is_equal, None, [C(HF)], [K(24)])
+    V(lambda v: v.tensor_copy(T.c0[:], T.d0h[:]), ["d0h"], ["c0"])
+    for i, (src, least) in enumerate(((BK, 2.0), (BK, 1.0), (GR, 1.0))):
+        ts(cf(25 + 2 * i), ci(src), least, None, O.is_ge, None, [C(src)], [K(25 + 2 * i)])
+        ts(cf(26 + 2 * i), ci(src), least, 8.0, O.is_lt, O.mult, [C(src)], [K(26 + 2 * i)])
+    fill(T.top[:], 3.0e7, ["top"])
+    for n in ("wt", "w8", "ft"):
+        fill(T[n][:], 0, [n])
+    UNITS = (("e", 0, 1.0), ("h", 128, 0.5), ("g", 0, 128.0))
+
+    def unit(j):
+        k, i, val = UNITS[j]
+        for b in range(4):
+            act(T.et[:, 512 * b + b:512 * b + 512:4], T.idx[:, i:i + 128], AF.Copy, [("idx", i, i + 128)], [("et", 512 * b, 512 * b + 512)], scale=val)
+
+    def unit_done(j):
+        quant(UNITS[j][0], 0, 512, "et", 0, 2048)
+        if j < 2:
+            unit(j + 1)
+
+    def units():
+        V(lambda v: v.tensor_copy(cf(40), ci(0)), [C(0)], [K(40)])
+        for i in range(2):
+            a, b = 128 * i, 128 * i + 128
+            ts(T.idx[:, a:b], T.ix[:, a:b], cf(40), None, O.is_equal, None, [("ix", a, b), K(40)], [("idx", a, b)])
+        unit(0)
+
+    def scan(out, d0, d1, reads, writes):
+        V(lambda v: v.tensor_tensor_scan(out, d0, d1, -4.0, O.max, O.add), reads, writes)
+
+    def stage(st, todo):
+        d0 = "c0"
+        if st:
+            o = 16 * st - 16
+            d0 = "d0h"
+            for a, b in ((0, 96), (96, 160)):
+                tt(T.d0h[:, a:b], T.wt[:, 0:16].indirect(T.off12[:, o + a // 16:o + b // 16]), T.c0[:, a:b], O.add, ["wt", ("off12", o, o + 16), "c0"], [("d0h", a, b)])
+        dn, an = "dst%d" % st, "ast%d" % st
+        for h in range(4):
+            a, b = 40 * h, 40 * h + 40
+            scan(T.tt[:, a:b], T[d0][:, a:b], T[dn][:, a:b], [(d0, a, b), dn], [("tt", a, b)])
+        for a, b in ((0, 80), (80, 160)):
+            tt(T.vv[:, a:b], T.tt[:, a:b], T[an][:, a:b], O.max, [("tt", a, b), an], [("vv", a, b)])
+        for i in range(2):
+            V(lambda v: v.tensor_reduce(T.mcol[:, i:i + 1], T.vv[:, 80 * i:80 * i + 80], AxisListType.X, O.min), [("vv", 80 * i, 80 * i + 80)], [("mcol", i, i + 1)])
+        between(todo)
+        ts(T.mb[:], T.top[:], T.mcol[:, 0:1], T.mcol[:, 1:2], O.min, O.min, ["top", "mcol"], ["mb"])
+        between(todo)
+        V(lambda v: v.transpose(T.tb[:], T.mb[:]), ["mb"], ["tb"])
+        between(todo)
+        tt(T.mi[:, 0:8], T.tb[:, 0:8], T.tb[:, 16:24], O.min, ["tb"], ["mi"])
+        between(todo)
+        if st < 2:
+            ts(T.wt[:, 0:8], T.mi[:, 0:8], 0xFFE00, None, O.bitwise_and, None, ["mi"], [("wt", 0, 8)])
+        else:
+            ts(T.w8[:, 0:8], T.mi[:, 0:8], 0xFFE00, 6, O.bitwise_and, O.arith_shift_right, ["mi"], [("w8", 0, 8)])
+        while todo:
+            between(todo)
+
+    def lists(src, dst, at, j, n, mk):
+        k = n // 2
+        return [lambda e=e: ts(T[dst][:, at + e:at + n:2], T[src][:, j + e:16 * n:32], cf(mk), cf(mk + 1), O.mult, O.add, [src, K(mk), K(mk + 1)], [(dst, at + k * e, at + k * e + k)]) for e in range(2)]
+
+    def symbols(part):
+        sts = ()
+        if part == 0:
+            mm(2, 160, "a", 0, "f", 16, True, False)
+            mm(2, 160, "a", 128, "f", 176, False, True)
+            for i, (a, sh) in enumerate(((256, 0), (256, 144), (384, 16), (384, 160))):
+                mm(3, 160, "a", a, "f", 16 + sh, i == 0, i == 3)
+            sts = ((0, 2),)
+        elif part == 1:
+            for st in (1, 2):
+                mm(3 + st, 160, "b", 256 * (st - 1), "f", 16, True, False)
+                mm(3 + st, 160, "b", 256 * (st - 1) + 128, "f", 176, False, True)
+            sts = ((1, 4), (2, 5))
+        else:
+            for i, (a, sh) in enumerate(((128, 0), (256, -16), (384, 16))):
+                mm(7, 320, "c", a, "f", 16 + sh, i == 0, i == 2)
+            mm(6, 320, "c", 0, "f", 16)
+        for st, bank in sts:
+            pb = "pb%d" % bank
+            act(T["dst%d" % st][:], T[pb][:, 0:160], AF.Identity, [pb], ["dst%d" % st], scale=512.0, bias=513.0)
+            act(T["ast%d" % st][:], T[pb][:, 0:160], AF.Abs, [pb, K(20)], ["ast%d" % st], scale=BIG, bias=cf(20))
+        if part == 2:
+            act(T.dow[:], T.pb6[:, 0:320], AF.Identity, ["pb6"], ["dow"], scale=8.0, bias=8.0)
+
+    def decode(r):
+        for i in range(8):
+            k, dst, b = ("e", "fp", i) if i < 4 else ("h", "f2", i - 4)
+            bank = i % 2
+            mm(bank, 320, k, 128 * b, str(r), 0)
+            act(T[dst][:, 320 * b:320 * b + 320], T["pb%d" % bank][:, 0:320], AF.Copy, ["pb%d" % bank], [(dst, 320 * b, 320 * b + 320)])
+
+    def first_table(r):
+        ca, cb = (1.0, 40.0) if r == 0 else (8.0, 1.0)
+
+        def X(i):
+            return T.fx[:, 16 * i:16 * i + 8]
+
+        def F(i):
+            return ("fx", 16 * i, 16 * i + 8)
+        m = T.mi[:, 0:8]
+        return [lambda: ts(X(0), m, 63, None, O.bitwise_and, None, ["mi"], [F(0)]),
+                lambda: ts(X(1), m, 448, 6, O.bitwise_and, O.arith_shift_right, ["mi"], [F(1)]),
+                lambda: ts(X(2), X(0), ca, 1.0, O.mult, O.add, [F(0)], [F(2)]),
+                lambda: ts(X(5), X(1), cb, None, O.mult, None, [F(1)], [F(5)]),
+                lambda: ts(X(4), m, BIG, 512.0, O.is_lt, O.mult, ["mi"], [F(4)]),
+                lambda: tt(X(3), X(2), X(5), O.add, [F(2), F(5)], [F(3)]),
+                lambda: tt(T.ft[:, 0:8], X(3), X(4), O.mult, [F(3), F(4)], [("ft", 0, 8)])]
+
+    def order(r):
+        todo = first_table(r)
+        for a in (0, 160):
+            tt(T.d0o[:, a:a + 160], T.w8[:, 0:16].indirect(T.offd[:, a // 16:a // 16 + 10]), T.hrow[:, a:a + 160], O.add, ["w8", "offd", "hrow"], [("d0o", a, a + 160)])
+        for h in range(8):
+            a, b = 40 * h, 40 * h + 40
+            scan(T.kap[:, 16 + a:16 + b], T.d0o[:, a:b], T.dow[:, a:b], [("d0o", a, b), "dow"], [("kap", 16 + a, 16 + b)])
+        for a in (0, 160):
+            V(lambda v: v.transpose(T.kt[:, a:a + 160], T.kap[:, 16 + a:176 + a]), [("kap", 16 + a, 176 + a)], [("kt", a, a + 160)])
+        V(lambda v: v.transpose(T.kt[:, 320:672], T.kap[:]), ["kap"], [("kt", 320, 672)])
+        between(todo)
+        between(todo)
+        ts(T.ex[:, 0:21], T.kt[:, 0:672:32], cf(23), None, O.mult, None, ["kt", K(23)], [("ex", 0, 21)])
+        ts(T.ex[:, 24:45], T.kt[:, 16:672:32], cf(24), None, O.mult, None, ["kt", K(24)], [("ex", 24, 45)])
+        between(todo)
+        tt(T.my[:, 0:10], T.ex[:, 0:10], T.ex[:, 34:44], O.add, ["ex"], [("my", 0, 10)])
+        tt(T.my[:, 10:20], T.ex[:, 11:21], T.ex[:, 24:34], O.add, ["ex"], [("my", 10, 20)])
+        for q in range(NS):
+            a = 320 * (q % 2)
+            act(T.sj[:, a:a + 320], T.kap[:, 16:336], AF.Sign, [("kap", 16, 336), ("my", q, q + 1)], [("sj", a, a + 320), ("acc", q, q + 1)], scale=-1.0, bias=T.my[:, q:q + 1], accum_out=T.acc[:, q:q + 1])
+        V(lambda v: v.tensor_copy(T.ku[:], T.kap[:, 16:336]), [("kap", 16, 336)], ["ku"])
+        between(todo)
+
+        def less(p):
+            a = 320 * (p % 3)
+            ts(T.fab[:, a:a + 320], T.ku[:], T.my[:, NS + p:NS + p + 1], None, O.is_lt, None, ["ku", ("my", NS + p, NS + p + 1)], [("fab", a, a + 320)])
+        less(0)
+        for p in range(NV):
+            if p + 1 < NV:
+                less(p + 1)
+            a, lo = 320 * (p % 3), 160 * p
+            V(lambda v: v.tensor_tensor_scan(T.scn[:, lo:lo + 160], T.fab[:, a:a + 160], T.fab[:, a + 160:a + 320], -160.0, O.add, O.add), [("fab", a, a + 320)], [("scn", lo, lo + 160)])
+            between(todo)
+        si = "si0" if r == 0 else "si1"
+        tt(T.vrow[:], T.ft[:, 0:16].indirect(T.offd[:, 0:20]), T[si][:], O.add, ["ft", "offd", si], ["vrow"])
+        for src, n, a, b, m, c in (("scn", slice(159, 160 * NV, 160), NS, 20, 0.0625, 10.0), ("acc", slice(0, NS), 0, NS, 0.03125, 9.96875)):
+            ts(T.rf[:, a:b], T[src][:, n], m, c, O.mult, O.add, [src], [("rf", a, b)])
+            ts(T.rx[:, a:b], T[src][:, n], m, c - 0.46875, O.mult, O.add, [src], [("rx", a, b)])
+        tt(T.rf[:, 32:52], T.rf[:, 0:20], T.rx[:, 0:20], O.add, [("rf", 0, 20), ("rx", 0, 20)], [("rf", 32, 52)])
+        for e in range(2):
+            ts(T.offs[:, e:20:2], T.rf[:, 32 + 10 * e:42 + 10 * e], 16.0, cf(22), O.mult, O.add, [("rf", 32, 52), K(22)], [("offs", 10 * e, 10 * e + 10)])
+        V(lambda v: v.tensor_copy(T.win[:, 0:640].indirect(T.offs[:, 0:20]), T.vrow[:]), ["vrow", "offs"], ["win"])
+
+    def L(i):
+        return T.lx[:, 16 * i:16 * i + 10]
+
+    def LR(i):
+        return ("lx", 16 * i, 16 * i + 10)
+
+    def plane(n, b):
+        return (n, 320 * b, 320 * b + 320)
+
+    def laid(r):
+        V(lambda v: v.transpose(T.tw[:, 0:320], T.win[:, 0:320]), [("win", 0, 320)], [("tw", 0, 320)])
+        tt(L(0), T.tw[:, 0:320:32], T.tw[:, 16:320:32], O.add, [("tw", 0, 320)], [LR(0)])
+        ts(L(1), L(0), 511, None, O.bitwise_and, None, [LR(0)], [LR(1)])
+        ts(L(3), L(0), 512.0, None, O.is_lt, None, [LR(0)], [LR(3)])
+        ts(L(2), L(0), 9, None, O.arith_shift_right, None, [LR(0)], [LR(2)])
+        ts(T.ll[:, 0:10], L(1), -1.0, None, O.add, None, [LR(1)], ["ll"])
+        for b in range(4):
+            act(T.pz[:, 160 * b:160 * b + 160], T.fp[:, 320 * b:320 * b + 320].indirect(T.ll[:, 0:10]), AF.Copy, [plane("fp", b), "ll"], [("pz", 160 * b, 160 * b + 160)], scale=0.5)
+        tt(L(4), L(3), L(1), O.mult, [LR(3), LR(1)], [LR(4)])
+        tt(L(5), L(4), L(2), O.add, [LR(4), LR(2)], [LR(5)])
+        ts(T.bl[:, 0:10], L(5), -1.0, None, O.add, None, [LR(5)], ["bl"])
+        for b in range(4):
+            tt(T.zt[:, b:640:4], T.f2[:, 320 * b:320 * b + 320].indirect(T.bl[:, 0:10]), T.pz[:, 160 * b:160 * b + 160], O.add,
+               [plane("f2", b), "bl", ("pz", 160 * b, 160 * b + 160)], [("zt", 160 * b, 160 * b + 160)])
+        z, l = "z%d" % r, "l%d" % r
+        quant(z, 0, 160, "zt", 0, 640)
+        rid, pid, _ = topo.addr(nxt)
+        m = topo.mask(core, nxt)
+        arr = "arr%d" % r
+        waits("G", accesses(["q" + z, "s" + z + "_p"], []))
+        g.remote_dma(T["q" + l][:, 0:160].bitcast(dt.uint8), T["q" + z][:, 0:160].bitcast(dt.uint8), T.sem[arr], T.sem["loc"], pid, rid, m)
+        g.remote_dma(T["s" + l + "_p"][:, 0:160], T["s" + z + "_p"][:, 0:160], T.sem[arr], T.sem["loc"], pid, rid, m)
+        k = 2 * len(topo.engines(core, nxt))
+        count["loc"] = count.get("loc", 0) + k
+        count[arr] = k
+        for n in ("q" + l, "s" + l + "_p"):
+            hist[n] = [[0, 160, "w", arr, k]]
+
+    def kept(r):
+        V(lambda v: v.transpose(T.tw[:, 320:640], T.win[:, 320:640]), [("win", 320, 640)], [("tw", 320, 640)])
+        tt(L(6), T.tw[:, 320:640:32], T.tw[:, 336:640:32], O.add, [("tw", 320, 640)], [LR(6)])
+        ts(L(7), L(6), 511, None, O.bitwise_and, None, [LR(6)], [LR(7)])
+        ts(T.kl[:, 0:10], L(7), -1.0, None, O.add, None, [LR(7)], ["kl"])
+        for b in range(4):
+            rd, wr = [plane("fp", b), "kl"], [("xk", 160 * b, 160 * b + 160)]
+            if b % 2:
+                act(T.xk[:, b:640:4], T.fp[:, 320 * b:320 * b + 320].indirect(T.kl[:, 0:10]), AF.Copy, rd, wr)
+            else:
+                V(lambda v: v.tensor_copy(T.xk[:, b:640:4], T.fp[:, 320 * b:320 * b + 320].indirect(T.kl[:, 0:10])), rd, wr)
+        quant(str(r + 1), 0, 160, "xk", 0, 640)
+
+    def arrive(r):
+        for b in range(4):
+            mm(2 + b, 160, "w", 128 * b, "l%d" % r, 0, True, False)
+            mm(2 + b, 160, "g", 128 * b, "l%d" % r, 0, False, True)
+        for b in range(4):
+            pb, wr = "pb%d" % (2 + b), [("xh", 160 * b, 160 * b + 160)]
+            if b % 2:
+                ts(T.xh[:, b:640:4], T[pb][:, 0:160], 0.0078125, None, O.mult, None, [pb], wr)
+            else:
+                act(T.xh[:, b:640:4], T[pb][:, 0:160], AF.Copy, [pb], wr, scale=0.0078125)
+        quant(str(r + 1), 160, 320, "xh", 0, 640)
+
+    def product_v(half):
+        mm(half, 160, "v", 0, "3", 160 * half)
+        for h in range(8):
+            a = 40 * h + 20 * half
+            act(T.yo[:, a:a + 20], T["pb%d" % half][:, h:160:8], AF.Copy, ["pb%d" % half], [("yo", a, a + 20)])
+
+    def flags(half, bank):
+        for h in range(8):
+            a = 40 * h + 20 * half
+            tt(T.fl[:, 64 + 4 * a:144 + 4 * a:4], T["pb%d" % bank][:, h:160:8], T.th[:, a:a + 20], O.is_gt, ["pb%d" % bank, "th"], [("fl", 64 + 4 * a, 144 + 4 * a)])
+
+    for r in range(3):
+        if r == 0:
+            mm(0, 320, "up", 0, "0", 0)
+            for a in (0, 160):
+                tt(T.fl[:, 64 + 4 * a:704 + 4 * a:4], T.pb0[:, a:a + 160], T.th[:, a:a + 160], O.is_gt, ["pb0", "th"], [("fl", 64 + 4 * a, 704 + 4 * a)])
+        else:
+            mm(1, 160, "up", 0, str(r), 160)
+            flags(1, 1)
+        quant("f", 0, 176, "fl", 0, 704)
+        quant("f", 176, 352, "fl", 704, 1408)
+        symbols(0)
+        half = [lambda: V(lambda v: v.transpose(T.tl[:], T.pb3[:, 0:160]), ["pb3"], ["tl"])] + lists("tl", "off12", 0, 0, 10, 25) + lists("tl", "off12", 16, 2, 10, 27)
+        full = [lambda: V(lambda v: v.transpose(T.tlo[:], T.pb7[:, 0:320]), ["pb7"], ["tlo"])] + lists("tlo", "offd", 0, 0, 20, 29)
+        if r == 0:
+            conts(1, "b")
+            symbols(1)
+            stage(0, half + [lambda: conts(2, "c"), units])
+            symbols(2)
+            stage(1, [lambda: fill(T.kap[:], 0.0, ["kap"]), lambda: unit_done(0), lambda: fill(T.win[:], 0.0, ["win"]), lambda: unit_done(1)])
+            unit_done(2)
+            decode(r)
+        else:
+            symbols(1)
+            symbols(2)
+            decode(r)
+            stage(0, half)
+            stage(1, [])
+        stage(2, full)
+        order(r)
+        laid(r)
+        kept(r)
+        if r < 2:
+            mm(0, 160, "up", 0, str(r + 1), 0)
+            flags(0, 0)
+        else:
+            quant("v", 0, 128, "uv", 512, 1024)
+            product_v(0)
+            for e in range(2):
+                ts(T.offo[:, e:20:2], T.rf[:, 10 * e:10 * e + 10], 16.0, None, O.mult, None, [("rf", 0, 20)], [("offo", 10 * e, 10 * e + 10)])
+            V(lambda v: v.tensor_copy(T.oprow[:, 0:320].indirect(T.offo[:, 0:20]), T.ccol[:]), ["ccol", "offo"], ["oprow"])
+            for k in range(8):
+                dma("Y", T.op[k:k + 1, :], T.oprow[16 * k:16 * k + 1, :], ["oprow"], [], "doy")
+
+            def N(i):
+                return T.nx[:, 20 * i:20 * i + 20]
+
+            def NR(i):
+                return ("nx", 20 * i, 20 * i + 20)
+            V(lambda v: v.tensor_copy(cf(41), ci(RK)), [C(RK)], [K(41)])
+            ts(N(1), N(0), cf(41), None, O.add, None, [NR(0), K(41)], [NR(1)])
+            ts(N(0), N(1), 205.0, None, O.mult, None, [NR(1)], [NR(0)])
+            ts(N(2), N(0), 13, None, O.arith_shift_right, None, [NR(0)], [NR(2)])
+            ts(N(0), N(2), -319.0, None, O.mult, None, [NR(2)], [NR(0)])
+            ts(N(2), N(1), 8.0, None, O.mult, None, [NR(1)], [NR(2)])
+            tt(T.fx[:, 96:116], N(0), N(2), O.add, [NR(0), NR(2)], [("fx", 96, 116)])
+            V(lambda v: v.tensor_copy(T.nat[:, 0:20], T.fx[:, 96:116]), [("fx", 96, 116)], ["nat"])
+        arrive(r)
+    product_v(1)
+    dma("S", T.y[:], T.yo[:], ["yo"], [], "doa")
+    V(lambda v: v.tensor_copy(T["sn_p"][:, 0:320], T["s3_p"][:, 0:320].indirect(T.nat[:, 0:20])), ["s3_p", "nat"], ["sn_p"])
+    for k in range(4):
+        dma("S" if k % 2 else "Y", T.osc[4 * k:4 * k + 4, :], T["sn_p"][32 * k:32 * k + 4, :], ["sn_p"], [], "doa" if k % 2 else "doy")
+    V(lambda v: v.tensor_copy(T.qn[:, 0:320].bitcast(dt.uint32), T.q3[:, 0:320].bitcast(dt.uint32).indirect(T.nat[:, 0:20])), ["q3", "nat"], ["qn"])
+    dma("Y", T.oc[:], T.qn[:].bitcast(dt.uint8), ["qn"], [], "doy")
+    for s in sorted(count):
+        if known["G"].get(s, 0) < count[s]:
+            g.wait_ge(T.sem[s], count[s])

@@ -1,10 +1,14 @@
-from concourse.mybir import dt, AluOpType as O, AxisListType, ActivationFunctionType as AF
+from concourse.mybir import dt, AluOpType as O, ActivationFunctionType as AF
 
 NS = 10
 NV = 20 - NS
-HUGE = 1.0e25
-BIG = float(2 ** 20)
+TOP = 1023.0
+MISS = float(2 ** 22)
+KEEP = float(2 ** 19)
+LOW = -1.0e9
 F4 = "float8_e4m3fn_x4"
+BLOCKS = (0, 1, 2, 3, 0, 0, 1, 1)
+WINDOW = (64, 128, 0)
 
 
 def _decl():
@@ -15,40 +19,36 @@ def _decl():
             d[k] = ("sbuf", [128, n], t)
     sb("xt fp f2", 1280, "bfloat16")
     sb("xk xh zt pz sj", 640, "bfloat16")
-    sb("uv", 1024, "bfloat16")
-    sb("zz", 512, "bfloat16")
-    sb("ct et", 2048, "bfloat16")
-    sb("fl", 1408, "bfloat16")
+    sb("uv cs cd", 1024, "bfloat16")
+    sb("cf eg eh zz", 520, "bfloat16")
+    sb("fl", 776, "bfloat16")
     sb("fab", 960, "bfloat16")
     sb("scn", 160 * NV, "bfloat16")
-    sb("idx ix", 256, "bfloat16")
-    sb("tg", 1536, "bfloat16")
-    for k, n in (("u", 128), ("up", 128), ("v", 128), ("w", 512), ("e", 512), ("h", 512), ("g", 512), ("a", 512), ("b", 512), ("c", 512), ("f", 352), ("n", 320)):
+    sb("w4 sg4 tgf ixg ixh", 128, "bfloat16")
+    sb("jm jn", 320, "bfloat16")
+    for k, n in (("u", 128), ("v", 128), ("w", 512), ("h", 512), ("g", 512), ("s", 256), ("d", 256), ("c", 256), ("f", 194), ("n", 320)):
         d["q" + k] = ("sbuf", [128, n], F4)
-        d["s" + k + "_p"] = ("sbuf", [128, n], "uint8")
+        d["p" + k] = ("sbuf", [128, n], "uint8")
     for r in range(4):
         d["q%d" % r] = ("sbuf", [128, 320], F4)
-        d["s%d_p" % r] = ("sbuf", [128, 320], "uint8")
+        d["p%d" % r] = ("sbuf", [128, 320], "uint8")
     for r in range(3):
         for k in ("z", "l"):
             d["q%s%d" % (k, r)] = ("sbuf", [128, 160], F4)
-            d["s%s%d_p" % (k, r)] = ("sbuf", [128, 160], "uint8")
-    sb("par th hrow si0 si1 ccol d0o dow vrow yo oprow tlo", 320, "float32")
-    sb("c0 d0h tt vv dst0 dst1 dst2 ast0 ast1 ast2 tl", 160, "float32")
-    sb("kap", 352, "float32")
-    sb("kt", 672, "float32")
-    sb("ex", 48, "float32")
-    sb("my acc", 20, "float32")
-    sb("win tw", 640, "float32")
-    sb("mcol", 8, "float32")
-    sb("top mb tb", 32, "float32")
-    sb("cf rf", 64, "float32")
-    sb("ci mi wt w8 ft ub", 16, "int32")
-    sb("fx lx", 128, "int32")
-    sb("rx", 32, "int32")
-    sb("nx", 64, "int32")
-    sb("off12 offd offs offo nat", 32, "uint16")
-    sb("ll bl kl ulist", 16, "uint16")
+            d["p%s%d" % (k, r)] = ("sbuf", [128, 160], "uint8")
+    sb("dg hr0 hr1 si0 si1 ccol natr d0o dow row2 vrow yo oprow kap kas my win dw df", 320, "float32")
+    sb("n0 n1 n2 n3 d1 d2 cr0 cr1 mx", 200, "float32")
+    sb("d0 inc1 inc2 dl", 160, "float32")
+    sb("one", 40, "float32")
+    sb("acc", 20, "float32")
+    sb("tb ta", 32, "float32")
+    sb("k", 48, "float32")
+    sb("wt mt am v16", 16, "float32")
+    sb("mi w8 ft", 16, "int32")
+    sb("ci", 48, "int32")
+    sb("lx", 32, "int32")
+    sb("off1 off2 ll bl kl", 16, "uint16")
+    sb("offd offs nat", 32, "uint16")
     sb("ku", 320, "uint16")
     for b in range(8):
         d["pb%d" % b] = ("psum", [128, 512], "float32")
@@ -71,26 +71,34 @@ def rank_program(g, core, T, topo):
     known = {k: {} for k in queue}
     hist = {}
 
-    def norm(a):
-        if isinstance(a, str):
-            a = (a, 0, 1 << 20)
-        if a[0][:2] == "pb":
-            return (a[0], 0, 1 << 20)
-        return a
+    def R(name, a=0, b=None, s=1):
+        b = SCRATCH[name][1][1] if b is None else b
+        m = 0
+        for c in range(a, b, s):
+            m |= 1 << c
+        if name[:2] == "pb":
+            m = 1
+        return (T[name][:, a:b:s] if s > 1 else T[name][:, a:b], [(name, m)])
+
+    def pick(win, off):
+        return (win[0].indirect(off[0]), win[1] + off[1])
+
+    def words(v):
+        return (v[0].bitcast(dt.uint32), v[1])
 
     def accesses(reads, writes):
-        r = [norm(a) for a in reads]
-        return [(a, "p" if a[0][:2] == "pb" else "r") for a in r] + [(norm(a), "w") for a in writes]
+        r = [a for v in reads if isinstance(v, tuple) for a in v[1]]
+        return [(a, "p" if a[0][:2] == "pb" else "r") for a in r] + [(a, "w") for v in writes for a in v[1]]
 
     def waits(q, acc):
         need = {}
-        for (b, lo, hi), kind in acc:
+        for (b, m), kind in acc:
             for e in hist.get(b, []):
-                if e[0] >= hi or e[1] <= lo or (kind == "r" and e[2] == "r"):
+                if not e[0] & m or (kind == "r" and e[1] == "r"):
                     continue
-                if b[:2] == "pb" and kind == ("w" if e[2] == "w" else "p") and own.get(q) == e[3]:
+                if b[:2] == "pb" and kind == ("w" if e[1] == "w" else "p") and own.get(q) == e[2]:
                     continue
-                need[e[3]] = max(need.get(e[3], 0), e[4])
+                need[e[2]] = max(need.get(e[2], 0), e[3])
         kn = known[q]
         for s in sorted(need, key=lambda s: -need[s]):
             if kn.get(s, 0) >= need[s]:
@@ -104,13 +112,13 @@ def rank_program(g, core, T, topo):
         count[sem] = count.get(sem, 0) + n
         v = count[sem]
         clock[(sem, v)] = dict(known[q])
-        for (b, lo, hi), kind in acc:
+        for (b, m), kind in acc:
             h = hist.setdefault(b, [])
             if kind == "r":
-                h[:] = [e for e in h if not (e[2] == "r" and e[3] == sem and e[0] >= lo and e[1] <= hi)]
+                h[:] = [e for e in h if not (e[1] == "r" and e[2] == sem and not e[0] & ~m)]
             else:
-                h[:] = [e for e in h if not (e[0] >= lo and e[1] <= hi)]
-            h.append([lo, hi, kind, sem, v])
+                h[:] = [e for e in h if e[0] & ~m]
+            h.append([m, kind, sem, v])
 
     def op(q, call, reads, writes):
         acc = accesses(reads, writes)
@@ -124,426 +132,401 @@ def rank_program(g, core, T, topo):
         queue[q].dma_start(out, in_).then_inc(T.sem[sem], 16)
         record(q, sem, 16, acc)
 
-    def V(call, reads, writes):
-        op("V", call, reads, writes)
+    def ap(v):
+        return v[0] if isinstance(v, tuple) else v
 
-    def ts(out, in0, s1, s2, o0, o1, reads, writes):
+    def ts(out, a, s1, o0, s2=None, o1=None):
         if o1 is None:
-            V(lambda v: v.tensor_scalar(out, in0, s1, None, o0), reads, writes)
+            op("V", lambda v: v.tensor_scalar(out[0], a[0], ap(s1), None, o0), [a, s1], [out])
         else:
-            V(lambda v: v.tensor_scalar(out, in0, s1, s2, o0, o1), reads, writes)
+            op("V", lambda v: v.tensor_scalar(out[0], a[0], ap(s1), ap(s2), o0, o1), [a, s1, s2], [out])
 
-    def tt(out, a, b, o, reads, writes):
-        V(lambda v: v.tensor_tensor(out, a, b, o), reads, writes)
+    def tt(out, a, b, o):
+        op("V", lambda v: v.tensor_tensor(out[0], a[0], b[0], o), [a, b], [out])
 
-    def fill(out, val, writes):
-        V(lambda v: v.memset(out, val), [], writes)
+    def copy(out, a):
+        op("V", lambda v: v.tensor_copy(out[0], a[0]), [a], [out])
 
-    def act(out, in_, f, reads, writes, **kw):
-        op("S", lambda s: s.activation(out, in_, f, **kw), reads, writes)
+    def scatter(win, off, a):
+        op("V", lambda v: v.tensor_copy(win[0].indirect(off[0]), a[0]), [a, off], [win])
 
-    def iota(out, pat, base, cm, writes, f=True):
-        if f:
-            op("G", lambda e: e.iota(out, pat, base, cm, allow_small_or_imprecise_dtypes=True), [], writes)
+    def fill(out, val):
+        op("V", lambda v: v.memset(out[0], val), [], [out])
+
+    def scan(out, a, b, init, o0, o1):
+        op("V", lambda v: v.tensor_tensor_scan(out[0], a[0], b[0], ap(init), o0, o1), [a, b, init], [out])
+
+    def turn(out, a):
+        op("V", lambda v: v.transpose(out[0], a[0]), [a], [out])
+
+    def act(out, a, f=AF.Copy, acc=None, **kw):
+        more = {k: ap(v) for k, v in kw.items()}
+        if acc:
+            more["accum_out"] = acc[0]
+        op("S", lambda s: s.activation(out[0], a[0], f, **more), [a] + list(kw.values()), [out] + ([acc] if acc else []))
+
+    def iota(out, pat, base=0, cm=0):
+        if SCRATCH[out[1][0][0]][2] == "int32":
+            op("G", lambda e: e.iota(out[0], pat, base, cm), [], [out])
         else:
-            op("G", lambda e: e.iota(out, pat, base, cm), [], writes)
+            op("G", lambda e: e.iota(out[0], pat, base, cm, allow_small_or_imprecise_dtypes=True), [], [out])
 
-    def quant(k, a, b, tile, lo, hi):
-        qn, sn = "q" + k, "s" + k + "_p"
-        V(lambda v: v.quantize_mx(T[qn][:, a:b], T[sn][:, a:b], T[tile][:, lo:hi]), [(tile, lo, hi)], [(qn, a, b), (sn, a, b)])
+    def level(name, a, b, val, s=1):
+        iota(R(name, a, b, s), [[0, len(range(a, b, s))]], int(val))
+
+    def quant(k, a, b, tile, lo):
+        q, p, t = R("q" + k, a, b), R("p" + k, a, b), R(tile, lo, lo + 4 * (b - a))
+        op("V", lambda v: v.quantize_mx(q[0], p[0], t[0]), [t], [q, p])
 
     def mm(bank, n, k, a, m, b, start=True, stop=True):
-        qa, sa, qb, sq = "q" + k, "s" + k + "_p", "q" + m, "s" + m + "_p"
-        op("P", lambda t: t.matmul_mx(T["pb%d" % bank][:, 0:n], T[qa][:, a:a + 128], T[sa][:, a:a + 128], T[qb][:, b:b + n], T[sq][:, b:b + n], start, stop),
-           [(qa, a, a + 128), (sa, a, a + 128), (qb, b, b + n), (sq, b, b + n)], ["pb%d" % bank])
+        v = [R("q" + k, a, a + 128), R("p" + k, a, a + 128), R("q" + m, b, b + n), R("p" + m, b, b + n)]
+        out = R("pb%d" % bank, 0, n)
+        op("P", lambda t: t.matmul_mx(out[0], v[0][0], v[1][0], v[2][0], v[3][0], start, stop), v, [out])
 
-    def between(todo):
-        if todo:
-            todo.pop(0)()
+    def diagonal(out, row, n):
+        scan(out, R("dg", 0, n), row, LOW, O.add, O.max)
 
-    dma("Y", T.xt[:], T.x[:], [], ["xt"], "dx")
-    dma("S", T.uv[:, 0:512], T.u[:], [], [("uv", 0, 512)], "du")
-    dma("Y", T.qw[:].bitcast(dt.uint8), T.wc[:], [], ["qw"], "dw")
-    dma("Y", T["sw_p"][:], T.ws[:], [], ["sw_p"], "dws")
-    dma("Y", T.uv[:, 512:1024], T.v[:], [], [("uv", 512, 1024)], "dv")
+    def run(calls):
+        for c in calls:
+            c()
 
-    fill(T.zz[:], 0.0, ["zz"])
-    fill(T.tg[:, 256:512], -1.0, [("tg", 256, 512)])
-    iota(T.ci[:, 0:1], [[1, 1]], 0, 1, [("ci", 0, 1)], f=False)
-    iota(T.ub[:, 0:8], [[16, 8]], 0, 0, ["ub"], f=False)
-    iota(T.tg[:, 0:128], [[0, 4], [100, 2], [0, 16]], 0, 0, [("tg", 0, 128)])
-    iota(T.tg[:, 128:256], [[0, 4], [100, 2], [0, 16]], -100, 0, [("tg", 128, 256)])
-    for base, jj, code in ((256, 0, 8), (384, 1, 16)):
-        iota(T.tg[:, base + jj:base + 128:32], [[1, 2], [0, 2]], code, 0, [("tg", base, base + 64)])
-        iota(T.tg[:, base + jj + 2:base + 128:32], [[1, 4]], code, 0, [("tg", base + 64, base + 128)])
-    iota(T.par[:], [[0, 10], [1, 2], [0, 16]], 0, 0, ["par"])
-    iota(T.c0[:], [[64, 4], [1, 40]], -1, 0, ["c0"])
-    for h in range(2):
-        for k in range(2):
-            lo = 512 + 128 * h + 64 * k
-            iota(T.tg[:, lo:lo + 64], [[0, 2], [100, 2], [0, 16]], k - 100 * h, 0, [("tg", lo, lo + 64)])
-    for h in range(2):
-        lo = 768 + 128 * h
-        iota(T.tg[:, lo:lo + 128], [[1, 4], [100, 2], [0, 16]], -100 * h, 0, [("tg", lo, lo + 128)])
-    iota(T.tg[:, 1024:1152], [[1, 8], [0, 16]], 0, 0, [("tg", 1024, 1152)])
-    fill(T.tg[:, 1152:1536], -1.0, [("tg", 1152, 1536)])
-    for i, (base, jj, code) in enumerate(((1152, 0, 8), (1152, 1, 17), (1280, 0, 9), (1408, 1, 16))):
-        iota(T.tg[:, base + jj:base + 128:32], [[2, 4]], code, 0, [("tg", 1152 + 96 * i, 1248 + 96 * i)])
-    iota(T.ix[:, 0:128], [[1, 128]], 0, 0, [("ix", 0, 128)])
-    iota(T.ix[:, 128:256], [[16, 4], [0, 2], [1, 16]], 0, 0, [("ix", 128, 256)])
-    iota(T.ix[:, 128:144], [[1, 16]], 112, 0, [("ix", 128, 256)])
-    iota(T.hrow[:], [[1, 8], [0, 40]], 0, 0, ["hrow"])
-    iota(T.si0[:], [[1, 320]], 1, 0, ["si0"])
-    iota(T.si1[:], [[1, 8], [8, 40]], 1, 0, ["si1"])
-    iota(T.ccol[:], [[1, 320]], 0, 0, ["ccol"])
-    iota(T.nx[:, 0:20], [[16, 20]], 0, 0, [("nx", 0, 20)], f=False)
-    for n, w in (("ct", 512), ("fl", 352)):
-        for b in range(4):
-            act(T[n][:, w * b:w * b + w], T.zz[:, 0:w], AF.Copy, ["zz"], [(n, w * b, w * b + w)])
+    dma("Y", T.xt[:], T.x[:], [], [R("xt")], "dx")
+    dma("S", T.uv[:, 0:512], T.u[:], [], [R("uv", 0, 512)], "du")
+    g.sync.wait_ge(T.sem["dx"], 16)
+    dma("Y", T.qw[:].bitcast(dt.uint8), T.wc[:], [], [R("qw")], "dw")
+    dma("Y", T.pw[:], T.ws[:], [], [R("pw")], "dws")
+    dma("Y", T.uv[:, 512:1024], T.v[:], [], [R("uv", 512, 1024)], "dv")
 
     def ci(i):
-        return T.ci[:, i:i + 1]
-
-    def cf(i):
-        return T.cf[:, i:i + 1]
-
-    def C(i):
-        return ("ci", i, i + 1)
+        return R("ci", i, i + 1)
 
     def K(i):
-        return ("cf", i, i + 1)
-    RK, SG, HF, BK, GR = 1, 2, 3, 4, 5
-    ts(ci(RK), ci(0), 15, None, O.bitwise_and, None, [C(0)], [C(RK)])
-    ts(ci(GR), ci(0), 4, None, O.arith_shift_right, None, [C(0)], [C(GR)])
-    ts(ci(SG), ci(0), 7, None, O.bitwise_and, None, [C(0)], [C(SG)])
-    ts(ci(HF), ci(0), 16, 4, O.bitwise_and, O.arith_shift_right, [C(0)], [C(HF)])
-    ts(ci(BK), ci(0), 5, None, O.arith_shift_right, None, [C(0)], [C(BK)])
-    ts(cf(0), ci(RK), 3.0, None, O.is_ge, None, [C(RK)], [K(0)])
-    ts(cf(1), ci(RK), 6.0, None, O.is_ge, None, [C(RK)], [K(1)])
-    ts(cf(9), ci(RK), 9.0, 100.0, O.is_ge, O.mult, [C(RK)], [K(9)])
-    tt(cf(2), cf(0), cf(1), O.add, [K(0), K(1)], [K(2)])
-    tt(cf(10), cf(9), ci(GR), O.add, [K(9), C(GR)], [K(10)])
-    ts(cf(3), cf(2), -3.0, None, O.mult, None, [K(2)], [K(3)])
-    ts(cf(8), cf(2), 8.0, None, O.mult, None, [K(2)], [K(8)])
-    ts(cf(13), cf(2), 2.0, HUGE, O.is_equal, O.mult, [K(2)], [K(13)])
-    ts(cf(12), cf(2), 1.0, HUGE, O.is_equal, O.mult, [K(2)], [K(12)])
-    tt(cf(4), cf(3), ci(RK), O.add, [K(3), C(RK)], [K(4)])
-    tt(cf(11), cf(8), cf(10), O.add, [K(8), K(10)], [K(11)])
-    tt(cf(14), cf(12), cf(13), O.subtract, [K(12), K(13)], [K(14)])
-    ts(cf(5), cf(4), 1.0, 1.0, O.is_equal, O.add, [K(4)], [K(5)])
-    ts(cf(6), cf(4), 0.0, 3.0, O.is_equal, O.mult, [K(4)], [K(6)])
-    ts(T.ulist[:, 0:8], T.ub[:, 0:8], cf(4), None, O.add, None, ["ub", K(4)], ["ulist"])
-    tt(cf(7), cf(5), cf(6), O.add, [K(5), K(6)], [K(7)])
-    act(T.th[:], T.par[:], AF.Identity, ["par", K(14), K(13)], ["th"], scale=cf(14), bias=cf(13))
-    for b in range(4):
-        act(T.et[:, 512 * b:512 * b + 512], T.zz[:], AF.Copy, ["zz"], [("et", 512 * b, 512 * b + 512)])
+        return R("k", i, i + 1)
+    RK, SG, S1, S2, HF, BK, GR, PC, PD = range(1, 10)
+    RF, GF, PF, LT3, WA, WT, RA, RW, CP, NK, I0, CK, CL, CN = range(14)
+    WM, MK, LA, LB, G4, WH = 16, 20, 24, 28, 32, 36
+    iota(ci(0), [[1, 1]], 0, 1)
+    iota(R("k", G4, G4 + 4), [[1, 4]])
+    iota(R("v16"), [[0, 2], [1, 8]])
+    level("one", 0, 40, -1)
+    iota(R("jm"), [[0, 20], [1, 16]])
+    iota(R("tgf"), [[1, 8], [0, 16]])
+    for i, low in enumerate((-TOP, -TOP, -1, -1)):
+        level("n%d" % i, 160, 161, -(2 ** 24 - 1))
+        level("n%d" % i, 161, 193, low)
+    level("wt", 8, 16, TOP)
+    level("d1", 162, 193, 0)
+    level("d2", 162, 193, 0)
+    level("cr0", 1, 160, 1)
+    level("cr0", 40, 160, 513, 40)
+    level("n3", 0, 160, 0)
+    level("mt", 8, 16, 1023)
+    iota(R("ixg"), [[1, 128]])
+    iota(R("ixh"), [[16, 4], [0, 2], [1, 16]])
+    iota(R("ixh", 0, 16), [[1, 16]], 112)
+    iota(R("si0"), [[1, 320]])
+    level("w8", 8, 16, 8 * TOP)
+    level("ft", 8, 16, 511)
+    iota(R("hr0"), [[-1, 8], [0, 40]], 7)
+    level("cr1", 1, 160, 1026)
+    level("cr1", 4, 160, -3070, 4)
+    iota(R("si1"), [[1, 2], [2, 160]])
+    iota(R("hr1"), [[-1, 2], [0, 40], [-2, 4]], 7)
+    iota(R("ccol"), [[40, 2], [1, 40], [80, 4]])
+    iota(R("natr"), [[1, 8], [8, 40]])
 
-    def conts(i, k):
-        lo, hi = 512 * i, 512 * i + 512
-        ts(T.ct[:, 0:2048:4], T.tg[:, lo:hi], cf(11), cf(7), O.is_equal, O.mult, [("tg", lo, hi), K(11), K(7)], ["ct"])
-        quant(k, 0, 512, "ct", 0, 2048)
-    conts(0, "a")
-    quant("u", 0, 128, "uv", 0, 512)
-    quant("0", 0, 320, "xt", 0, 1280)
-    V(lambda v: v.tensor_copy(T.qup[:, 0:128].bitcast(dt.uint32), T.qu[:, 0:128].bitcast(dt.uint32).indirect(T.ulist[:, 0:8])), ["qu", "ulist"], ["qup"])
-    V(lambda v: v.tensor_copy(T["sup_p"][:, 0:128], T["su_p"][:, 0:128].indirect(T.ulist[:, 0:8])), ["su_p", "ulist"], ["sup_p"])
-    ts(cf(20), ci(SG), -BIG, None, O.mult, None, [C(SG)], [K(20)])
-    ts(cf(21), ci(HF), 256.0, None, O.mult, None, [C(HF)], [K(21)])
-    ts(cf(22), ci(HF), 16.0, None, O.mult, None, [C(HF)], [K(22)])
-    ts(T.d0h[:], T.c0[:], cf(21), None, O.add, None, ["c0", K(21)], ["d0h"])
-    ts(cf(23), ci(HF), 0.0, None, O.is_equal, None, [C(HF)], [K(23)])
-    ts(cf(24), ci(HF), 1.0, None, O.is_equal, None, [C(HF)], [K(24)])
-    V(lambda v: v.tensor_copy(T.c0[:], T.d0h[:]), ["d0h"], ["c0"])
-    for i, (src, least) in enumerate(((BK, 2.0), (BK, 1.0), (GR, 1.0))):
-        ts(cf(25 + 2 * i), ci(src), least, None, O.is_ge, None, [C(src)], [K(25 + 2 * i)])
-        ts(cf(26 + 2 * i), ci(src), least, 8.0, O.is_lt, O.mult, [C(src)], [K(26 + 2 * i)])
-    fill(T.top[:], 3.0e7, ["top"])
-    for n in ("wt", "w8", "ft"):
-        fill(T[n][:], 0, [n])
-    UNITS = (("e", 0, 1.0), ("h", 128, 0.5), ("g", 0, 128.0))
+    fill(R("zz"), 0.0)
+    fill(R("w4"), 0.0)
+    fill(R("sg4"), 0.0)
+    ts(ci(RK), ci(0), 15, O.bitwise_and)
+    ts(ci(GR), ci(0), 4, O.arith_shift_right)
+    act(R("fl", 0, 520), R("zz"))
+    act(R("fl", 520, 776), R("zz", 0, 256))
+    fill(R("w4", 0, 64, 4), 1.0)
+    fill(R("w4", 66, 128, 4), 1.0)
+    ts(K(WA), ci(RK), -2.0, O.mult, 4.0, O.add)
+    ts(K(LT3), ci(RK), 3.0, O.is_lt)
+    ts(K(RA), ci(RK), 0.25, O.mult, 0.25, O.add)
+    copy(K(GF), ci(GR))
+    ts(ci(SG), ci(0), 7, O.bitwise_and)
+    ts(K(WT), K(WA), 1.0, O.max, K(LT3), O.mult)
+    ts(K(RW), ci(RK), -1.0, O.add, K(RA), O.max)
+    ts(R("k", MK, MK + 4), R("k", G4, G4 + 4), K(GF), O.is_equal, K(LT3), O.mult)
+    ts(ci(S1), ci(0), 7, O.bitwise_and, 1, O.arith_shift_right)
+    ts(ci(S2), ci(0), 7, O.bitwise_and, 2, O.arith_shift_right)
+    ts(R("k", WM, WM + 4), R("k", G4, G4 + 4), K(GF), O.is_equal, K(WT), O.mult)
+    ts(R("ci", 16, 32), R("v16"), K(RW), O.mult, -0.375, O.add)
+    copy(K(RF), ci(RK))
+    tt(ci(PC), ci(SG), ci(S1), O.subtract)
+    ts(R("ci", 32, 48), R("ci", 16, 32), 1, O.bitwise_and)
+    for i, b in enumerate(BLOCKS):
+        act(R("cs", 128 * i, 128 * i + 128), R("w4"), AF.Identity, scale=K(WM + b))
+    tt(ci(PD), ci(PC), ci(S2), O.subtract)
+    ts(ci(HF), ci(0), 16, O.bitwise_and, 4, O.arith_shift_right)
+    ts(ci(BK), ci(0), 5, O.arith_shift_right)
+    for at, sign in ((0, 1.0), (1, -1.0), (66, 1.0), (67, -1.0)):
+        ts(R("sg4", at, at + 61, 4), R("ci", 32, 48), -2.0 * MISS * sign, O.mult, MISS * sign, O.add)
+    ts(K(I0), ci(PD), -MISS, O.mult, TOP, O.add)
+    ts(K(CP), ci(RK), -KEEP, O.mult, 15.0 * KEEP, O.add)
+    ts(R("jn"), R("jm"), K(RF), O.is_gt, 33.0, O.mult)
+    for i, b in enumerate(BLOCKS):
+        ts(R("cd", 128 * i, 128 * i + 128), R("sg4"), K(MK + b), O.mult)
+    act(R("dg"), R("jn"), AF.Identity, scale=KEEP, bias=-32.0 * KEEP)
+    for n in ("cf", "eg", "eh"):
+        act(R(n), R("zz"))
+    quant("f", 66, 194, "fl", 264)
+    quant("s", 0, 256, "cs", 0)
+    quant("d", 0, 256, "cd", 0)
 
-    def unit(j):
-        k, i, val = UNITS[j]
-        for b in range(4):
-            act(T.et[:, 512 * b + b:512 * b + 512:4], T.idx[:, i:i + 128], AF.Copy, [("idx", i, i + 128)], [("et", 512 * b, 512 * b + 512)], scale=val)
+    def waiters():
+        out = []
+        for i, (src, least, unit, one) in enumerate(((BK, 2.0, 1.0, 0.0), (BK, 1.0, 2.0 ** -12, 1.0), (GR, 1.0, 0.125, 1.0))):
+            out += [lambda i=i, src=src, least=least, unit=unit: ts(K(LA + i), ci(src), least, O.is_ge, unit, O.mult),
+                    lambda i=i, src=src, least=least, one=one: ts(K(WH + i), ci(src), least, O.is_lt, 8.0 + one, O.mult),
+                    lambda i=i, one=one: ts(K(WH + 4 + i), K(LA + i), K(CP), O.mult, one, O.add),
+                    lambda i=i: tt(K(LB + i), K(WH + i), K(WH + 4 + i), O.subtract)]
+        return out
 
-    def unit_done(j):
-        quant(UNITS[j][0], 0, 512, "et", 0, 2048)
-        if j < 2:
-            unit(j + 1)
+    def ends(r):
+        e, last = ((2208.0, 4095.0 - 552 * 3 - 39), (513.0, 4095.0 - 8 * 39 - 1026 * 3))[r]
+        n = "cr%d" % r
+        return [lambda: ts(R(n, 0, 1), ci(HF), e, O.mult, -4095.0, O.add),
+                lambda: ts(R(n, 160, 161), ci(HF), -e, O.mult, last, O.add),
+                lambda: ts(R(n, 161, 162), ci(PD), -MISS, O.mult)]
 
     def units():
-        V(lambda v: v.tensor_copy(cf(40), ci(0)), [C(0)], [K(40)])
-        for i in range(2):
-            a, b = 128 * i, 128 * i + 128
-            ts(T.idx[:, a:b], T.ix[:, a:b], cf(40), None, O.is_equal, None, [("ix", a, b), K(40)], [("idx", a, b)])
-        unit(0)
+        out = [lambda: copy(K(PF), ci(0)),
+               lambda: ts(R("eg", 3, 515, 4), R("ixg"), K(PF), O.is_equal, 128.0, O.mult),
+               lambda: ts(R("eh", 3, 515, 4), R("ixh"), K(PF), O.is_equal)]
+        for k in "gh":
+            out += [lambda k=k, b=b: quant(k, 128 * b, 128 * b + 128, "e" + k, 3 - b) for b in range(4)]
+        return out
 
-    def scan(out, d0, d1, reads, writes):
-        V(lambda v: v.tensor_tensor_scan(out, d0, d1, -4.0, O.max, O.add), reads, writes)
+    def stack(name, r, h, at=0):
+        return R(name, at + 40 * h, at + 40 * h + 40) if r == 0 else R(name, at + h, at + 160, 4)
 
-    def stage(st, todo):
-        d0 = "c0"
-        if st:
-            o = 16 * st - 16
-            d0 = "d0h"
-            for a, b in ((0, 96), (96, 160)):
-                tt(T.d0h[:, a:b], T.wt[:, 0:16].indirect(T.off12[:, o + a // 16:o + b // 16]), T.c0[:, a:b], O.add, ["wt", ("off12", o, o + 16), "c0"], [("d0h", a, b)])
-        dn, an = "dst%d" % st, "ast%d" % st
-        for h in range(4):
-            a, b = 40 * h, 40 * h + 40
-            scan(T.tt[:, a:b], T[d0][:, a:b], T[dn][:, a:b], [(d0, a, b), dn], [("tt", a, b)])
-        for a, b in ((0, 80), (80, 160)):
-            tt(T.vv[:, a:b], T.tt[:, a:b], T[an][:, a:b], O.max, [("tt", a, b), an], [("vv", a, b)])
-        for i in range(2):
-            V(lambda v: v.tensor_reduce(T.mcol[:, i:i + 1], T.vv[:, 80 * i:80 * i + 80], AxisListType.X, O.min), [("vv", 80 * i, 80 * i + 80)], [("mcol", i, i + 1)])
-        between(todo)
-        ts(T.mb[:], T.top[:], T.mcol[:, 0:1], T.mcol[:, 1:2], O.min, O.min, ["top", "mcol"], ["mb"])
-        between(todo)
-        V(lambda v: v.transpose(T.tb[:], T.mb[:]), ["mb"], ["tb"])
-        between(todo)
-        tt(T.mi[:, 0:8], T.tb[:, 0:8], T.tb[:, 16:24], O.min, ["tb"], ["mi"])
-        between(todo)
-        if st < 2:
-            ts(T.wt[:, 0:8], T.mi[:, 0:8], 0xFFE00, None, O.bitwise_and, None, ["mi"], [("wt", 0, 8)])
-        else:
-            ts(T.w8[:, 0:8], T.mi[:, 0:8], 0xFFE00, 6, O.bitwise_and, O.arith_shift_right, ["mi"], [("w8", 0, 8)])
-        while todo:
-            between(todo)
+    def flags(bank, at, step):
+        for a in (at, at + 5):
+            ts(R("fl", a, a + 160 * step - 1, step), R("pb%d" % bank, 0, 160), 0.0, O.is_gt)
 
-    def lists(src, dst, at, j, n, mk):
-        k = n // 2
-        return [lambda e=e: ts(T[dst][:, at + e:at + n:2], T[src][:, j + e:16 * n:32], cf(mk), cf(mk + 1), O.mult, O.add, [src, K(mk), K(mk + 1)], [(dst, at + k * e, at + k * e + k)]) for e in range(2)]
-
-    def symbols(part):
-        sts = ()
+    def products(part):
         if part == 0:
-            mm(2, 160, "a", 0, "f", 16, True, False)
-            mm(2, 160, "a", 128, "f", 176, False, True)
-            for i, (a, sh) in enumerate(((256, 0), (256, 144), (384, 16), (384, 160))):
-                mm(3, 160, "a", a, "f", 16 + sh, i == 0, i == 3)
-            sts = ((0, 2),)
-        elif part == 1:
-            for st in (1, 2):
-                mm(3 + st, 160, "b", 256 * (st - 1), "f", 16, True, False)
-                mm(3 + st, 160, "b", 256 * (st - 1) + 128, "f", 176, False, True)
-            sts = ((1, 4), (2, 5))
+            for st in range(3):
+                mm(2 * st, 160, "s", WINDOW[st], "f", 0)
+                mm(2 * st + 1, 194 if st == 0 else 162, "d", WINDOW[st], "f", 0)
         else:
-            for i, (a, sh) in enumerate(((128, 0), (256, -16), (384, 16))):
-                mm(7, 320, "c", a, "f", 16 + sh, i == 0, i == 2)
-            mm(6, 320, "c", 0, "f", 16)
-        for st, bank in sts:
-            pb = "pb%d" % bank
-            act(T["dst%d" % st][:], T[pb][:, 0:160], AF.Identity, [pb], ["dst%d" % st], scale=512.0, bias=513.0)
-            act(T["ast%d" % st][:], T[pb][:, 0:160], AF.Abs, [pb, K(20)], ["ast%d" % st], scale=BIG, bias=cf(20))
-        if part == 2:
-            act(T.dow[:], T.pb6[:, 0:320], AF.Identity, ["pb6"], ["dow"], scale=8.0, bias=8.0)
+            for e in range(2):
+                mm(6 + e, 160, "c", 128 * e, "f", 0)
 
     def decode(r):
+        out = []
         for i in range(8):
-            k, dst, b = ("e", "fp", i) if i < 4 else ("h", "f2", i - 4)
-            bank = i % 2
-            mm(bank, 320, k, 128 * b, str(r), 0)
-            act(T[dst][:, 320 * b:320 * b + 320], T["pb%d" % bank][:, 0:320], AF.Copy, ["pb%d" % bank], [(dst, 320 * b, 320 * b + 320)])
+            k, dst, b, sc = ("g", "fp", i, 0.0078125) if i < 4 else ("h", "f2", i - 4, 0.5)
 
-    def first_table(r):
-        ca, cb = (1.0, 40.0) if r == 0 else (8.0, 1.0)
+            def one(k=k, dst=dst, b=b, sc=sc, bank=2 + i % 2):
+                mm(bank, 320, k, 128 * b, str(r), 0)
+                act(R(dst, 320 * b, 320 * b + 320), R("pb%d" % bank, 0, 320), scale=sc)
+            out.append(one)
+        return out
 
-        def X(i):
-            return T.fx[:, 16 * i:16 * i + 8]
+    def stage(r, st, gaps):
+        n = "n%d" % st
+        if st:
+            act(R("d0"), pick(R("wt"), R("off%d" % st, 0, 10)), AF.Abs, scale=(1.0, 4096.0)[st - 1])
+        run(gaps[0])
+        for h in range(4):
+            if st:
+                scan(stack(n, r, h), stack("d0", r, h), stack("inc%d" % st, r, h), -LOW, O.min, O.subtract)
+            else:
+                scan(stack(n, r, h), R("one"), stack("pb0", r, h), K(I0), O.add, O.subtract)
+        run(gaps[1])
+        scan(R("mx", 0, 193), R(("pb1", "d1", "d2")[st], 0, 193), R(n, 0, 193), LOW, O.add, O.max)
+        run(gaps[2])
+        turn(R("tb"), R("mx", 161, 193))
+        run(gaps[3])
+        tt(R("mi" if st == 2 else "wt", 0, 8), R("tb", 0, 8), R("tb", 16, 24), O.max)
+        run(gaps[4])
 
-        def F(i):
-            return ("fx", 16 * i, 16 * i + 8)
-        m = T.mi[:, 0:8]
-        return [lambda: ts(X(0), m, 63, None, O.bitwise_and, None, ["mi"], [F(0)]),
-                lambda: ts(X(1), m, 448, 6, O.bitwise_and, O.arith_shift_right, ["mi"], [F(1)]),
-                lambda: ts(X(2), X(0), ca, 1.0, O.mult, O.add, [F(0)], [F(2)]),
-                lambda: ts(X(5), X(1), cb, None, O.mult, None, [F(1)], [F(5)]),
-                lambda: ts(X(4), m, BIG, 512.0, O.is_lt, O.mult, ["mi"], [F(4)]),
-                lambda: tt(X(3), X(2), X(5), O.add, [F(2), F(5)], [F(3)]),
-                lambda: tt(T.ft[:, 0:8], X(3), X(4), O.mult, [F(3), F(4)], [("ft", 0, 8)])]
+    def listed(off, n, row, i):
+        return lambda: ts(R(off, 0, n), R(row, 15, 16 * n, 16), K(LA + i), O.mult, K(LB + i), O.add)
+
+    def times(r, more):
+        c = min(r, 1)
+        dec = more["decode"]
+
+        def half(n, e):
+            return R(n, 160 * e, 160 * e + 160)
+        dow = [lambda e=e: act(half("dow", e), R("pb%d" % (6 + e), 0, 160), AF.Identity, scale=8.0, bias=8.0) for e in range(2)]
+        stage(r, 0, [more["a"],
+                     [lambda: diagonal(R("dl"), R("pb2", 0, 160), 160),
+                      lambda: act(R("d1", 0, 161), R("pb3", 0, 161)),
+                      lambda: act(R("inc2"), R("pb4", 0, 160), AF.Identity, scale=4096.0, bias=4096.0),
+                      lambda: act(R("inc1"), R("pb2", 0, 160), AF.Identity, bias=1.0)],
+                     [listed("off1", 10, "dl", 0)] + more["b"],
+                     [lambda: tt(R("d2", 0, 162), R("pb5", 0, 162), R("cr%d" % c, 0, 162), O.add)],
+                     more["c"] + dow])
+        stage(r, 1, [[lambda: diagonal(R("dl"), R("inc2"), 160),
+                      lambda: scan(R("mx", 0, 193), R("d2", 0, 193), R("n3", 0, 193), LOW, O.add, O.max),
+                      lambda: diagonal(half("df", 0), half("dow", 0), 160),
+                      lambda: diagonal(half("df", 1), half("dow", 1), 160),
+                      lambda: turn(R("ta"), R("mx", 161, 193))] + dec[0],
+                     [listed("off2", 10, "dl", 1), listed("offd", 20, "df", 2), lambda: tt(R("am", 0, 8), R("ta", 0, 8), R("ta", 16, 24), O.max)],
+                     [lambda: ts(R("mt", 0, 8), R("am", 0, 8), 0.0, O.is_ge, 1023.0, O.add)] + more["d"],
+                     more["e"], more["f"]])
+        stage(r, 2, [[lambda e=e: tt(half("row2", e), pick(R("mt"), R("offd", 10 * e, 10 * e + 10)), half("si%d" % c, e), O.mult) for e in range(2)] + dec[1],
+                     more["g"], more["h"], more["i"], more["j"]])
+        ts(R("w8", 0, 8), R("mi", 0, 8), 9, O.arith_shift_right, 0x1FF8, O.bitwise_and)
+        ts(R("ft", 0, 8), R("mi", 0, 8), 511, O.bitwise_and)
 
     def order(r):
-        todo = first_table(r)
-        for a in (0, 160):
-            tt(T.d0o[:, a:a + 160], T.w8[:, 0:16].indirect(T.offd[:, a // 16:a // 16 + 10]), T.hrow[:, a:a + 160], O.add, ["w8", "offd", "hrow"], [("d0o", a, a + 160)])
-        for h in range(8):
-            a, b = 40 * h, 40 * h + 40
-            scan(T.kap[:, 16 + a:16 + b], T.d0o[:, a:b], T.dow[:, a:b], [("d0o", a, b), "dow"], [("kap", 16 + a, 16 + b)])
-        for a in (0, 160):
-            V(lambda v: v.transpose(T.kt[:, a:a + 160], T.kap[:, 16 + a:176 + a]), [("kap", 16 + a, 176 + a)], [("kt", a, a + 160)])
-        V(lambda v: v.transpose(T.kt[:, 320:672], T.kap[:]), ["kap"], [("kt", 320, 672)])
-        between(todo)
-        between(todo)
-        ts(T.ex[:, 0:21], T.kt[:, 0:672:32], cf(23), None, O.mult, None, ["kt", K(23)], [("ex", 0, 21)])
-        ts(T.ex[:, 24:45], T.kt[:, 16:672:32], cf(24), None, O.mult, None, ["kt", K(24)], [("ex", 24, 45)])
-        between(todo)
-        tt(T.my[:, 0:10], T.ex[:, 0:10], T.ex[:, 34:44], O.add, ["ex"], [("my", 0, 10)])
-        tt(T.my[:, 10:20], T.ex[:, 11:21], T.ex[:, 24:34], O.add, ["ex"], [("my", 10, 20)])
-        for q in range(NS):
-            a = 320 * (q % 2)
-            act(T.sj[:, a:a + 320], T.kap[:, 16:336], AF.Sign, [("kap", 16, 336), ("my", q, q + 1)], [("sj", a, a + 320), ("acc", q, q + 1)], scale=-1.0, bias=T.my[:, q:q + 1], accum_out=T.acc[:, q:q + 1])
-        V(lambda v: v.tensor_copy(T.ku[:], T.kap[:, 16:336]), [("kap", 16, 336)], ["ku"])
-        between(todo)
+        c = min(r, 1)
 
-        def less(p):
-            a = 320 * (p % 3)
-            ts(T.fab[:, a:a + 320], T.ku[:], T.my[:, NS + p:NS + p + 1], None, O.is_lt, None, ["ku", ("my", NS + p, NS + p + 1)], [("fab", a, a + 320)])
-        less(0)
+        def half(n, e):
+            return R(n, 160 * e, 160 * e + 160)
+        for e in range(2):
+            tt(half("d0o", e), pick(R("w8"), R("offd", 10 * e, 10 * e + 10)), half("hr%d" % c, e), O.add)
+        for e in range(2):
+            for h in range(4):
+                scan(stack("kap", r, h, 160 * e), stack("d0o", r, h, 160 * e), stack("dow", r, h, 160 * e), -LOW, O.min, O.subtract)
+            act(half("kas", e), half("kap", e), AF.Identity, bias=K(CP))
+        for e in range(2):
+            diagonal(half("my", e), half("kap", e), 160)
+            ts(half("ku", e), half("kap", e), 4096.0, O.add)
+
+        def mine(q):
+            return R("my", 16 * q + 15, 16 * q + 16)
+        for q in range(NS):
+            act(R("sj", 320 * (q % 2), 320 * (q % 2) + 320), R("kas"), AF.Sign, acc=R("acc", q, q + 1), scale=-1.0, bias=mine(q))
+
+        def value(e):
+            tt(half("vrow", e), pick(R("ft"), R("offd", 10 * e, 10 * e + 10)), half("row2", e), O.add)
+
+        def more(p):
+            ts(R("fab", 320 * (p % 3), 320 * (p % 3) + 320), R("ku"), K(CK), O.add, mine(NS + p), O.is_gt)
+        value(1)
+        more(0)
         for p in range(NV):
             if p + 1 < NV:
-                less(p + 1)
-            a, lo = 320 * (p % 3), 160 * p
-            V(lambda v: v.tensor_tensor_scan(T.scn[:, lo:lo + 160], T.fab[:, a:a + 160], T.fab[:, a + 160:a + 320], -160.0, O.add, O.add), [("fab", a, a + 320)], [("scn", lo, lo + 160)])
-            between(todo)
-        si = "si0" if r == 0 else "si1"
-        tt(T.vrow[:], T.ft[:, 0:16].indirect(T.offd[:, 0:20]), T[si][:], O.add, ["ft", "offd", si], ["vrow"])
-        for src, n, a, b, m, c in (("scn", slice(159, 160 * NV, 160), NS, 20, 0.0625, 10.0), ("acc", slice(0, NS), 0, NS, 0.03125, 9.96875)):
-            ts(T.rf[:, a:b], T[src][:, n], m, c, O.mult, O.add, [src], [("rf", a, b)])
-            ts(T.rx[:, a:b], T[src][:, n], m, c - 0.46875, O.mult, O.add, [src], [("rx", a, b)])
-        tt(T.rf[:, 32:52], T.rf[:, 0:20], T.rx[:, 0:20], O.add, [("rf", 0, 20), ("rx", 0, 20)], [("rf", 32, 52)])
-        for e in range(2):
-            ts(T.offs[:, e:20:2], T.rf[:, 32 + 10 * e:42 + 10 * e], 16.0, cf(22), O.mult, O.add, [("rf", 32, 52), K(22)], [("offs", 10 * e, 10 * e + 10)])
-        V(lambda v: v.tensor_copy(T.win[:, 0:640].indirect(T.offs[:, 0:20]), T.vrow[:]), ["vrow", "offs"], ["win"])
-
-    def L(i):
-        return T.lx[:, 16 * i:16 * i + 10]
-
-    def LR(i):
-        return ("lx", 16 * i, 16 * i + 10)
+                more(p + 1)
+            else:
+                value(0)
+            a = 320 * (p % 3)
+            scan(R("scn", 160 * p, 160 * p + 160), R("fab", a, a + 160), R("fab", a + 160, a + 320), -160.0, O.add, O.add)
+        ts(R("offs", NS, 20), R("scn", 159, 160 * NV, 160), 160.0, O.add)
+        ts(R("offs", 0, NS - 2), R("acc", 0, NS - 2), -0.5, O.mult, 159.5, O.add)
+        scatter(R("win"), R("offs", NS, 20), R("vrow", 16 * NS, 320))
+        ts(R("offs", NS - 2, NS), R("acc", NS - 2, NS), -0.5, O.mult, 159.5, O.add)
+        scatter(R("win"), R("offs", 0, NS), R("vrow", 0, 16 * NS))
 
     def plane(n, b):
-        return (n, 320 * b, 320 * b + 320)
+        return R(n, 320 * b, 320 * b + 320)
 
     def laid(r):
-        V(lambda v: v.transpose(T.tw[:, 0:320], T.win[:, 0:320]), [("win", 0, 320)], [("tw", 0, 320)])
-        tt(L(0), T.tw[:, 0:320:32], T.tw[:, 16:320:32], O.add, [("tw", 0, 320)], [LR(0)])
-        ts(L(1), L(0), 511, None, O.bitwise_and, None, [LR(0)], [LR(1)])
-        ts(L(3), L(0), 512.0, None, O.is_lt, None, [LR(0)], [LR(3)])
-        ts(L(2), L(0), 9, None, O.arith_shift_right, None, [LR(0)], [LR(2)])
-        ts(T.ll[:, 0:10], L(1), -1.0, None, O.add, None, [LR(1)], ["ll"])
+        diagonal(R("dw", 0, 160), R("win", 0, 160), 160)
+        diagonal(R("dw", 160, 320), R("win", 160, 320), 160)
+        x = R("dw", 15, 160, 16)
+        ts(R("ll", 0, 10), x, 2.0 ** -10, O.mult, K(CL), O.add)
+        copy(R("lx", 0, 10), x)
         for b in range(4):
-            act(T.pz[:, 160 * b:160 * b + 160], T.fp[:, 320 * b:320 * b + 320].indirect(T.ll[:, 0:10]), AF.Copy, [plane("fp", b), "ll"], [("pz", 160 * b, 160 * b + 160)], scale=0.5)
-        tt(L(4), L(3), L(1), O.mult, [LR(3), LR(1)], [LR(4)])
-        tt(L(5), L(4), L(2), O.add, [LR(4), LR(2)], [LR(5)])
-        ts(T.bl[:, 0:10], L(5), -1.0, None, O.add, None, [LR(5)], ["bl"])
+            act(R("pz", 160 * b, 160 * b + 160), pick(plane("fp", b), R("ll", 0, 10)), scale=0.5)
+        ts(R("kl", 0, 10), R("dw", 175, 320, 16), 2.0 ** -10, O.mult, K(CL), O.add)
+        ts(R("lx", 16, 26), R("lx", 0, 10), 1023, O.bitwise_and)
+        ts(R("bl", 0, 10), R("lx", 16, 26), -1.0, O.mult, 511.0, O.add)
         for b in range(4):
-            tt(T.zt[:, b:640:4], T.f2[:, 320 * b:320 * b + 320].indirect(T.bl[:, 0:10]), T.pz[:, 160 * b:160 * b + 160], O.add,
-               [plane("f2", b), "bl", ("pz", 160 * b, 160 * b + 160)], [("zt", 160 * b, 160 * b + 160)])
+            tt(R("zt", b, 640, 4), pick(plane("f2", b), R("bl", 0, 10)), R("pz", 160 * b, 160 * b + 160), O.add)
         z, l = "z%d" % r, "l%d" % r
-        quant(z, 0, 160, "zt", 0, 640)
+        quant(z, 0, 160, "zt", 0)
         rid, pid, _ = topo.addr(nxt)
         m = topo.mask(core, nxt)
         arr = "arr%d" % r
-        waits("G", accesses(["q" + z, "s" + z + "_p"], []))
+        waits("G", accesses([R("q" + z), R("p" + z)], []))
         g.remote_dma(T["q" + l][:, 0:160].bitcast(dt.uint8), T["q" + z][:, 0:160].bitcast(dt.uint8), T.sem[arr], T.sem["loc"], pid, rid, m)
-        g.remote_dma(T["s" + l + "_p"][:, 0:160], T["s" + z + "_p"][:, 0:160], T.sem[arr], T.sem["loc"], pid, rid, m)
+        g.remote_dma(T["p" + l][:, 0:160], T["p" + z][:, 0:160], T.sem[arr], T.sem["loc"], pid, rid, m)
         k = 2 * len(topo.engines(core, nxt))
         count["loc"] = count.get("loc", 0) + k
         count[arr] = k
-        for n in ("q" + l, "s" + l + "_p"):
-            hist[n] = [[0, 160, "w", arr, k]]
+        for n in ("q" + l, "p" + l):
+            hist[n] = [[R(n)[1][0][1], "w", arr, k]]
 
     def kept(r):
-        V(lambda v: v.transpose(T.tw[:, 320:640], T.win[:, 320:640]), [("win", 320, 640)], [("tw", 320, 640)])
-        tt(L(6), T.tw[:, 320:640:32], T.tw[:, 336:640:32], O.add, [("tw", 320, 640)], [LR(6)])
-        ts(L(7), L(6), 511, None, O.bitwise_and, None, [LR(6)], [LR(7)])
-        ts(T.kl[:, 0:10], L(7), -1.0, None, O.add, None, [LR(7)], ["kl"])
         for b in range(4):
-            rd, wr = [plane("fp", b), "kl"], [("xk", 160 * b, 160 * b + 160)]
-            if b % 2:
-                act(T.xk[:, b:640:4], T.fp[:, 320 * b:320 * b + 320].indirect(T.kl[:, 0:10]), AF.Copy, rd, wr)
-            else:
-                V(lambda v: v.tensor_copy(T.xk[:, b:640:4], T.fp[:, 320 * b:320 * b + 320].indirect(T.kl[:, 0:10])), rd, wr)
-        quant(str(r + 1), 0, 160, "xk", 0, 640)
+            (act if b % 2 else copy)(R("xk", b, 640, 4), pick(plane("fp", b), R("kl", 0, 10)))
+        quant(str(r + 1), 0, 160, "xk", 0)
 
     def arrive(r):
         for b in range(4):
             mm(2 + b, 160, "w", 128 * b, "l%d" % r, 0, True, False)
             mm(2 + b, 160, "g", 128 * b, "l%d" % r, 0, False, True)
         for b in range(4):
-            pb, wr = "pb%d" % (2 + b), [("xh", 160 * b, 160 * b + 160)]
+            out, pb = R("xh", b, 640, 4), R("pb%d" % (2 + b), 0, 160)
             if b % 2:
-                ts(T.xh[:, b:640:4], T[pb][:, 0:160], 0.0078125, None, O.mult, None, [pb], wr)
+                ts(out, pb, 0.0078125, O.mult)
             else:
-                act(T.xh[:, b:640:4], T[pb][:, 0:160], AF.Copy, [pb], wr, scale=0.0078125)
-        quant(str(r + 1), 160, 320, "xh", 0, 640)
+                act(out, pb, scale=0.0078125)
+        quant(str(r + 1), 160, 320, "xh", 0)
 
-    def product_v(half):
-        mm(half, 160, "v", 0, "3", 160 * half)
-        for h in range(8):
-            a = 40 * h + 20 * half
-            act(T.yo[:, a:a + 20], T["pb%d" % half][:, h:160:8], AF.Copy, ["pb%d" % half], [("yo", a, a + 20)])
-
-    def flags(half, bank):
-        for h in range(8):
-            a = 40 * h + 20 * half
-            tt(T.fl[:, 64 + 4 * a:144 + 4 * a:4], T["pb%d" % bank][:, h:160:8], T.th[:, a:a + 20], O.is_gt, ["pb%d" % bank, "th"], [("fl", 64 + 4 * a, 144 + 4 * a)])
-
+    w = waiters()
+    run(w[0:2] + [lambda: ts(R("d1", 161, 162), ci(PD), -MISS, O.mult)] + w[2:4])
+    quant("u", 0, 128, "uv", 0)
+    for e in range(2):
+        quant("0", 160 * e, 160 * e + 160, "xt", 640 * e)
+        mm(e, 160, "u", 0, "0", 160 * e)
+    run(ends(0) + [lambda: ts(R("cf", 2, 514, 4), R("tgf"), K(GF), O.is_equal, K(WT), O.mult)] + w[4:6] + w[8:10])
     for r in range(3):
         if r == 0:
-            mm(0, 320, "up", 0, "0", 0)
-            for a in (0, 160):
-                tt(T.fl[:, 64 + 4 * a:704 + 4 * a:4], T.pb0[:, a:a + 160], T.th[:, a:a + 160], O.is_gt, ["pb0", "th"], [("fl", 64 + 4 * a, 704 + 4 * a)])
+            for e in range(2):
+                flags(e, 2 * e, 4)
+            run(w[6:7] + w[10:11])
         else:
-            mm(1, 160, "up", 0, str(r), 160)
-            flags(1, 1)
-        quant("f", 0, 176, "fl", 0, 704)
-        quant("f", 176, 352, "fl", 704, 1408)
-        symbols(0)
-        half = [lambda: V(lambda v: v.transpose(T.tl[:], T.pb3[:, 0:160]), ["pb3"], ["tl"])] + lists("tl", "off12", 0, 0, 10, 25) + lists("tl", "off12", 16, 2, 10, 27)
-        full = [lambda: V(lambda v: v.transpose(T.tlo[:], T.pb7[:, 0:320]), ["pb7"], ["tlo"])] + lists("tlo", "offd", 0, 0, 20, 29)
+            mm(0, 160, "u", 0, str(r), 160)
+            flags(0, 320, 2)
+        quant("f", 0, 162, "fl", 0)
+        products(0)
+        more = {k: [] for k in "abcdefghij"}
+        dec = decode(r)
         if r == 0:
-            conts(1, "b")
-            symbols(1)
-            stage(0, half + [lambda: conts(2, "c"), units])
-            symbols(2)
-            stage(1, [lambda: fill(T.kap[:], 0.0, ["kap"]), lambda: unit_done(0), lambda: fill(T.win[:], 0.0, ["win"]), lambda: unit_done(1)])
-            unit_done(2)
-            decode(r)
+            for e in range(2):
+                quant("c", 128 * e, 128 * e + 128, "cf", 2 - 2 * e)
+            products(1)
+            u = units()
+            more.update(a=w[7:8] + w[11:12], b=u[0:2], c=u[2:3], d=u[3:4], e=u[4:6], f=u[6:8], g=u[8:9], h=u[9:11],
+                        i=[lambda: ts(K(CK), K(CP), -4096.0, O.add), lambda: ts(K(CL), K(CP), -(2.0 ** -10), O.mult)])
+            more["decode"] = ([], [])
+            more["g"] = more["g"] + dec[0:4]
+            more["j"] = dec[4:8]
         else:
-            symbols(1)
-            symbols(2)
-            decode(r)
-            stage(0, half)
-            stage(1, [])
-        stage(2, full)
+            products(1)
+            more["decode"] = (dec[0:4], dec[4:8])
+        times(r, more)
         order(r)
         laid(r)
         kept(r)
         if r < 2:
-            mm(0, 160, "up", 0, str(r + 1), 0)
-            flags(0, 0)
+            mm(0, 160, "u", 0, str(r + 1), 0)
+            if r == 0:
+                run(ends(1))
+            flags(0, 0, 2)
         else:
-            quant("v", 0, 128, "uv", 512, 1024)
-            product_v(0)
-            for e in range(2):
-                ts(T.offo[:, e:20:2], T.rf[:, 10 * e:10 * e + 10], 16.0, None, O.mult, None, [("rf", 0, 20)], [("offo", 10 * e, 10 * e + 10)])
-            V(lambda v: v.tensor_copy(T.oprow[:, 0:320].indirect(T.offo[:, 0:20]), T.ccol[:]), ["ccol", "offo"], ["oprow"])
+            quant("v", 0, 128, "uv", 512)
+            mm(0, 160, "v", 0, "3", 0)
+            for h in range(8):
+                act(R("yo", 40 * h, 40 * h + 20), R("pb0", h, 160, 8))
+            scatter(R("oprow"), R("offs", 0, 20), R("ccol"))
             for k in range(8):
-                dma("Y", T.op[k:k + 1, :], T.oprow[16 * k:16 * k + 1, :], ["oprow"], [], "doy")
-
-            def N(i):
-                return T.nx[:, 20 * i:20 * i + 20]
-
-            def NR(i):
-                return ("nx", 20 * i, 20 * i + 20)
-            V(lambda v: v.tensor_copy(cf(41), ci(RK)), [C(RK)], [K(41)])
-            ts(N(1), N(0), cf(41), None, O.add, None, [NR(0), K(41)], [NR(1)])
-            ts(N(0), N(1), 205.0, None, O.mult, None, [NR(1)], [NR(0)])
-            ts(N(2), N(0), 13, None, O.arith_shift_right, None, [NR(0)], [NR(2)])
-            ts(N(0), N(2), -319.0, None, O.mult, None, [NR(2)], [NR(0)])
-            ts(N(2), N(1), 8.0, None, O.mult, None, [NR(1)], [NR(2)])
-            tt(T.fx[:, 96:116], N(0), N(2), O.add, [NR(0), NR(2)], [("fx", 96, 116)])
-            V(lambda v: v.tensor_copy(T.nat[:, 0:20], T.fx[:, 96:116]), [("fx", 96, 116)], ["nat"])
+                dma("Y", T.op[k:k + 1, :], T.oprow[16 * k:16 * k + 1, :], [R("oprow")], [], "doy")
+            diagonal(R("df"), R("natr"), 320)
+            ts(R("nat", 0, 20), R("df", 15, 320, 16), K(CP), O.subtract)
         arrive(r)
-    product_v(1)
-    dma("S", T.y[:], T.yo[:], ["yo"], [], "doa")
-    V(lambda v: v.tensor_copy(T["sn_p"][:, 0:320], T["s3_p"][:, 0:320].indirect(T.nat[:, 0:20])), ["s3_p", "nat"], ["sn_p"])
+    for e in range(2):
+        mm(e, 160, "v", 0, "3", 160)
+    act(R("pn"), pick(R("p3"), R("nat", 0, 20)))
+    copy(words(R("qn")), pick(words(R("q3")), R("nat", 0, 20)))
+    dma("Y", T.oc[:], T.qn[:].bitcast(dt.uint8), [R("qn")], [], "doy")
+    for h in range(8):
+        (act if h % 2 else copy)(R("yo", 40 * h + 20, 40 * h + 40), R("pb%d" % (h % 2), h, 160, 8))
     for k in range(4):
-        dma("S" if k % 2 else "Y", T.osc[4 * k:4 * k + 4, :], T["sn_p"][32 * k:32 * k + 4, :], ["sn_p"], [], "doa" if k % 2 else "doy")
-    V(lambda v: v.tensor_copy(T.qn[:, 0:320].bitcast(dt.uint32), T.q3[:, 0:320].bitcast(dt.uint32).indirect(T.nat[:, 0:20])), ["q3", "nat"], ["qn"])
-    dma("Y", T.oc[:], T.qn[:].bitcast(dt.uint8), ["qn"], [], "doy")
+        dma("Y", T.osc[4 * k:4 * k + 4, :], T.pn[32 * k:32 * k + 4, :], [R("pn")], [], "doy")
+    dma("S", T.y[:], T.yo[:], [R("yo")], [], "doa")
     for s in sorted(count):
         if known["G"].get(s, 0) < count[s]:
             g.wait_ge(T.sem[s], count[s])

@@ -1,7 +1,9 @@
 from concourse.mybir import dt, AluOpType as O, ActivationFunctionType as AF
 
-NS = 10
+NS = 9
 NV = 20 - NS
+EARLY = 6
+TAIL = 0
 TOP = 1023.0
 MISS = float(2 ** 22)
 KEEP = float(2 ** 19)
@@ -9,6 +11,12 @@ LOW = -1.0e9
 F4 = "float8_e4m3fn_x4"
 BLOCKS = (0, 1, 2, 3, 0, 0, 1, 1)
 WINDOW = (64, 128, 0)
+LISTS = {"off1": 0, "off2": 16, "ll": 32, "bl": 48, "kl": 64, "offd": 80, "offs": 112, "nat": 144, "first": 176}
+ROWS = ["dg", "hr0", "hr1", "si0", "si1", "ccol", "natr"]
+WIDTH = {"bfloat16": 2, "uint16": 2}
+PIECES = ((0, 6), (6, 10), (10, 16), (16, 20))
+TURNS = 3
+WAKE, LOAD, HOP, SLACK = 200, 2400, 2500, 30
 
 
 def _decl():
@@ -17,16 +25,17 @@ def _decl():
     def sb(names, n, t):
         for k in names.split():
             d[k] = ("sbuf", [128, n], t)
-    sb("xt fp f2", 1280, "bfloat16")
+    sb("xt fp", 1280, "bfloat16")
+    sb("f2", 1344, "bfloat16")
     sb("xk xh zt pz sj", 640, "bfloat16")
     sb("uv cs cd", 1024, "bfloat16")
     sb("cf eg eh zz", 520, "bfloat16")
-    sb("fl", 776, "bfloat16")
-    sb("fab", 960, "bfloat16")
-    sb("scn", 160 * NV, "bfloat16")
+    sb("fa fb", 776, "bfloat16")
+    sb("fab", 320 * 12, "bfloat16")
+    sb("scn", 160 * 12, "bfloat16")
     sb("w4 sg4 tgf ixg ixh", 128, "bfloat16")
     sb("jm jn", 320, "bfloat16")
-    for k, n in (("u", 128), ("v", 128), ("w", 512), ("h", 512), ("g", 512), ("s", 256), ("d", 256), ("c", 256), ("f", 194), ("n", 320)):
+    for k, n in (("u", 128), ("v", 128), ("w", 512), ("h", 512), ("g", 512), ("s", 256), ("d", 256), ("c", 256), ("a", 194), ("b", 194), ("n", 320)):
         d["q" + k] = ("sbuf", [128, n], F4)
         d["p" + k] = ("sbuf", [128, n], "uint8")
     for r in range(4):
@@ -36,19 +45,20 @@ def _decl():
         for k in ("z", "l"):
             d["q%s%d" % (k, r)] = ("sbuf", [128, 160], F4)
             d["p%s%d" % (k, r)] = ("sbuf", [128, 160], "uint8")
-    sb("dg hr0 hr1 si0 si1 ccol natr d0o dow row2 vrow yo oprow kap kas my win dw df", 320, "float32")
-    sb("n0 n1 n2 n3 d1 d2 cr0 cr1 mx", 200, "float32")
-    sb("d0 inc1 inc2 dl", 160, "float32")
+    sb("rows", 320 * len(ROWS), "float32")
+    sb("d0o dow row2 vrow yo oprow kas my win df", 320, "float32")
+    sb("dw", 320, "int32")
+    sb("n0 n1 n2 n3 d1 d2 cr0 cr1 mx my2", 200, "float32")
+    sb("d0 inc1 inc2 dl dm", 160, "float32")
     sb("one", 40, "float32")
     sb("acc", 20, "float32")
     sb("tb ta", 32, "float32")
-    sb("k", 48, "float32")
-    sb("wt mt am v16", 16, "float32")
-    sb("mi w8 ft", 16, "int32")
+    sb("k", 56, "float32")
+    sb("wt mt at am an ao v16", 16, "float32")
+    sb("mi w8", 16, "int32")
     sb("ci", 48, "int32")
-    sb("lx", 32, "int32")
-    sb("off1 off2 ll bl kl", 16, "uint16")
-    sb("offd offs nat", 32, "uint16")
+    sb("lx", 48, "int32")
+    sb("lists", 192, "uint16")
     sb("ku", 320, "uint16")
     for b in range(8):
         d["pb%d" % b] = ("psum", [128, 512], "float32")
@@ -56,7 +66,7 @@ def _decl():
 
 
 SCRATCH = _decl()
-SEMAPHORES = ["sV", "sS", "sP", "sG", "dx", "du", "dw", "dws", "dv", "arr0", "arr1", "arr2", "loc", "doy", "doa"]
+SEMAPHORES = ["sV", "sS", "sP", "sG", "dx0", "dx1", "du", "dw", "dws", "dv", "arr0", "arr1", "arr2", "loc", "doy", "doa"]
 
 
 def rank_program(g, core, T, topo):
@@ -66,39 +76,47 @@ def rank_program(g, core, T, topo):
     nxt = T.cores[(rank + 1) % len(T.cores)]
     queue = {"V": g.vector, "S": g.scalar, "P": g.tensor, "G": g, "Y": g.sync}
     own = {"V": "sV", "S": "sS", "P": "sP", "G": "sG"}
+    calls = []
     count = {}
     clock = {}
     known = {k: {} for k in queue}
     hist = {}
 
     def R(name, a=0, b=None, s=1):
+        if name in LISTS:
+            name, a, b = "lists", LISTS[name] + a, LISTS[name] + b
+        if name in ROWS:
+            at = 320 * ROWS.index(name)
+            name, a, b = "rows", at + a, at + (320 if b is None else b)
         b = SCRATCH[name][1][1] if b is None else b
         m = 0
         for c in range(a, b, s):
             m |= 1 << c
         if name[:2] == "pb":
             m = 1
-        return (T[name][:, a:b:s] if s > 1 else T[name][:, a:b], [(name, m)])
+        return (T[name][:, a:b:s] if s > 1 else T[name][:, a:b], [(name, m)], len(range(a, b, s)), WIDTH.get(SCRATCH[name][2], 4))
 
     def pick(win, off):
-        return (win[0].indirect(off[0]), win[1] + off[1])
+        return (win[0].indirect(off[0]), win[1] + off[1], 16 * off[2], 0)
 
     def words(v):
-        return (v[0].bitcast(dt.uint32), v[1])
+        return (v[0].bitcast(dt.uint32),) + v[1:]
 
     def accesses(reads, writes):
         r = [a for v in reads if isinstance(v, tuple) for a in v[1]]
         return [(a, "p" if a[0][:2] == "pb" else "r") for a in r] + [(a, "w") for v in writes for a in v[1]]
 
+    def clash(b, k0, k1, same):
+        if b == "turn" or (k0 == "r" and k1 == "r"):
+            return False
+        return not (b[:2] == "pb" and k0 == k1 and same)
+
     def waits(q, acc):
         need = {}
         for (b, m), kind in acc:
             for e in hist.get(b, []):
-                if not e[0] & m or (kind == "r" and e[1] == "r"):
-                    continue
-                if b[:2] == "pb" and kind == ("w" if e[1] == "w" else "p") and own.get(q) == e[2]:
-                    continue
-                need[e[2]] = max(need.get(e[2], 0), e[3])
+                if e[0] & m and clash(b, e[1], kind, own.get(q) == e[2]):
+                    need[e[2]] = max(need.get(e[2], 0), e[3])
         kn = known[q]
         for s in sorted(need, key=lambda s: -need[s]):
             if kn.get(s, 0) >= need[s]:
@@ -120,335 +138,378 @@ def rank_program(g, core, T, topo):
                 h[:] = [e for e in h if e[0] & ~m]
             h.append([m, kind, sem, v])
 
-    def op(q, call, reads, writes):
-        acc = accesses(reads, writes)
-        waits(q, acc)
-        call(queue[q]).then_inc(T.sem[own[q]], 1)
-        record(q, own[q], 1, acc)
+    strict = []
+
+    def op(q, call, reads, writes, time):
+        calls.append((q, own[q], 1, call, accesses(reads, writes) + [(("turn", 1), "w")] * (q in strict), time, WAKE))
 
     def dma(q, out, in_, reads, writes, sem):
-        acc = accesses(reads, writes)
-        waits(q, acc)
-        queue[q].dma_start(out, in_).then_inc(T.sem[sem], 16)
-        record(q, sem, 16, acc)
+        calls.append((q, sem, 16, lambda e: e.dma_start(out, in_), accesses(reads, writes), 60, LOAD))
+
+    def issue():
+        last, before = {}, []
+        for i, c in enumerate(calls):
+            p = {}
+            for (b, m), kind in c[4]:
+                for mj, kj, j in last.get(b, []):
+                    if mj & m and clash(b, kj, kind, calls[j][0] == c[0]):
+                        p[j] = calls[j][5] + calls[j][6]
+                    elif mj & m and kind == "w":
+                        p.setdefault(j, calls[j][5])
+            for (b, m), kind in c[4]:
+                h = last.setdefault(b, [])
+                if kind == "w":
+                    h[:] = [e for e in h if e[0] & ~m]
+                h.append((m, kind, i))
+            before.append(p)
+        chain = [c[5] + c[6] for c in calls]
+        after = [{} for c in calls]
+        for i in range(len(calls) - 1, -1, -1):
+            for j, d in before[i].items():
+                chain[j] = max(chain[j], d + chain[i])
+                after[j][i] = calls[i][5] + d - calls[j][5]
+
+        def place(urge, links, first):
+            start, busy = {}, {q: [] for q in queue}
+            for i in sorted(range(len(calls)), key=lambda i: -urge[i]):
+                q, time = calls[i][0], calls[i][5]
+                t = max([start[j] + d for j, d in links[i].items()] + [first[i]])
+                for a, b in sorted(busy[q]):
+                    if t < a and t + time <= a + SLACK:
+                        break
+                    t = max(t, b)
+                start[i] = t
+                busy[q].append((t, t + time))
+            return start, [start[i] + c[5] for i, c in enumerate(calls)]
+        start, end = place(chain, before, [0] * len(calls))
+        for _ in range(TURNS):
+            start, end = place(place(end, after, [c[6] for c in calls])[1], before, [0] * len(calls))
+        for i in sorted(start, key=lambda i: (start[i], i)):
+            q, sem, n, call, acc = calls[i][:5]
+            waits(q, acc)
+            if n:
+                call(queue[q]).then_inc(T.sem[sem], n)
+                record(q, sem, n, acc)
+            else:
+                call(queue[q])
+
+    def cycles(n, *v):
+        full = [x for x in v if x[2] > 1]
+        if any(x[3] == 0 for x in full):
+            return 50 + 1.3 * n
+        return 0.83 * max(64, n / 2 if full and all(x[3] == 2 for x in full) else n)
 
     def ap(v):
         return v[0] if isinstance(v, tuple) else v
 
     def ts(out, a, s1, o0, s2=None, o1=None):
         if o1 is None:
-            op("V", lambda v: v.tensor_scalar(out[0], a[0], ap(s1), None, o0), [a, s1], [out])
+            op("V", lambda v: v.tensor_scalar(out[0], a[0], ap(s1), None, o0), [a, s1], [out], cycles(out[2], out, a))
         else:
-            op("V", lambda v: v.tensor_scalar(out[0], a[0], ap(s1), ap(s2), o0, o1), [a, s1, s2], [out])
+            op("V", lambda v: v.tensor_scalar(out[0], a[0], ap(s1), ap(s2), o0, o1), [a, s1, s2], [out], cycles(out[2], out, a))
 
     def tt(out, a, b, o):
-        op("V", lambda v: v.tensor_tensor(out[0], a[0], b[0], o), [a, b], [out])
+        both = a[3] and "pb" not in (a[1][0][0][:2], b[1][0][0][:2])
+        op("V", lambda v: v.tensor_tensor(out[0], a[0], b[0], o), [a, b], [out], cycles(2 * out[2]) if both else cycles(out[2], a))
 
     def copy(out, a):
-        op("V", lambda v: v.tensor_copy(out[0], a[0]), [a], [out])
+        op("V", lambda v: v.tensor_copy(out[0], a[0]), [a], [out], cycles(out[2], out, a))
 
     def scatter(win, off, a):
-        op("V", lambda v: v.tensor_copy(win[0].indirect(off[0]), a[0]), [a, off], [win])
+        op("V", lambda v: v.tensor_copy(win[0].indirect(off[0]), a[0]), [a, off], [win], 50 + 3.2 * a[2])
 
     def fill(out, val):
-        op("V", lambda v: v.memset(out[0], val), [], [out])
+        op("V", lambda v: v.memset(out[0], val), [], [out], cycles(out[2], out))
 
     def scan(out, a, b, init, o0, o1):
-        op("V", lambda v: v.tensor_tensor_scan(out[0], a[0], b[0], ap(init), o0, o1), [a, b, init], [out])
+        op("V", lambda v: v.tensor_tensor_scan(out[0], a[0], b[0], ap(init), o0, o1), [a, b, init], [out], cycles(out[2], out, a, b))
 
     def turn(out, a):
-        op("V", lambda v: v.transpose(out[0], a[0]), [a], [out])
+        op("V", lambda v: v.transpose(out[0], a[0]), [a], [out], cycles(out[2]))
 
     def act(out, a, f=AF.Copy, acc=None, **kw):
         more = {k: ap(v) for k, v in kw.items()}
         if acc:
             more["accum_out"] = acc[0]
-        op("S", lambda s: s.activation(out[0], a[0], f, **more), [a] + list(kw.values()), [out] + ([acc] if acc else []))
+        op("S", lambda s: s.activation(out[0], a[0], f, **more), [a] + list(kw.values()), [out] + ([acc] if acc else []),
+           (cycles(out[2]) if a[3] else 65 + 1.3 * out[2]) + (20 if acc else 0))
 
     def iota(out, pat, base=0, cm=0):
-        if SCRATCH[out[1][0][0]][2] == "int32":
-            op("G", lambda e: e.iota(out[0], pat, base, cm), [], [out])
-        else:
-            op("G", lambda e: e.iota(out[0], pat, base, cm, allow_small_or_imprecise_dtypes=True), [], [out])
+        more = {} if SCRATCH[out[1][0][0]][2] == "int32" else {"allow_small_or_imprecise_dtypes": True}
+        op("G", lambda e: e.iota(out[0], pat, base, cm, **more), [], [out], 130 + 1.66 * out[2])
 
     def level(name, a, b, val, s=1):
         iota(R(name, a, b, s), [[0, len(range(a, b, s))]], int(val))
 
     def quant(k, a, b, tile, lo):
         q, p, t = R("q" + k, a, b), R("p" + k, a, b), R(tile, lo, lo + 4 * (b - a))
-        op("V", lambda v: v.quantize_mx(q[0], p[0], t[0]), [t], [q, p])
+        op("V", lambda v: v.quantize_mx(q[0], p[0], t[0]), [t], [q, p], 12 + 0.22 * t[2])
 
     def mm(bank, n, k, a, m, b, start=True, stop=True):
         v = [R("q" + k, a, a + 128), R("p" + k, a, a + 128), R("q" + m, b, b + n), R("p" + m, b, b + n)]
         out = R("pb%d" % bank, 0, n)
-        op("P", lambda t: t.matmul_mx(out[0], v[0][0], v[1][0], v[2][0], v[3][0], start, stop), v, [out])
+        op("P", lambda t: t.matmul_mx(out[0], v[0][0], v[1][0], v[2][0], v[3][0], start, stop), v, [out], 0.5 * (n + 16))
 
-    def diagonal(out, row, n):
-        scan(out, R("dg", 0, n), row, LOW, O.add, O.max)
+    def diagonal(out, row):
+        scan(out, R("dg", 0, row[2]), row, LOW, O.add, O.max)
 
-    def run(calls):
-        for c in calls:
-            c()
+    def half(n, e):
+        return R(n, 160 * e, 160 * e + 160)
 
-    dma("Y", T.xt[:], T.x[:], [], [R("xt")], "dx")
+    for e in range(2):
+        dma("Y", T.xt[:, 640 * e:640 * e + 640], T.x[:, 640 * e:640 * e + 640], [], [R("xt", 640 * e, 640 * e + 640)], "dx%d" % e)
     dma("S", T.uv[:, 0:512], T.u[:], [], [R("uv", 0, 512)], "du")
-    g.sync.wait_ge(T.sem["dx"], 16)
-    dma("Y", T.qw[:].bitcast(dt.uint8), T.wc[:], [], [R("qw")], "dw")
-    dma("Y", T.pw[:], T.ws[:], [], [R("pw")], "dws")
-    dma("Y", T.uv[:, 512:1024], T.v[:], [], [R("uv", 512, 1024)], "dv")
+    dma("Y", T.qw[:].bitcast(dt.uint8), T.wc[:], [R("xt")], [R("qw")], "dw")
+    dma("Y", T.pw[:], T.ws[:], [R("xt")], [R("pw")], "dws")
+    dma("Y", T.uv[:, 512:1024], T.v[:], [R("xt")], [R("uv", 512, 1024)], "dv")
 
     def ci(i):
         return R("ci", i, i + 1)
 
-    def K(i):
-        return R("k", i, i + 1)
+    def K(i, n=1):
+        return R("k", i, i + n)
     RK, SG, S1, S2, HF, BK, GR, PC, PD = range(1, 10)
-    RF, GF, PF, LT3, WA, WT, RA, RW, CP, NK, I0, CK, CL, CN = range(14)
-    WM, MK, LA, LB, G4, WH = 16, 20, 24, 28, 32, 36
+    RF, GF, PF, LT3, WA, WT, RA, RW, CP, I0, CK, CL = range(12)
+    WM, MK, LA, LB, G4, WH, WI, C8 = 16, 20, 24, 28, 32, 36, 40, 48
     iota(ci(0), [[1, 1]], 0, 1)
-    iota(R("k", G4, G4 + 4), [[1, 4]])
+    iota(K(G4, 4), [[1, 4]])
+    iota(K(C8, 8), [[1, 8]], 320)
     iota(R("v16"), [[0, 2], [1, 8]])
     level("one", 0, 40, -1)
     iota(R("jm"), [[0, 20], [1, 16]])
     iota(R("tgf"), [[1, 8], [0, 16]])
     for i, low in enumerate((-TOP, -TOP, -1, -1)):
-        level("n%d" % i, 160, 161, -(2 ** 24 - 1))
-        level("n%d" % i, 161, 193, low)
+        level("n%d" % i, 160, 193, low)
     level("wt", 8, 16, TOP)
     level("d1", 162, 193, 0)
     level("d2", 162, 193, 0)
     level("cr0", 1, 160, 1)
     level("cr0", 40, 160, 513, 40)
     level("n3", 0, 160, 0)
-    level("mt", 8, 16, 1023)
+    level("mt", 8, 16, 1025)
+    level("at", 8, 16, 0)
     iota(R("ixg"), [[1, 128]])
     iota(R("ixh"), [[16, 4], [0, 2], [1, 16]])
     iota(R("ixh", 0, 16), [[1, 16]], 112)
     iota(R("si0"), [[1, 320]])
     level("w8", 8, 16, 8 * TOP)
-    level("ft", 8, 16, 511)
-    iota(R("hr0"), [[-1, 8], [0, 40]], 7)
+    iota(R("hr0"), [[-1, 8], [0, 40]], 4103)
     level("cr1", 1, 160, 1026)
     level("cr1", 4, 160, -3070, 4)
     iota(R("si1"), [[1, 2], [2, 160]])
-    iota(R("hr1"), [[-1, 2], [0, 40], [-2, 4]], 7)
+    iota(R("hr1"), [[-1, 2], [0, 40], [-2, 4]], 4103)
     iota(R("ccol"), [[40, 2], [1, 40], [80, 4]])
     iota(R("natr"), [[1, 8], [8, 40]])
 
     fill(R("zz"), 0.0)
     fill(R("w4"), 0.0)
     fill(R("sg4"), 0.0)
-    ts(ci(RK), ci(0), 15, O.bitwise_and)
-    ts(ci(GR), ci(0), 4, O.arith_shift_right)
-    act(R("fl", 0, 520), R("zz"))
-    act(R("fl", 520, 776), R("zz", 0, 256))
+    for n in ("fa", "fb"):
+        act(R(n, 0, 520), R("zz"))
+        act(R(n, 520, 776), R("zz", 0, 256))
+    for n in ("cf", "eg", "eh"):
+        act(R(n), R("zz"))
     fill(R("w4", 0, 64, 4), 1.0)
     fill(R("w4", 66, 128, 4), 1.0)
+    ts(ci(RK), ci(0), 15, O.bitwise_and)
+    ts(ci(GR), ci(0), 4, O.arith_shift_right)
+    ts(ci(SG), ci(0), 7, O.bitwise_and)
+    ts(ci(S1), ci(0), 7, O.bitwise_and, 1, O.arith_shift_right)
+    ts(ci(S2), ci(0), 7, O.bitwise_and, 2, O.arith_shift_right)
+    ts(ci(HF), ci(0), 16, O.bitwise_and, 4, O.arith_shift_right)
+    ts(ci(BK), ci(0), 5, O.arith_shift_right)
+    tt(ci(PC), ci(SG), ci(S1), O.subtract)
+    tt(ci(PD), ci(PC), ci(S2), O.subtract)
+    copy(K(RF), ci(RK))
+    copy(K(GF), ci(GR))
+    copy(K(PF), ci(0))
     ts(K(WA), ci(RK), -2.0, O.mult, 4.0, O.add)
     ts(K(LT3), ci(RK), 3.0, O.is_lt)
     ts(K(RA), ci(RK), 0.25, O.mult, 0.25, O.add)
-    copy(K(GF), ci(GR))
-    ts(ci(SG), ci(0), 7, O.bitwise_and)
     ts(K(WT), K(WA), 1.0, O.max, K(LT3), O.mult)
     ts(K(RW), ci(RK), -1.0, O.add, K(RA), O.max)
-    ts(R("k", MK, MK + 4), R("k", G4, G4 + 4), K(GF), O.is_equal, K(LT3), O.mult)
-    ts(ci(S1), ci(0), 7, O.bitwise_and, 1, O.arith_shift_right)
-    ts(ci(S2), ci(0), 7, O.bitwise_and, 2, O.arith_shift_right)
-    ts(R("k", WM, WM + 4), R("k", G4, G4 + 4), K(GF), O.is_equal, K(WT), O.mult)
+    ts(K(MK, 4), K(G4, 4), K(GF), O.is_equal, K(LT3), O.mult)
+    ts(K(WM, 4), K(G4, 4), K(GF), O.is_equal, K(WT), O.mult)
     ts(R("ci", 16, 32), R("v16"), K(RW), O.mult, -0.375, O.add)
-    copy(K(RF), ci(RK))
-    tt(ci(PC), ci(SG), ci(S1), O.subtract)
     ts(R("ci", 32, 48), R("ci", 16, 32), 1, O.bitwise_and)
-    for i, b in enumerate(BLOCKS):
-        act(R("cs", 128 * i, 128 * i + 128), R("w4"), AF.Identity, scale=K(WM + b))
-    tt(ci(PD), ci(PC), ci(S2), O.subtract)
-    ts(ci(HF), ci(0), 16, O.bitwise_and, 4, O.arith_shift_right)
-    ts(ci(BK), ci(0), 5, O.arith_shift_right)
     for at, sign in ((0, 1.0), (1, -1.0), (66, 1.0), (67, -1.0)):
         ts(R("sg4", at, at + 61, 4), R("ci", 32, 48), -2.0 * MISS * sign, O.mult, MISS * sign, O.add)
-    ts(K(I0), ci(PD), -MISS, O.mult, TOP, O.add)
-    ts(K(CP), ci(RK), -KEEP, O.mult, 15.0 * KEEP, O.add)
-    ts(R("jn"), R("jm"), K(RF), O.is_gt, 33.0, O.mult)
     for i, b in enumerate(BLOCKS):
+        act(R("cs", 128 * i, 128 * i + 128), R("w4"), AF.Identity, scale=K(WM + b))
         ts(R("cd", 128 * i, 128 * i + 128), R("sg4"), K(MK + b), O.mult)
-    act(R("dg"), R("jn"), AF.Identity, scale=KEEP, bias=-32.0 * KEEP)
-    for n in ("cf", "eg", "eh"):
-        act(R(n), R("zz"))
-    quant("f", 66, 194, "fl", 264)
     quant("s", 0, 256, "cs", 0)
     quant("d", 0, 256, "cd", 0)
-
-    def waiters():
-        out = []
-        for i, (src, least, unit, one) in enumerate(((BK, 2.0, 1.0, 0.0), (BK, 1.0, 2.0 ** -12, 1.0), (GR, 1.0, 0.125, 1.0))):
-            out += [lambda i=i, src=src, least=least, unit=unit: ts(K(LA + i), ci(src), least, O.is_ge, unit, O.mult),
-                    lambda i=i, src=src, least=least, one=one: ts(K(WH + i), ci(src), least, O.is_lt, 8.0 + one, O.mult),
-                    lambda i=i, one=one: ts(K(WH + 4 + i), K(LA + i), K(CP), O.mult, one, O.add),
-                    lambda i=i: tt(K(LB + i), K(WH + i), K(WH + 4 + i), O.subtract)]
-        return out
-
-    def ends(r):
-        e, last = ((2208.0, 4095.0 - 552 * 3 - 39), (513.0, 4095.0 - 8 * 39 - 1026 * 3))[r]
+    ts(R("cf", 2, 514, 4), R("tgf"), K(GF), O.is_equal, K(WT), O.mult)
+    for e in range(2):
+        quant("c", 128 * e, 128 * e + 128, "cf", 2 - 2 * e)
+    ts(K(I0), ci(PD), -MISS, O.mult, TOP, O.add)
+    ts(R("d1", 161, 162), ci(PD), -MISS, O.mult)
+    ts(K(CP), ci(RK), -KEEP, O.mult, 15.0 * KEEP, O.add)
+    act(K(CK), K(CP), AF.Identity, bias=511.0)
+    act(K(CL), K(CP), AF.Identity, scale=-(2.0 ** -10))
+    ts(R("jn"), R("jm"), K(RF), O.is_gt, 33.0, O.mult)
+    act(R("dg"), R("jn"), AF.Identity, scale=KEEP, bias=-32.0 * KEEP)
+    for i, (src, least, unit, one) in enumerate(((BK, 2.0, 1.0, 0.0), (BK, 1.0, 2.0 ** -12, 1.0), (GR, 1.0, 0.125, 1.0))):
+        ts(K(LA + i), ci(src), least, O.is_ge, unit, O.mult)
+        ts(K(WH + i), ci(src), least, O.is_lt, 8.0 + one, O.mult)
+        act(K(WI + i), K(LA + i), AF.Identity, scale=K(CP), bias=one)
+        act(K(LB + i), K(WI + i), AF.Identity, scale=-1.0, bias=K(WH + i))
+    for r, (e, end) in enumerate(((2208.0, 4095.0 - 552 * 3 - 39), (513.0, 4095.0 - 8 * 39 - 1026 * 3))):
         n = "cr%d" % r
-        return [lambda: ts(R(n, 0, 1), ci(HF), e, O.mult, -4095.0, O.add),
-                lambda: ts(R(n, 160, 161), ci(HF), -e, O.mult, last, O.add),
-                lambda: ts(R(n, 161, 162), ci(PD), -MISS, O.mult)]
-
-    def units():
-        out = [lambda: copy(K(PF), ci(0)),
-               lambda: ts(R("eg", 3, 515, 4), R("ixg"), K(PF), O.is_equal, 128.0, O.mult),
-               lambda: ts(R("eh", 3, 515, 4), R("ixh"), K(PF), O.is_equal)]
-        for k in "gh":
-            out += [lambda k=k, b=b: quant(k, 128 * b, 128 * b + 128, "e" + k, 3 - b) for b in range(4)]
-        return out
+        ts(R(n, 0, 1), ci(HF), e, O.mult, -4095.0, O.add)
+        ts(R(n, 160, 161), ci(HF), -e, O.mult, end, O.add)
+        ts(R(n, 161, 162), ci(PD), -MISS, O.mult)
+    ts(R("eg", 3, 515, 4), R("ixg"), K(PF), O.is_equal, 128.0, O.mult)
+    ts(R("eh", 3, 515, 4), R("ixh"), K(PF), O.is_equal)
+    for k in "gh":
+        for b in range(4):
+            quant(k, 128 * b, 128 * b + 128, "e" + k, 3 - b)
 
     def stack(name, r, h, at=0):
         return R(name, at + 40 * h, at + 40 * h + 40) if r == 0 else R(name, at + h, at + 160, 4)
 
     def flags(bank, at, step):
-        for a in (at, at + 5):
-            ts(R("fl", a, a + 160 * step - 1, step), R("pb%d" % bank, 0, 160), 0.0, O.is_gt)
-
-    def products(part):
-        if part == 0:
-            for st in range(3):
-                mm(2 * st, 160, "s", WINDOW[st], "f", 0)
-                mm(2 * st + 1, 194 if st == 0 else 162, "d", WINDOW[st], "f", 0)
-        else:
-            for e in range(2):
-                mm(6 + e, 160, "c", 128 * e, "f", 0)
-
-    def decode(r):
-        out = []
-        for i in range(8):
-            k, dst, b, sc = ("g", "fp", i, 0.0078125) if i < 4 else ("h", "f2", i - 4, 0.5)
-
-            def one(k=k, dst=dst, b=b, sc=sc, bank=2 + i % 2):
-                mm(bank, 320, k, 128 * b, str(r), 0)
-                act(R(dst, 320 * b, 320 * b + 320), R("pb%d" % bank, 0, 320), scale=sc)
-            out.append(one)
-        return out
-
-    def stage(r, st, gaps):
-        n = "n%d" % st
-        if st:
-            act(R("d0"), pick(R("wt"), R("off%d" % st, 0, 10)), AF.Abs, scale=(1.0, 4096.0)[st - 1])
-        run(gaps[0])
-        for h in range(4):
-            if st:
-                scan(stack(n, r, h), stack("d0", r, h), stack("inc%d" % st, r, h), -LOW, O.min, O.subtract)
-            else:
-                scan(stack(n, r, h), R("one"), stack("pb0", r, h), K(I0), O.add, O.subtract)
-        run(gaps[1])
-        scan(R("mx", 0, 193), R(("pb1", "d1", "d2")[st], 0, 193), R(n, 0, 193), LOW, O.add, O.max)
-        run(gaps[2])
-        turn(R("tb"), R("mx", 161, 193))
-        run(gaps[3])
-        tt(R("mi" if st == 2 else "wt", 0, 8), R("tb", 0, 8), R("tb", 16, 24), O.max)
-        run(gaps[4])
+        for n, a in (("fa", at), ("fb", at + 5)):
+            ts(R(n, a, a + 160 * step - 1, step), R("pb%d" % bank, 0, 160), 0.0, O.is_gt)
 
     def listed(off, n, row, i):
-        return lambda: ts(R(off, 0, n), R(row, 15, 16 * n, 16), K(LA + i), O.mult, K(LB + i), O.add)
+        ts(R(off, 0, n), R(row, 15, 16 * n, 16), K(LA + i), O.mult, K(LB + i), O.add)
 
-    def times(r, more):
+    def symbols(r):
         c = min(r, 1)
-        dec = more["decode"]
+        quant("a", 0, 160 if r else 194, "fa", 0)
+        quant("b", 0, 162 if r else 194, "fb", 0)
+        for st in range(3):
+            mm(2 * st, 160, "s", WINDOW[st], "a", 0)
+            mm(2 * st + 1, 162 if st else 194, "d", WINDOW[st], "a", 0, True, False)
+            mm(2 * st + 1, 162 if st else 194, "d", WINDOW[st], "b", 0, False, True)
+        for e in range(2):
+            mm(6 + e, 160, "c", 128 * e, "a", 0)
+            act(half("dow", e), R("pb%d" % (6 + e), 0, 160), AF.Identity, scale=8.0, bias=8.0)
+            diagonal(half("df", e), half("dow", e))
+        listed("offd", 20, "df", 2)
+        diagonal(R("dl"), R("pb2", 0, 160))
+        listed("off1", 10, "dl", 0)
+        act(R("inc1"), R("pb2", 0, 160), AF.Identity, bias=1.0)
+        act(R("d1", 0, 161), R("pb3", 0, 161))
+        act(R("inc2"), R("pb4", 0, 160), AF.Identity, scale=4096.0, bias=4096.0)
+        diagonal(R("dm"), R("inc2"))
+        listed("off2", 10, "dm", 1)
+        tt(R("d2", 0, 162), R("pb5", 0, 162), R("cr%d" % c, 0, 162), O.add)
+        scan(R("my2", 0, 193), R("d2", 0, 193), R("n3", 0, 193), LOW, O.add, O.max)
+        turn(R("ta"), R("my2", 161, 193))
+        tt(R("am", 0, 8), R("ta", 0, 8), R("ta", 16, 24), O.max)
+        ts(R("mt", 0, 8), R("am", 0, 8), 0.0, O.is_lt, 1024.0, O.add)
+        ts(R("am", 8, 16), R("am", 0, 8), 0.0, O.is_ge)
+        tt(R("at", 0, 8), R("am", 8, 16), K(C8, 8), O.mult)
+        for a, b in PIECES:
+            tt(R("row2", 16 * a, 16 * b), pick(R("mt"), R("offd", a, b)), R("si%d" % c, 16 * a, 16 * b), O.mult)
+            tt(R("vrow", 16 * a, 16 * b), pick(R("at"), R("offd", a, b)), R("row2", 16 * a, 16 * b), O.add)
 
-        def half(n, e):
-            return R(n, 160 * e, 160 * e + 160)
-        dow = [lambda e=e: act(half("dow", e), R("pb%d" % (6 + e), 0, 160), AF.Identity, scale=8.0, bias=8.0) for e in range(2)]
-        stage(r, 0, [more["a"],
-                     [lambda: diagonal(R("dl"), R("pb2", 0, 160), 160),
-                      lambda: act(R("d1", 0, 161), R("pb3", 0, 161)),
-                      lambda: act(R("inc2"), R("pb4", 0, 160), AF.Identity, scale=4096.0, bias=4096.0),
-                      lambda: act(R("inc1"), R("pb2", 0, 160), AF.Identity, bias=1.0)],
-                     [listed("off1", 10, "dl", 0)] + more["b"],
-                     [lambda: tt(R("d2", 0, 162), R("pb5", 0, 162), R("cr%d" % c, 0, 162), O.add)],
-                     more["c"] + dow])
-        stage(r, 1, [[lambda: diagonal(R("dl"), R("inc2"), 160),
-                      lambda: scan(R("mx", 0, 193), R("d2", 0, 193), R("n3", 0, 193), LOW, O.add, O.max),
-                      lambda: diagonal(half("df", 0), half("dow", 0), 160),
-                      lambda: diagonal(half("df", 1), half("dow", 1), 160),
-                      lambda: turn(R("ta"), R("mx", 161, 193))] + dec[0],
-                     [listed("off2", 10, "dl", 1), listed("offd", 20, "df", 2), lambda: tt(R("am", 0, 8), R("ta", 0, 8), R("ta", 16, 24), O.max)],
-                     [lambda: ts(R("mt", 0, 8), R("am", 0, 8), 0.0, O.is_ge, 1023.0, O.add)] + more["d"],
-                     more["e"], more["f"]])
-        stage(r, 2, [[lambda e=e: tt(half("row2", e), pick(R("mt"), R("offd", 10 * e, 10 * e + 10)), half("si%d" % c, e), O.mult) for e in range(2)] + dec[1],
-                     more["g"], more["h"], more["i"], more["j"]])
+    def plane(n, b, w=320):
+        a = b * (SCRATCH[n][1][1] // 4)
+        return R(n, a, a + w)
+
+    def decode(r):
+        for i in range(8):
+            k, dst, b, sc = ("g", "fp", i - 4, 0.0078125) if i >= 4 else ("h", "f2", i, 0.5)
+            mm(2 + i % 2, 320, k, 128 * b, str(r), 0)
+            act(plane(dst, b), R("pb%d" % (2 + i % 2), 0, 320), scale=sc)
+
+    def times(r):
+        for st in range(3):
+            n = "n%d" % st
+            if st:
+                act(R("d0"), pick(R("wt"), R("off%d" % st, 0, 10)), AF.Abs, scale=(1.0, 4096.0)[st - 1])
+            for h in range(4):
+                if st:
+                    scan(stack(n, r, h), stack("d0", r, h), stack("inc%d" % st, r, h), -LOW, O.min, O.subtract)
+                else:
+                    scan(stack(n, r, h), R("one"), stack("pb0", r, h), K(I0), O.add, O.subtract)
+            scan(R("mx", 0, 193), R(("pb1", "d1", "d2")[st], 0, 193), R(n, 0, 193), LOW, O.add, O.max)
+            turn(R("tb"), R("mx", 161, 193))
+            w = 16 if st == 2 else 8
+            tt(R("mi" if st == 2 else "wt", 0, w), R("tb", 0, w), R("tb", 16, 16 + w), O.max)
         ts(R("w8", 0, 8), R("mi", 0, 8), 9, O.arith_shift_right, 0x1FF8, O.bitwise_and)
-        ts(R("ft", 0, 8), R("mi", 0, 8), 511, O.bitwise_and)
+        ts(R("lx", 32, 48), R("mi"), 511, O.bitwise_and)
+        diagonal(R("ao"), R("lx", 32, 48))
+        ts(R("first", 0, 1), R("ao", 15, 16), -1.0, O.mult, K(CK), O.add)
+        for b in range(4):
+            act(R("f2", 336 * b + 320, 336 * b + 336), pick(plane("f2", b), R("first", 0, 1)))
 
     def order(r):
         c = min(r, 1)
-
-        def half(n, e):
-            return R(n, 160 * e, 160 * e + 160)
+        strict.append("V")
         for e in range(2):
             tt(half("d0o", e), pick(R("w8"), R("offd", 10 * e, 10 * e + 10)), half("hr%d" % c, e), O.add)
         for e in range(2):
             for h in range(4):
-                scan(stack("kap", r, h, 160 * e), stack("d0o", r, h, 160 * e), stack("dow", r, h, 160 * e), -LOW, O.min, O.subtract)
-            act(half("kas", e), half("kap", e), AF.Identity, bias=K(CP))
+                scan(stack("ku", r, h, 160 * e), stack("d0o", r, h, 160 * e), stack("dow", r, h, 160 * e), -LOW, O.min, O.subtract)
+            act(half("kas", e), half("ku", e), AF.Identity, bias=K(CP))
         for e in range(2):
-            diagonal(half("my", e), half("kap", e), 160)
-            ts(half("ku", e), half("kap", e), 4096.0, O.add)
+            diagonal(half("my", e), half("ku", e))
 
         def mine(q):
             return R("my", 16 * q + 15, 16 * q + 16)
+
+        def places(a, b):
+            ts(R("offs", a, b), R("acc", a, b), -0.5, O.mult, 159.5, O.add)
+
+        def lay(a, b):
+            scatter(R("win"), R("offs", a, b), R("vrow", 16 * a, 16 * b))
         for q in range(NS):
             act(R("sj", 320 * (q % 2), 320 * (q % 2) + 320), R("kas"), AF.Sign, acc=R("acc", q, q + 1), scale=-1.0, bias=mine(q))
-
-        def value(e):
-            tt(half("vrow", e), pick(R("ft"), R("offd", 10 * e, 10 * e + 10)), half("row2", e), O.add)
-
-        def more(p):
-            ts(R("fab", 320 * (p % 3), 320 * (p % 3) + 320), R("ku"), K(CK), O.add, mine(NS + p), O.is_gt)
-        value(1)
-        more(0)
-        for p in range(NV):
-            if p + 1 < NV:
-                more(p + 1)
-            else:
-                value(0)
-            a = 320 * (p % 3)
-            scan(R("scn", 160 * p, 160 * p + 160), R("fab", a, a + 160), R("fab", a + 160, a + 320), -160.0, O.add, O.add)
+        for p in range(NV + 2):
+            if p < NV:
+                ts(R("fab", 320 * p, 320 * p + 320), R("ku"), K(CP), O.add, mine(NS + p), O.is_gt)
+            if p == NV:
+                places(0, EARLY)
+            if p >= 2:
+                a = 320 * (p - 2)
+                scan(half("scn", p - 2), R("fab", a, a + 160), R("fab", a + 160, a + 320), -160.0, O.add, O.add)
+        if TAIL == 0:
+            lay(0, EARLY)
         ts(R("offs", NS, 20), R("scn", 159, 160 * NV, 160), 160.0, O.add)
-        ts(R("offs", 0, NS - 2), R("acc", 0, NS - 2), -0.5, O.mult, 159.5, O.add)
-        scatter(R("win"), R("offs", NS, 20), R("vrow", 16 * NS, 320))
-        ts(R("offs", NS - 2, NS), R("acc", NS - 2, NS), -0.5, O.mult, 159.5, O.add)
-        scatter(R("win"), R("offs", 0, NS), R("vrow", 0, 16 * NS))
-
-    def plane(n, b):
-        return R(n, 320 * b, 320 * b + 320)
+        if TAIL == 0:
+            places(EARLY, NS)
+            lay(EARLY, 20)
+        else:
+            lay(0, EARLY)
+            if TAIL == 1:
+                places(EARLY, NS)
+            lay(10, 20)
+            if TAIL == 2:
+                places(EARLY, NS)
+            lay(EARLY, 10)
+        strict.pop()
 
     def laid(r):
-        diagonal(R("dw", 0, 160), R("win", 0, 160), 160)
-        diagonal(R("dw", 160, 320), R("win", 160, 320), 160)
+        diagonal(half("dw", 0), half("win", 0))
         x = R("dw", 15, 160, 16)
         ts(R("ll", 0, 10), x, 2.0 ** -10, O.mult, K(CL), O.add)
-        copy(R("lx", 0, 10), x)
+        ts(R("lx", 0, 10), x, 1023, O.bitwise_and)
+        copy(R("bl", 0, 10), R("lx", 0, 10))
         for b in range(4):
-            act(R("pz", 160 * b, 160 * b + 160), pick(plane("fp", b), R("ll", 0, 10)), scale=0.5)
-        ts(R("kl", 0, 10), R("dw", 175, 320, 16), 2.0 ** -10, O.mult, K(CL), O.add)
-        ts(R("lx", 16, 26), R("lx", 0, 10), 1023, O.bitwise_and)
-        ts(R("bl", 0, 10), R("lx", 16, 26), -1.0, O.mult, 511.0, O.add)
-        for b in range(4):
-            tt(R("zt", b, 640, 4), pick(plane("f2", b), R("bl", 0, 10)), R("pz", 160 * b, 160 * b + 160), O.add)
-        z, l = "z%d" % r, "l%d" % r
+            act(half("pz", b), pick(plane("fp", b), R("ll", 0, 10)), scale=0.5)
+            tt(R("zt", b, 640, 4), pick(plane("f2", b, 336), R("bl", 0, 10)), half("pz", b), O.add)
+        z, l, arr = "z%d" % r, "l%d" % r, "arr%d" % r
         quant(z, 0, 160, "zt", 0)
-        rid, pid, _ = topo.addr(nxt)
-        m = topo.mask(core, nxt)
-        arr = "arr%d" % r
-        waits("G", accesses([R("q" + z), R("p" + z)], []))
-        g.remote_dma(T["q" + l][:, 0:160].bitcast(dt.uint8), T["q" + z][:, 0:160].bitcast(dt.uint8), T.sem[arr], T.sem["loc"], pid, rid, m)
-        g.remote_dma(T["p" + l][:, 0:160], T["p" + z][:, 0:160], T.sem[arr], T.sem["loc"], pid, rid, m)
-        k = 2 * len(topo.engines(core, nxt))
-        count["loc"] = count.get("loc", 0) + k
-        count[arr] = k
-        for n in ("q" + l, "p" + l):
-            hist[n] = [[R(n)[1][0][1], "w", arr, k]]
+
+        def send(e):
+            rid, pid, _ = topo.addr(nxt)
+            m = topo.mask(core, nxt)
+            e.remote_dma(T["q" + l][:, 0:160].bitcast(dt.uint8), T["q" + z][:, 0:160].bitcast(dt.uint8), T.sem[arr], T.sem["loc"], pid, rid, m)
+            e.remote_dma(T["p" + l][:, 0:160], T["p" + z][:, 0:160], T.sem[arr], T.sem["loc"], pid, rid, m)
+            k = 2 * len(topo.engines(core, nxt))
+            count["loc"] = count.get("loc", 0) + k
+            count[arr] = k
+            for n in ("q" + l, "p" + l):
+                hist[n] = [[R(n)[1][0][1], "w", arr, k]]
+        calls.append(("G", None, 0, send, accesses([R("q" + z), R("p" + z)], [R("q" + l), R("p" + l)]), 600, HOP))
 
     def kept(r):
+        diagonal(half("dw", 1), half("win", 1))
+        ts(R("kl", 0, 10), R("dw", 175, 320, 16), 2.0 ** -10, O.mult, K(CL), O.add)
         for b in range(4):
             (act if b % 2 else copy)(R("xk", b, 640, 4), pick(plane("fp", b), R("kl", 0, 10)))
         quant(str(r + 1), 0, 160, "xk", 0)
@@ -465,68 +526,45 @@ def rank_program(g, core, T, topo):
                 act(out, pb, scale=0.0078125)
         quant(str(r + 1), 160, 320, "xh", 0)
 
-    w = waiters()
-    run(w[0:2] + [lambda: ts(R("d1", 161, 162), ci(PD), -MISS, O.mult)] + w[2:4])
     quant("u", 0, 128, "uv", 0)
+    quant("v", 0, 128, "uv", 512)
     for e in range(2):
         quant("0", 160 * e, 160 * e + 160, "xt", 640 * e)
         mm(e, 160, "u", 0, "0", 160 * e)
-    run(ends(0) + [lambda: ts(R("cf", 2, 514, 4), R("tgf"), K(GF), O.is_equal, K(WT), O.mult)] + w[4:6] + w[8:10])
+        flags(e, 2 * e, 4)
     for r in range(3):
-        if r == 0:
-            for e in range(2):
-                flags(e, 2 * e, 4)
-            run(w[6:7] + w[10:11])
-        else:
-            mm(0, 160, "u", 0, str(r), 160)
-            flags(0, 320, 2)
-        quant("f", 0, 162, "fl", 0)
-        products(0)
-        more = {k: [] for k in "abcdefghij"}
-        dec = decode(r)
-        if r == 0:
-            for e in range(2):
-                quant("c", 128 * e, 128 * e + 128, "cf", 2 - 2 * e)
-            products(1)
-            u = units()
-            more.update(a=w[7:8] + w[11:12], b=u[0:2], c=u[2:3], d=u[3:4], e=u[4:6], f=u[6:8], g=u[8:9], h=u[9:11],
-                        i=[lambda: ts(K(CK), K(CP), -4096.0, O.add), lambda: ts(K(CL), K(CP), -(2.0 ** -10), O.mult)])
-            more["decode"] = ([], [])
-            more["g"] = more["g"] + dec[0:4]
-            more["j"] = dec[4:8]
-        else:
-            products(1)
-            more["decode"] = (dec[0:4], dec[4:8])
-        times(r, more)
+        symbols(r)
+        decode(r)
+        times(r)
         order(r)
         laid(r)
         kept(r)
         if r < 2:
             mm(0, 160, "u", 0, str(r + 1), 0)
-            if r == 0:
-                run(ends(1))
             flags(0, 0, 2)
-        else:
-            quant("v", 0, 128, "uv", 512)
-            mm(0, 160, "v", 0, "3", 0)
-            for h in range(8):
-                act(R("yo", 40 * h, 40 * h + 20), R("pb0", h, 160, 8))
-            scatter(R("oprow"), R("offs", 0, 20), R("ccol"))
-            for k in range(8):
-                dma("Y", T.op[k:k + 1, :], T.oprow[16 * k:16 * k + 1, :], [R("oprow")], [], "doy")
-            diagonal(R("df"), R("natr"), 320)
-            ts(R("nat", 0, 20), R("df", 15, 320, 16), K(CP), O.subtract)
-        arrive(r)
+            arrive(r)
+            mm(1, 160, "u", 0, str(r + 1), 160)
+            flags(1, 320, 2)
+    mm(0, 160, "v", 0, "3", 0)
+    for h in range(8):
+        act(R("yo", 40 * h, 40 * h + 20), R("pb0", h, 160, 8))
+    scatter(R("oprow"), R("offs", 0, 20), R("ccol"))
+    for k in range(8):
+        dma("Y", T.op[k:k + 1, :], T.oprow[16 * k:16 * k + 1, :], [R("oprow")], [], "doy")
+    diagonal(R("df"), R("natr"))
+    ts(R("nat", 0, 20), R("df", 15, 320, 16), K(CP), O.subtract)
+    arrive(2)
     for e in range(2):
-        mm(e, 160, "v", 0, "3", 160)
+        mm(6 + e, 160, "v", 0, "3", 160)
     act(R("pn"), pick(R("p3"), R("nat", 0, 20)))
     copy(words(R("qn")), pick(words(R("q3")), R("nat", 0, 20)))
     dma("Y", T.oc[:], T.qn[:].bitcast(dt.uint8), [R("qn")], [], "doy")
     for h in range(8):
-        (act if h % 2 else copy)(R("yo", 40 * h + 20, 40 * h + 40), R("pb%d" % (h % 2), h, 160, 8))
+        (act if h % 2 else copy)(R("yo", 40 * h + 20, 40 * h + 40), R("pb%d" % (6 + h % 2), h, 160, 8))
     for k in range(4):
         dma("Y", T.osc[4 * k:4 * k + 4, :], T.pn[32 * k:32 * k + 4, :], [R("pn")], [], "doy")
     dma("S", T.y[:], T.yo[:], [R("yo")], [], "doa")
+    issue()
     for s in sorted(count):
         if known["G"].get(s, 0) < count[s]:
             g.wait_ge(T.sem[s], count[s])

@@ -3,20 +3,20 @@ from concourse.mybir import dt, AluOpType as O, ActivationFunctionType as AF
 NS = 9
 NV = 20 - NS
 EARLY = 6
-TAIL = 0
 TOP = 1023.0
 MISS = float(2 ** 22)
-KEEP = float(2 ** 19)
+KEEP = float(2 ** 14)
 LOW = -1.0e9
 F4 = "float8_e4m3fn_x4"
 BLOCKS = (0, 1, 2, 3, 0, 0, 1, 1)
 WINDOW = (64, 128, 0)
-LISTS = {"off1": 0, "off2": 16, "ll": 32, "bl": 48, "kl": 64, "offd": 80, "offs": 112, "nat": 144, "first": 176}
-ROWS = ["dg", "hr0", "hr1", "si0", "si1", "ccol", "natr"]
+LISTS = {"off1": 0, "off2": 16, "kl": 32, "offd": 48, "offs": 80, "nat": 112, "own": 144}
+SENT = {"ll": 0, "first": 16, "mate": 32}
+ROWS = ["hr0", "hr1", "si0", "si1", "ccol", "natr"]
 WIDTH = {"bfloat16": 2, "uint16": 2}
 PIECES = ((0, 6), (6, 10), (10, 16), (16, 20))
-TURNS = 3
-WAKE, LOAD, HOP, SLACK = 200, 2400, 2500, 30
+TURNS = 1
+WAKE, LOAD, HOP, HOPE, HOPL, SLACK = 200, 2400, 3000, 3500, 2000, 30
 
 
 def _decl():
@@ -25,48 +25,46 @@ def _decl():
     def sb(names, n, t):
         for k in names.split():
             d[k] = ("sbuf", [128, n], t)
-    sb("xt fp", 1280, "bfloat16")
+    sb("xt fp gp za", 1280, "bfloat16")
     sb("f2", 1344, "bfloat16")
-    sb("xk xh zt pz sj", 640, "bfloat16")
+    sb("xk xh zt sj", 640, "bfloat16")
     sb("uv cs cd", 1024, "bfloat16")
     sb("cf eg eh zz", 520, "bfloat16")
     sb("fa fb", 776, "bfloat16")
     sb("fab", 320 * 12, "bfloat16")
     sb("scn", 160 * 12, "bfloat16")
     sb("w4 sg4 tgf ixg ixh", 128, "bfloat16")
-    sb("jm jn", 320, "bfloat16")
-    for k, n in (("u", 128), ("v", 128), ("w", 512), ("h", 512), ("g", 512), ("s", 256), ("d", 256), ("c", 256), ("a", 194), ("b", 194), ("n", 320)):
+    sb("dg dow", 320, "bfloat16")
+    for k, n in (("u", 128), ("v", 128), ("w", 512), ("h", 512), ("g", 512), ("s", 256), ("d", 256), ("c", 256), ("a", 194), ("b", 194), ("n", 320), ("z", 160)):
         d["q" + k] = ("sbuf", [128, n], F4)
         d["p" + k] = ("sbuf", [128, n], "uint8")
     for r in range(4):
         d["q%d" % r] = ("sbuf", [128, 320], F4)
         d["p%d" % r] = ("sbuf", [128, 320], "uint8")
     for r in range(3):
-        for k in ("z", "l"):
-            d["q%s%d" % (k, r)] = ("sbuf", [128, 160], F4)
-            d["p%s%d" % (k, r)] = ("sbuf", [128, 160], "uint8")
+        d["ql%d" % r] = ("sbuf", [128, 320], F4)
+        d["pl%d" % r] = ("sbuf", [128, 320], "uint8")
+    sb("out came", 192, "uint16")
     sb("rows", 320 * len(ROWS), "float32")
-    sb("d0o dow row2 vrow yo oprow kas my win df", 320, "float32")
-    sb("dw", 320, "int32")
+    sb("d0o yo oprow kas my win", 320, "float32")
+    sb("ku dw df mate dp", 320, "uint16")
     sb("n0 n1 n2 n3 d1 d2 cr0 cr1 mx my2", 200, "float32")
     sb("d0 inc1 inc2 dl dm", 160, "float32")
     sb("one", 40, "float32")
     sb("acc", 20, "float32")
-    sb("tb ta", 32, "float32")
+    sb("tb ta e16", 32, "float32")
     sb("k", 56, "float32")
-    sb("wt mt at am an ao v16", 16, "float32")
-    sb("mi w8", 16, "int32")
+    sb("wt at am ao v16 j16 d16", 16, "float32")
+    sb("mi w8 lx", 16, "int32")
     sb("ci", 48, "int32")
-    sb("lx", 48, "int32")
-    sb("lists", 192, "uint16")
-    sb("ku", 320, "uint16")
+    sb("lists", 176, "uint16")
     for b in range(8):
         d["pb%d" % b] = ("psum", [128, 512], "float32")
     return d
 
 
 SCRATCH = _decl()
-SEMAPHORES = ["sV", "sS", "sP", "sG", "dx0", "dx1", "du", "dw", "dws", "dv", "arr0", "arr1", "arr2", "loc", "doy", "doa"]
+SEMAPHORES = ["sV", "sS", "sP", "sG", "dx0", "dx1", "du", "dw", "dws", "dv", "loc", "doy", "doa"] + [k % r for r in range(3) for k in ("ax%d0", "ax%d1", "af%d", "al%d", "ab%d")]
 
 
 def rank_program(g, core, T, topo):
@@ -77,6 +75,7 @@ def rank_program(g, core, T, topo):
     queue = {"V": g.vector, "S": g.scalar, "P": g.tensor, "G": g, "Y": g.sync}
     own = {"V": "sV", "S": "sS", "P": "sP", "G": "sG"}
     calls = []
+    strict = []
     count = {}
     clock = {}
     known = {k: {} for k in queue}
@@ -99,8 +98,8 @@ def rank_program(g, core, T, topo):
     def pick(win, off):
         return (win[0].indirect(off[0]), win[1] + off[1], 16 * off[2], 0)
 
-    def words(v):
-        return (v[0].bitcast(dt.uint32),) + v[1:]
+    def cast(v, t):
+        return (v[0].bitcast(t),) + v[1:]
 
     def accesses(reads, writes):
         r = [a for v in reads if isinstance(v, tuple) for a in v[1]]
@@ -138,13 +137,23 @@ def rank_program(g, core, T, topo):
                 h[:] = [e for e in h if e[0] & ~m]
             h.append([m, kind, sem, v])
 
-    strict = []
-
     def op(q, call, reads, writes, time):
-        calls.append((q, own[q], 1, call, accesses(reads, writes) + [(("turn", 1), "w")] * (q in strict), time, WAKE))
+        calls.append((q, own[q], 1, call, accesses(reads, writes) + [(("turn", 1 + (q == "S")), "w")] * (q in strict), time, WAKE))
 
     def dma(q, out, in_, reads, writes, sem):
         calls.append((q, sem, 16, lambda e: e.dma_start(out, in_), accesses(reads, writes), 60, LOAD))
+
+    def send(sem, pairs, hop):
+        def call(e):
+            rid, pid, _ = topo.addr(nxt)
+            for out, in_ in pairs:
+                e.remote_dma(out[0], in_[0], T.sem[sem], T.sem["loc"], pid, rid, topo.mask(core, nxt))
+            k = len(pairs) * len(topo.engines(core, nxt))
+            count["loc"] = count.get("loc", 0) + k
+            count[sem] = k
+            for out, in_ in pairs:
+                hist.setdefault(out[1][0][0], []).append([out[1][0][1], "w", sem, k])
+        calls.append(("G", None, 0, call, accesses([p[1] for p in pairs], [p[0] for p in pairs]), 300 * len(pairs), hop))
 
     def issue():
         last, before = {}, []
@@ -174,12 +183,14 @@ def rank_program(g, core, T, topo):
             for i in sorted(range(len(calls)), key=lambda i: -urge[i]):
                 q, time = calls[i][0], calls[i][5]
                 t = max([start[j] + d for j, d in links[i].items()] + [first[i]])
-                for a, b in sorted(busy[q]):
+                at = 0
+                for a, b in busy[q]:
                     if t < a and t + time <= a + SLACK:
                         break
                     t = max(t, b)
+                    at += 1
                 start[i] = t
-                busy[q].append((t, t + time))
+                busy[q].insert(at, (t, t + time))
             return start, [start[i] + c[5] for i, c in enumerate(calls)]
         start, end = place(chain, before, [0] * len(calls))
         for _ in range(TURNS):
@@ -234,6 +245,9 @@ def rank_program(g, core, T, topo):
         op("S", lambda s: s.activation(out[0], a[0], f, **more), [a] + list(kw.values()), [out] + ([acc] if acc else []),
            (cycles(out[2]) if a[3] else 65 + 1.3 * out[2]) + (20 if acc else 0))
 
+    def affine(out, a, scale, bias):
+        act(out, a, AF.Identity, scale=scale, bias=bias)
+
     def iota(out, pat, base=0, cm=0):
         more = {} if SCRATCH[out[1][0][0]][2] == "int32" else {"allow_small_or_imprecise_dtypes": True}
         op("G", lambda e: e.iota(out[0], pat, base, cm, **more), [], [out], 130 + 1.66 * out[2])
@@ -256,6 +270,10 @@ def rank_program(g, core, T, topo):
     def half(n, e):
         return R(n, 160 * e, 160 * e + 160)
 
+    def plane(n, b, w=320):
+        a = b * (SCRATCH[n][1][1] // 4)
+        return R(n, a, a + w)
+
     for e in range(2):
         dma("Y", T.xt[:, 640 * e:640 * e + 640], T.x[:, 640 * e:640 * e + 640], [], [R("xt", 640 * e, 640 * e + 640)], "dx%d" % e)
     dma("S", T.uv[:, 0:512], T.u[:], [], [R("uv", 0, 512)], "du")
@@ -268,15 +286,16 @@ def rank_program(g, core, T, topo):
 
     def K(i, n=1):
         return R("k", i, i + n)
-    RK, SG, S1, S2, HF, BK, GR, PC, PD = range(1, 10)
-    RF, GF, PF, LT3, WA, WT, RA, RW, CP, I0, CK, CL = range(12)
+    RK, SG, S1, S2, HF, BK, GR, PC, PD, P1, R1 = range(1, 12)
+    RF, GF, PF, LT3, WA, WT, RA, RW, CP, I0, CK, NF = range(12)
     WM, MK, LA, LB, G4, WH, WI, C8 = 16, 20, 24, 28, 32, 36, 40, 48
     iota(ci(0), [[1, 1]], 0, 1)
+    iota(ci(P1), [[1, 1]], 1, 1)
     iota(K(G4, 4), [[1, 4]])
     iota(K(C8, 8), [[1, 8]], 320)
     iota(R("v16"), [[0, 2], [1, 8]])
+    iota(R("j16"), [[1, 16]])
     level("one", 0, 40, -1)
-    iota(R("jm"), [[0, 20], [1, 16]])
     iota(R("tgf"), [[1, 8], [0, 16]])
     for i, low in enumerate((-TOP, -TOP, -1, -1)):
         level("n%d" % i, 160, 193, low)
@@ -286,7 +305,6 @@ def rank_program(g, core, T, topo):
     level("cr0", 1, 160, 1)
     level("cr0", 40, 160, 513, 40)
     level("n3", 0, 160, 0)
-    level("mt", 8, 16, 1025)
     level("at", 8, 16, 0)
     iota(R("ixg"), [[1, 128]])
     iota(R("ixh"), [[16, 4], [0, 2], [1, 16]])
@@ -298,20 +316,21 @@ def rank_program(g, core, T, topo):
     level("cr1", 4, 160, -3070, 4)
     iota(R("si1"), [[1, 2], [2, 160]])
     iota(R("hr1"), [[-1, 2], [0, 40], [-2, 4]], 4103)
-    iota(R("ccol"), [[40, 2], [1, 40], [80, 4]])
+    iota(R("ccol"), [[1, 40], [40, 8]])
     iota(R("natr"), [[1, 8], [8, 40]])
 
     fill(R("zz"), 0.0)
     fill(R("w4"), 0.0)
     fill(R("sg4"), 0.0)
-    for n in ("fa", "fb"):
-        act(R(n, 0, 520), R("zz"))
-        act(R(n, 520, 776), R("zz", 0, 256))
+    for n, a, b in (("fa", 1, 776), ("fa", 640, 776), ("fb", 0, 776), ("fb", 1, 4), ("fb", 645, 776)):
+        out = R(n, a, b, 2)
+        act(out, R("zz", 0, out[2]))
     for n in ("cf", "eg", "eh"):
         act(R(n), R("zz"))
     fill(R("w4", 0, 64, 4), 1.0)
     fill(R("w4", 66, 128, 4), 1.0)
     ts(ci(RK), ci(0), 15, O.bitwise_and)
+    ts(ci(R1), ci(P1), 15, O.bitwise_and)
     ts(ci(GR), ci(0), 4, O.arith_shift_right)
     ts(ci(SG), ci(0), 7, O.bitwise_and)
     ts(ci(S1), ci(0), 7, O.bitwise_and, 1, O.arith_shift_right)
@@ -320,9 +339,10 @@ def rank_program(g, core, T, topo):
     ts(ci(BK), ci(0), 5, O.arith_shift_right)
     tt(ci(PC), ci(SG), ci(S1), O.subtract)
     tt(ci(PD), ci(PC), ci(S2), O.subtract)
-    copy(K(RF), ci(RK))
     copy(K(GF), ci(GR))
-    copy(K(PF), ci(0))
+    act(K(RF), ci(RK))
+    act(K(NF), ci(R1))
+    act(K(PF), ci(0))
     ts(K(WA), ci(RK), -2.0, O.mult, 4.0, O.add)
     ts(K(LT3), ci(RK), 3.0, O.is_lt)
     ts(K(RA), ci(RK), 0.25, O.mult, 0.25, O.add)
@@ -333,7 +353,7 @@ def rank_program(g, core, T, topo):
     ts(R("ci", 16, 32), R("v16"), K(RW), O.mult, -0.375, O.add)
     ts(R("ci", 32, 48), R("ci", 16, 32), 1, O.bitwise_and)
     for at, sign in ((0, 1.0), (1, -1.0), (66, 1.0), (67, -1.0)):
-        ts(R("sg4", at, at + 61, 4), R("ci", 32, 48), -2.0 * MISS * sign, O.mult, MISS * sign, O.add)
+        affine(R("sg4", at, at + 61, 4), R("ci", 32, 48), -2.0 * MISS * sign, MISS * sign)
     for i, b in enumerate(BLOCKS):
         act(R("cs", 128 * i, 128 * i + 128), R("w4"), AF.Identity, scale=K(WM + b))
         ts(R("cd", 128 * i, 128 * i + 128), R("sg4"), K(MK + b), O.mult)
@@ -343,22 +363,24 @@ def rank_program(g, core, T, topo):
     for e in range(2):
         quant("c", 128 * e, 128 * e + 128, "cf", 2 - 2 * e)
     ts(K(I0), ci(PD), -MISS, O.mult, TOP, O.add)
-    ts(R("d1", 161, 162), ci(PD), -MISS, O.mult)
-    ts(K(CP), ci(RK), -KEEP, O.mult, 15.0 * KEEP, O.add)
-    act(K(CK), K(CP), AF.Identity, bias=511.0)
-    act(K(CL), K(CP), AF.Identity, scale=-(2.0 ** -10))
-    ts(R("jn"), R("jm"), K(RF), O.is_gt, 33.0, O.mult)
-    act(R("dg"), R("jn"), AF.Identity, scale=KEEP, bias=-32.0 * KEEP)
-    for i, (src, least, unit, one) in enumerate(((BK, 2.0, 1.0, 0.0), (BK, 1.0, 2.0 ** -12, 1.0), (GR, 1.0, 0.125, 1.0))):
+    affine(R("d1", 161, 162), ci(PD), -MISS, 0.0)
+    ts(K(CP), ci(RK), 15.0, O.is_lt, KEEP, O.mult)
+    affine(K(CK), K(CP), 1.0, 511.0)
+    ts(R("e16", 0, 16), R("j16"), K(RF), O.is_equal, -4.0 * KEEP, O.mult)
+    ts(R("e16", 16, 32), R("j16"), K(NF), O.is_equal, KEEP, O.mult)
+    tt(R("d16"), R("e16", 0, 16), R("e16", 16, 32), O.add)
+    affine(R("own", 0, 20), R("one", 0, 20), 0.0, K(RF))
+    act(R("dg"), pick(R("d16"), R("own", 0, 20)))
+    for i, (src, least, unit, one) in enumerate(((BK, 2.0, 1.0, 0.0), (BK, 1.0, 1.0, 0.0), (GR, 1.0, 0.125, 1.0))):
         ts(K(LA + i), ci(src), least, O.is_ge, unit, O.mult)
         ts(K(WH + i), ci(src), least, O.is_lt, 8.0 + one, O.mult)
-        act(K(WI + i), K(LA + i), AF.Identity, scale=K(CP), bias=one)
-        act(K(LB + i), K(WI + i), AF.Identity, scale=-1.0, bias=K(WH + i))
+        affine(K(WI + i), K(LA + i), K(CP), one)
+        affine(K(LB + i), K(WI + i), -1.0, K(WH + i))
     for r, (e, end) in enumerate(((2208.0, 4095.0 - 552 * 3 - 39), (513.0, 4095.0 - 8 * 39 - 1026 * 3))):
         n = "cr%d" % r
-        ts(R(n, 0, 1), ci(HF), e, O.mult, -4095.0, O.add)
-        ts(R(n, 160, 161), ci(HF), -e, O.mult, end, O.add)
-        ts(R(n, 161, 162), ci(PD), -MISS, O.mult)
+        affine(R(n, 0, 1), ci(HF), e, -4095.0)
+        affine(R(n, 160, 161), ci(HF), -e, end)
+        affine(R(n, 161, 162), ci(PD), -MISS, 0.0)
     ts(R("eg", 3, 515, 4), R("ixg"), K(PF), O.is_equal, 128.0, O.mult)
     ts(R("eh", 3, 515, 4), R("ixh"), K(PF), O.is_equal)
     for k in "gh":
@@ -375,6 +397,13 @@ def rank_program(g, core, T, topo):
     def listed(off, n, row, i):
         ts(R(off, 0, n), R(row, 15, 16 * n, 16), K(LA + i), O.mult, K(LB + i), O.add)
 
+    def state(r, e):
+        send("ax%d%d" % (r, e), [(cast(half("ql%d" % r, e), dt.uint8), cast(half("q%d" % r, e), dt.uint8)), (half("pl%d" % r, e), half("p%d" % r, e))], HOP)
+
+    def sent(r, name, n):
+        at = 64 * r + SENT[name]
+        return R("out", at, at + n), R("came", at, at + n)
+
     def symbols(r):
         c = min(r, 1)
         quant("a", 0, 160 if r else 194, "fa", 0)
@@ -385,36 +414,41 @@ def rank_program(g, core, T, topo):
             mm(2 * st + 1, 162 if st else 194, "d", WINDOW[st], "b", 0, False, True)
         for e in range(2):
             mm(6 + e, 160, "c", 128 * e, "a", 0)
-            act(half("dow", e), R("pb%d" % (6 + e), 0, 160), AF.Identity, scale=8.0, bias=8.0)
+            affine(half("dow", e), R("pb%d" % (6 + e), 0, 160), 8.0, 8.0)
             diagonal(half("df", e), half("dow", e))
         listed("offd", 20, "df", 2)
         diagonal(R("dl"), R("pb2", 0, 160))
         listed("off1", 10, "dl", 0)
-        act(R("inc1"), R("pb2", 0, 160), AF.Identity, bias=1.0)
+        affine(R("inc1"), R("pb2", 0, 160), 1.0, 1.0)
         act(R("d1", 0, 161), R("pb3", 0, 161))
-        act(R("inc2"), R("pb4", 0, 160), AF.Identity, scale=4096.0, bias=4096.0)
-        diagonal(R("dm"), R("inc2"))
+        diagonal(R("dm"), R("pb4", 0, 160))
         listed("off2", 10, "dm", 1)
+        affine(R("inc2"), R("pb4", 0, 160), 4096.0, 4096.0)
         tt(R("d2", 0, 162), R("pb5", 0, 162), R("cr%d" % c, 0, 162), O.add)
         scan(R("my2", 0, 193), R("d2", 0, 193), R("n3", 0, 193), LOW, O.add, O.max)
         turn(R("ta"), R("my2", 161, 193))
         tt(R("am", 0, 8), R("ta", 0, 8), R("ta", 16, 24), O.max)
-        ts(R("mt", 0, 8), R("am", 0, 8), 0.0, O.is_lt, 1024.0, O.add)
         ts(R("am", 8, 16), R("am", 0, 8), 0.0, O.is_ge)
         tt(R("at", 0, 8), R("am", 8, 16), K(C8, 8), O.mult)
         for a, b in PIECES:
-            tt(R("row2", 16 * a, 16 * b), pick(R("mt"), R("offd", a, b)), R("si%d" % c, 16 * a, 16 * b), O.mult)
-            tt(R("vrow", 16 * a, 16 * b), pick(R("at"), R("offd", a, b)), R("row2", 16 * a, 16 * b), O.add)
-
-    def plane(n, b, w=320):
-        a = b * (SCRATCH[n][1][1] // 4)
-        return R(n, a, a + w)
+            e = a // 10
+            out = R("mate", 32 * a - 319 * e, 32 * b - 319 * e - 1, 2) if r else R("mate", 16 * a, 16 * b)
+            tt(out, pick(R("at"), R("offd", a, b)), R("si%d" % c, 16 * a, 16 * b), O.max)
+        diagonal(R("dp"), R("mate"))
+        out, came = sent(r, "mate", 20)
+        ts(out, R("dp", 15, 320, 16), K(CP), O.subtract)
+        send("ab%d" % r, [(came, out)], HOPE)
 
     def decode(r):
-        for i in range(8):
-            k, dst, b, sc = ("g", "fp", i - 4, 0.0078125) if i >= 4 else ("h", "f2", i, 0.5)
-            mm(2 + i % 2, 320, k, 128 * b, str(r), 0)
-            act(plane(dst, b), R("pb%d" % (2 + i % 2), 0, 320), scale=sc)
+        for e in range(2):
+            for i in range(8):
+                k, dst, b, sc = ("g", "gp", i - 4, 2.0 ** -8) if i >= 4 else ("h", "f2", i, 0.5)
+                bank, at = 2 + 2 * e + i % 2, b * (SCRATCH[dst][1][1] // 4) + 160 * e
+                mm(bank, 160, k, 128 * b, "l%d" % r, 160 * e)
+                act(R(dst, at, at + 160), R("pb%d" % bank, 0, 160), scale=sc)
+        for b in range(4):
+            mm(6 + b % 2, 320, "g", 128 * b, str(r), 0)
+            act(plane("fp", b), R("pb%d" % (6 + b % 2), 0, 320), scale=0.0078125)
 
     def times(r):
         for st in range(3):
@@ -431,11 +465,13 @@ def rank_program(g, core, T, topo):
             w = 16 if st == 2 else 8
             tt(R("mi" if st == 2 else "wt", 0, w), R("tb", 0, w), R("tb", 16, 16 + w), O.max)
         ts(R("w8", 0, 8), R("mi", 0, 8), 9, O.arith_shift_right, 0x1FF8, O.bitwise_and)
-        ts(R("lx", 32, 48), R("mi"), 511, O.bitwise_and)
-        diagonal(R("ao"), R("lx", 32, 48))
-        ts(R("first", 0, 1), R("ao", 15, 16), -1.0, O.mult, K(CK), O.add)
+        ts(R("lx"), R("mi"), 511, O.bitwise_and)
+        diagonal(R("ao"), R("lx"))
+        out, came = sent(r, "first", 1)
+        ts(out, R("ao", 15, 16), -1.0, O.mult, K(CK), O.add)
+        send("af%d" % r, [(came, out)], HOPE)
         for b in range(4):
-            act(R("f2", 336 * b + 320, 336 * b + 336), pick(plane("f2", b), R("first", 0, 1)))
+            act(R("f2", 336 * b + 320, 336 * b + 336), pick(plane("f2", b), came))
 
     def order(r):
         c = min(r, 1)
@@ -445,7 +481,7 @@ def rank_program(g, core, T, topo):
         for e in range(2):
             for h in range(4):
                 scan(stack("ku", r, h, 160 * e), stack("d0o", r, h, 160 * e), stack("dow", r, h, 160 * e), -LOW, O.min, O.subtract)
-            act(half("kas", e), half("ku", e), AF.Identity, bias=K(CP))
+            affine(half("kas", e), half("ku", e), 1.0, K(CP))
         for e in range(2):
             diagonal(half("my", e), half("ku", e))
 
@@ -456,7 +492,7 @@ def rank_program(g, core, T, topo):
             ts(R("offs", a, b), R("acc", a, b), -0.5, O.mult, 159.5, O.add)
 
         def lay(a, b):
-            scatter(R("win"), R("offs", a, b), R("vrow", 16 * a, 16 * b))
+            scatter(R("win"), R("offs", a, b), R("si%d" % c, 16 * a, 16 * b))
         for q in range(NS):
             act(R("sj", 320 * (q % 2), 320 * (q % 2) + 320), R("kas"), AF.Sign, acc=R("acc", q, q + 1), scale=-1.0, bias=mine(q))
         for p in range(NV + 2):
@@ -467,57 +503,33 @@ def rank_program(g, core, T, topo):
             if p >= 2:
                 a = 320 * (p - 2)
                 scan(half("scn", p - 2), R("fab", a, a + 160), R("fab", a + 160, a + 320), -160.0, O.add, O.add)
-        if TAIL == 0:
-            lay(0, EARLY)
+        lay(0, EARLY)
         ts(R("offs", NS, 20), R("scn", 159, 160 * NV, 160), 160.0, O.add)
-        if TAIL == 0:
-            places(EARLY, NS)
-            lay(EARLY, 20)
-        else:
-            lay(0, EARLY)
-            if TAIL == 1:
-                places(EARLY, NS)
-            lay(10, 20)
-            if TAIL == 2:
-                places(EARLY, NS)
-            lay(EARLY, 10)
+        places(EARLY, NS)
+        lay(EARLY, 20)
         strict.pop()
 
-    def laid(r):
-        diagonal(half("dw", 0), half("win", 0))
-        x = R("dw", 15, 160, 16)
-        ts(R("ll", 0, 10), x, 2.0 ** -10, O.mult, K(CL), O.add)
-        ts(R("lx", 0, 10), x, 1023, O.bitwise_and)
-        copy(R("bl", 0, 10), R("lx", 0, 10))
+    def deal(r):
+        strict.extend("VS")
+        for e in range(2):
+            diagonal(half("dw", e), half("win", e))
+        ll, came = sent(r, "ll", 10)
+        ts(ll, R("dw", 15, 160, 16), K(CP), O.subtract)
+        send("al%d" % r, [(came, ll)], HOPL)
+        ts(R("kl", 0, 10), R("dw", 175, 320, 16), K(CP), O.subtract)
         for b in range(4):
-            act(half("pz", b), pick(plane("fp", b), R("ll", 0, 10)), scale=0.5)
-            tt(R("zt", b, 640, 4), pick(plane("f2", b, 336), R("bl", 0, 10)), half("pz", b), O.add)
-        z, l, arr = "z%d" % r, "l%d" % r, "arr%d" % r
-        quant(z, 0, 160, "zt", 0)
-
-        def send(e):
-            rid, pid, _ = topo.addr(nxt)
-            m = topo.mask(core, nxt)
-            e.remote_dma(T["q" + l][:, 0:160].bitcast(dt.uint8), T["q" + z][:, 0:160].bitcast(dt.uint8), T.sem[arr], T.sem["loc"], pid, rid, m)
-            e.remote_dma(T["p" + l][:, 0:160], T["p" + z][:, 0:160], T.sem[arr], T.sem["loc"], pid, rid, m)
-            k = 2 * len(topo.engines(core, nxt))
-            count["loc"] = count.get("loc", 0) + k
-            count[arr] = k
-            for n in ("q" + l, "p" + l):
-                hist[n] = [[R(n)[1][0][1], "w", arr, k]]
-        calls.append(("G", None, 0, send, accesses([R("q" + z), R("p" + z)], [R("q" + l), R("p" + l)]), 600, HOP))
-
-    def kept(r):
-        diagonal(half("dw", 1), half("win", 1))
-        ts(R("kl", 0, 10), R("dw", 175, 320, 16), 2.0 ** -10, O.mult, K(CL), O.add)
+            tt(plane("za", b), pick(plane("f2", b, 336), sent(r, "mate", 20)[1]), plane("gp", b), O.add)
+            act(R("xk", b, 640, 4), pick(plane("fp", b), R("kl", 0, 10)))
         for b in range(4):
-            (act if b % 2 else copy)(R("xk", b, 640, 4), pick(plane("fp", b), R("kl", 0, 10)))
+            (copy if b // 2 else act)(R("zt", b, 640, 4), pick(plane("za", b), came))
         quant(str(r + 1), 0, 160, "xk", 0)
+        quant("z", 0, 160, "zt", 0)
+        del strict[:]
 
     def arrive(r):
         for b in range(4):
-            mm(2 + b, 160, "w", 128 * b, "l%d" % r, 0, True, False)
-            mm(2 + b, 160, "g", 128 * b, "l%d" % r, 0, False, True)
+            mm(2 + b, 160, "w", 128 * b, "z", 0, True, False)
+            mm(2 + b, 160, "g", 128 * b, "z", 0, False, True)
         for b in range(4):
             out, pb = R("xh", b, 640, 4), R("pb%d" % (2 + b), 0, 160)
             if b % 2:
@@ -532,23 +544,26 @@ def rank_program(g, core, T, topo):
         quant("0", 160 * e, 160 * e + 160, "xt", 640 * e)
         mm(e, 160, "u", 0, "0", 160 * e)
         flags(e, 2 * e, 4)
+        state(0, e)
     for r in range(3):
         symbols(r)
         decode(r)
         times(r)
         order(r)
-        laid(r)
-        kept(r)
+        deal(r)
         if r < 2:
+            state(r + 1, 0)
             mm(0, 160, "u", 0, str(r + 1), 0)
             flags(0, 0, 2)
             arrive(r)
+            state(r + 1, 1)
             mm(1, 160, "u", 0, str(r + 1), 160)
             flags(1, 320, 2)
     mm(0, 160, "v", 0, "3", 0)
     for h in range(8):
         act(R("yo", 40 * h, 40 * h + 20), R("pb0", h, 160, 8))
-    scatter(R("oprow"), R("offs", 0, 20), R("ccol"))
+    for e, at in enumerate((sent(2, "ll", 10)[0], R("kl", 0, 10))):
+        act(half("oprow", e), pick(R("ccol"), at))
     for k in range(8):
         dma("Y", T.op[k:k + 1, :], T.oprow[16 * k:16 * k + 1, :], [R("oprow")], [], "doy")
     diagonal(R("df"), R("natr"))
@@ -557,7 +572,7 @@ def rank_program(g, core, T, topo):
     for e in range(2):
         mm(6 + e, 160, "v", 0, "3", 160)
     act(R("pn"), pick(R("p3"), R("nat", 0, 20)))
-    copy(words(R("qn")), pick(words(R("q3")), R("nat", 0, 20)))
+    copy(cast(R("qn"), dt.uint32), pick(cast(R("q3"), dt.uint32), R("nat", 0, 20)))
     dma("Y", T.oc[:], T.qn[:].bitcast(dt.uint8), [R("qn")], [], "doy")
     for h in range(8):
         (act if h % 2 else copy)(R("yo", 40 * h + 20, 40 * h + 40), R("pb%d" % (6 + h % 2), h, 160, 8))

@@ -1,8 +1,9 @@
 from concourse.mybir import dt, AluOpType as O, ActivationFunctionType as AF
 
-NS = 9
+NS = 8
 NV = 20 - NS
-EARLY = 6
+EARLY = 4
+AT = (9, 11, 13)
 TOP = 1023.0
 MISS = float(2 ** 22)
 KEEP = float(2 ** 14)
@@ -10,13 +11,13 @@ LOW = -1.0e9
 F4 = "float8_e4m3fn_x4"
 BLOCKS = (0, 1, 2, 3, 0, 0, 1, 1)
 WINDOW = (64, 128, 0)
-LISTS = {"off1": 0, "off2": 16, "kl": 32, "offd": 48, "offs": 80, "nat": 112, "own": 144}
+LISTS = {"off1": 0, "off2": 16, "kl": 32, "offd": 48, "offs": 80, "nat": 112, "own": 144, "keep": 168}
 SENT = {"ll": 0, "first": 16, "mate": 32}
 ROWS = ["hr0", "hr1", "si0", "si1", "ccol", "natr"]
 WIDTH = {"bfloat16": 2, "uint16": 2}
 PIECES = ((0, 6), (6, 10), (10, 16), (16, 20))
 TURNS = 1
-WAKE, LOAD, HOP, HOPE, HOPL, SLACK = 200, 2400, 3000, 3500, 2000, 30
+WAKE, LOAD, HOP, HOPE, HOPL, SLACK = 220, 2400, 3000, 3500, 2000, 30
 
 
 def _decl():
@@ -32,7 +33,6 @@ def _decl():
     sb("cf eg eh zz", 520, "bfloat16")
     sb("fa fb", 776, "bfloat16")
     sb("fab", 320 * 12, "bfloat16")
-    sb("scn", 160 * 12, "bfloat16")
     sb("w4 sg4 tgf ixg ixh", 128, "bfloat16")
     sb("dg dow", 320, "bfloat16")
     for k, n in (("u", 128), ("v", 128), ("w", 512), ("h", 512), ("g", 512), ("s", 256), ("d", 256), ("c", 256), ("a", 194), ("b", 194), ("n", 320), ("z", 160)):
@@ -46,8 +46,9 @@ def _decl():
         d["pl%d" % r] = ("sbuf", [128, 320], "uint8")
     sb("out came", 192, "uint16")
     sb("rows", 320 * len(ROWS), "float32")
-    sb("d0o yo oprow kas my win", 320, "float32")
-    sb("ku dw df mate dp", 320, "uint16")
+    sb("d0o yo oprow kas win", 320, "float32")
+    sb("ku dw df mate dp dn my", 320, "uint16")
+    sb("scn", 3200, "uint16")
     sb("n0 n1 n2 n3 d1 d2 cr0 cr1 mx my2", 200, "float32")
     sb("d0 inc1 inc2 dl dm", 160, "float32")
     sb("one", 40, "float32")
@@ -366,6 +367,7 @@ def rank_program(g, core, T, topo):
     affine(R("d1", 161, 162), ci(PD), -MISS, 0.0)
     ts(K(CP), ci(RK), 15.0, O.is_lt, KEEP, O.mult)
     affine(K(CK), K(CP), 1.0, 511.0)
+    act(R("keep", 0, 1), K(CP))
     ts(R("e16", 0, 16), R("j16"), K(RF), O.is_equal, -4.0 * KEEP, O.mult)
     ts(R("e16", 16, 32), R("j16"), K(NF), O.is_equal, KEEP, O.mult)
     tt(R("d16"), R("e16", 0, 16), R("e16", 16, 32), O.add)
@@ -383,6 +385,9 @@ def rank_program(g, core, T, topo):
         affine(R(n, 161, 162), ci(PD), -MISS, 0.0)
     ts(R("eg", 3, 515, 4), R("ixg"), K(PF), O.is_equal, 128.0, O.mult)
     ts(R("eh", 3, 515, 4), R("ixh"), K(PF), O.is_equal)
+    for e in range(2):
+        diagonal(half("dn", e), half("natr", e))
+    ts(R("nat", 0, 20), R("dn", 15, 320, 16), K(CP), O.subtract)
     for k in "gh":
         for b in range(4):
             quant(k, 128 * b, 128 * b + 128, "e" + k, 3 - b)
@@ -446,9 +451,6 @@ def rank_program(g, core, T, topo):
                 bank, at = 2 + 2 * e + i % 2, b * (SCRATCH[dst][1][1] // 4) + 160 * e
                 mm(bank, 160, k, 128 * b, "l%d" % r, 160 * e)
                 act(R(dst, at, at + 160), R("pb%d" % bank, 0, 160), scale=sc)
-        for b in range(4):
-            mm(6 + b % 2, 320, "g", 128 * b, str(r), 0)
-            act(plane("fp", b), R("pb%d" % (6 + b % 2), 0, 320), scale=0.0078125)
 
     def times(r):
         for st in range(3):
@@ -470,12 +472,10 @@ def rank_program(g, core, T, topo):
         out, came = sent(r, "first", 1)
         ts(out, R("ao", 15, 16), -1.0, O.mult, K(CK), O.add)
         send("af%d" % r, [(came, out)], HOPE)
-        for b in range(4):
-            act(R("f2", 336 * b + 320, 336 * b + 336), pick(plane("f2", b), came))
 
     def order(r):
         c = min(r, 1)
-        strict.append("V")
+        strict.extend("VS")
         for e in range(2):
             tt(half("d0o", e), pick(R("w8"), R("offd", 10 * e, 10 * e + 10)), half("hr%d" % c, e), O.add)
         for e in range(2):
@@ -489,25 +489,33 @@ def rank_program(g, core, T, topo):
             return R("my", 16 * q + 15, 16 * q + 16)
 
         def places(a, b):
-            ts(R("offs", a, b), R("acc", a, b), -0.5, O.mult, 159.5, O.add)
+            ts(R("scn", 3180 + a, 3180 + b), R("acc", a, b), -0.5, O.mult, 159.5, O.add)
 
         def lay(a, b):
-            scatter(R("win"), R("offs", a, b), R("si%d" % c, 16 * a, 16 * b))
+            scatter(R("win"), R("scn", 3180 + a, 3180 + b), R("si%d" % c, 16 * a, 16 * b))
         for q in range(NS):
             act(R("sj", 320 * (q % 2), 320 * (q % 2) + 320), R("kas"), AF.Sign, acc=R("acc", q, q + 1), scale=-1.0, bias=mine(q))
+        for b in range(4):
+            act(R("f2", 336 * b + 320, 336 * b + 336), pick(plane("f2", b), sent(r, "first", 1)[1]))
+        for b in range(4):
+            mm(6 + b % 2, 320, "g", 128 * b, str(r), 0)
+            act(plane("fp", b), R("pb%d" % (6 + b % 2), 0, 320), scale=0.0078125)
         for p in range(NV + 2):
             if p < NV:
-                ts(R("fab", 320 * p, 320 * p + 320), R("ku"), K(CP), O.add, mine(NS + p), O.is_gt)
-            if p == NV:
+                ts(R("fab", 320 * p, 320 * p + 320), R("ku"), R("keep", 0, 1), O.add, mine(NS + p), O.is_gt)
+            if p == AT[0]:
                 places(0, EARLY)
+            if p == AT[1]:
+                lay(0, EARLY)
+            if p == AT[2]:
+                places(EARLY, NS)
             if p >= 2:
                 a = 320 * (p - 2)
-                scan(half("scn", p - 2), R("fab", a, a + 160), R("fab", a + 160, a + 320), -160.0, O.add, O.add)
-        lay(0, EARLY)
-        ts(R("offs", NS, 20), R("scn", 159, 160 * NV, 160), 160.0, O.add)
-        places(EARLY, NS)
+                scan(R("scn", NS + p - 2, 3200, 20), R("fab", a, a + 160), R("fab", a + 160, a + 320), 0.0, O.add, O.add)
+        if AT[2] > NV + 1:
+            places(EARLY, NS)
         lay(EARLY, 20)
-        strict.pop()
+        del strict[:]
 
     def deal(r):
         strict.extend("VS")
@@ -566,8 +574,6 @@ def rank_program(g, core, T, topo):
         act(half("oprow", e), pick(R("ccol"), at))
     for k in range(8):
         dma("Y", T.op[k:k + 1, :], T.oprow[16 * k:16 * k + 1, :], [R("oprow")], [], "doy")
-    diagonal(R("df"), R("natr"))
-    ts(R("nat", 0, 20), R("df", 15, 320, 16), K(CP), O.subtract)
     arrive(2)
     for e in range(2):
         mm(6 + e, 160, "v", 0, "3", 160)

@@ -1,23 +1,23 @@
 from concourse.mybir import dt, AluOpType as O, ActivationFunctionType as AF
 
-NS = 8
+NS = 9
 NV = 20 - NS
-EARLY = 4
-AT = (9, 11, 13)
-TOP = 1023.0
-MISS = float(2 ** 22)
+EARLY = 6
+TOP = 8184.0
+MISS = float(2 ** 13)
 KEEP = float(2 ** 14)
 LOW = -1.0e9
 F4 = "float8_e4m3fn_x4"
 BLOCKS = (0, 1, 2, 3, 0, 0, 1, 1)
 WINDOW = (64, 128, 0)
-LISTS = {"off1": 0, "off2": 16, "kl": 32, "offd": 48, "offs": 80, "nat": 112, "own": 144, "keep": 168}
+LISTS = {"off1": 0, "off2": 16, "kl": 32, "offd": 48, "nat": 80, "own": 112, "keep": 128}
 SENT = {"ll": 0, "first": 16, "mate": 32}
-ROWS = ["hr0", "hr1", "si0", "si1", "ccol", "natr"]
-WIDTH = {"bfloat16": 2, "uint16": 2}
-PIECES = ((0, 6), (6, 10), (10, 16), (16, 20))
-TURNS = 1
-WAKE, LOAD, HOP, HOPE, HOPL, SLACK = 220, 2400, 3000, 3500, 2000, 30
+ROWS = ["hr0", "hr1", "ccol", "natr"]
+WIDTH = {"bfloat16": 2, "uint16": 2, "float16": 2}
+WAKE, LOAD, HOP, HOPE, HOPL, LATE = 200, 2400, 3000, 3500, 2000, 18000
+PLANS = tuple((p, s) for p in (1.0, 1.1, 1.2, 1.3) for s in (10, 30, 50))
+PACES = (1.0, 1.3)
+TURNS = 3
 
 
 def _decl():
@@ -28,14 +28,17 @@ def _decl():
             d[k] = ("sbuf", [128, n], t)
     sb("xt fp gp za", 1280, "bfloat16")
     sb("f2", 1344, "bfloat16")
-    sb("xk xh zt sj", 640, "bfloat16")
+    sb("xk xh zt sj sb", 640, "bfloat16")
     sb("uv cs cd", 1024, "bfloat16")
-    sb("cf eg eh zz", 520, "bfloat16")
-    sb("fa fb", 776, "bfloat16")
-    sb("fab", 320 * 12, "bfloat16")
-    sb("w4 sg4 tgf ixg ixh", 128, "bfloat16")
-    sb("dg dow", 320, "bfloat16")
-    for k, n in (("u", 128), ("v", 128), ("w", 512), ("h", 512), ("g", 512), ("s", 256), ("d", 256), ("c", 256), ("a", 194), ("b", 194), ("n", 320), ("z", 160)):
+    sb("eg zz", 520, "bfloat16")
+    sb("fa fb", 648, "bfloat16")
+    sb("fab", 320 * NV, "bfloat16")
+    sb("w4 sg4 tgf", 128, "bfloat16")
+    sb("ix", 256, "bfloat16")
+    sb("dow win", 320, "bfloat16")
+    sb("inc2 dg dh d4", 160, "bfloat16")
+    sb("kb", 8, "bfloat16")
+    for k, n in (("u", 128), ("v", 128), ("w", 512), ("h", 512), ("g", 512), ("s", 256), ("d", 256), ("c", 256), ("a", 162), ("b", 162), ("n", 320), ("z", 160)):
         d["q" + k] = ("sbuf", [128, n], F4)
         d["p" + k] = ("sbuf", [128, n], "uint8")
     for r in range(4):
@@ -46,19 +49,23 @@ def _decl():
         d["pl%d" % r] = ("sbuf", [128, 320], "uint8")
     sb("out came", 192, "uint16")
     sb("rows", 320 * len(ROWS), "float32")
-    sb("d0o yo oprow kas win", 320, "float32")
-    sb("ku dw df mate dp dn my", 320, "uint16")
+    sb("d0o yo oprow", 320, "float32")
+    sb("ku df dn my", 320, "uint16")
+    sb("dm", 160, "uint16")
     sb("scn", 3200, "uint16")
-    sb("n0 n1 n2 n3 d1 d2 cr0 cr1 mx my2", 200, "float32")
-    sb("d0 inc1 inc2 dl dm", 160, "float32")
-    sb("one", 40, "float32")
-    sb("acc", 20, "float32")
-    sb("tb ta e16", 32, "float32")
+    sb("dw mate dp", 320, "float16")
+    sb("n0 n1 n2 n3 d0 d1 d2 mx my2", 200, "float16")
+    sb("tb ta", 32, "float16")
+    sb("dk cr0 cr1 my3", 200, "float32")
+    sb("wg inc1 dl", 160, "float32")
+    sb("one self", 40, "float32")
+    sb("acc acd", 20, "float32")
+    sb("tc am e16 v16", 32, "float32")
     sb("k", 56, "float32")
-    sb("wt at am ao v16 j16 d16", 16, "float32")
-    sb("mi w8 lx", 16, "int32")
+    sb("wt w8 at ao ap az d16", 16, "float32")
+    sb("mi lx", 16, "int32")
     sb("ci", 48, "int32")
-    sb("lists", 176, "uint16")
+    sb("lists", 144, "uint16")
     for b in range(8):
         d["pb%d" % b] = ("psum", [128, 512], "float32")
     return d
@@ -76,6 +83,7 @@ def rank_program(g, core, T, topo):
     queue = {"V": g.vector, "S": g.scalar, "P": g.tensor, "G": g, "Y": g.sync}
     own = {"V": "sV", "S": "sS", "P": "sP", "G": "sG"}
     calls = []
+    wait = [0]
     strict = []
     count = {}
     clock = {}
@@ -139,10 +147,10 @@ def rank_program(g, core, T, topo):
             h.append([m, kind, sem, v])
 
     def op(q, call, reads, writes, time):
-        calls.append((q, own[q], 1, call, accesses(reads, writes) + [(("turn", 1 + (q == "S")), "w")] * (q in strict), time, WAKE))
+        calls.append((q, own[q], 1, call, accesses(reads, writes) + [(("turn", 1 + (q == "S")), "w")] * (q in strict), time, WAKE, wait[0]))
 
     def dma(q, out, in_, reads, writes, sem):
-        calls.append((q, sem, 16, lambda e: e.dma_start(out, in_), accesses(reads, writes), 60, LOAD))
+        calls.append((q, sem, 16, lambda e: e.dma_start(out, in_), accesses(reads, writes), 60, LOAD, 0))
 
     def send(sem, pairs, hop):
         def call(e):
@@ -154,49 +162,62 @@ def rank_program(g, core, T, topo):
             count[sem] = k
             for out, in_ in pairs:
                 hist.setdefault(out[1][0][0], []).append([out[1][0][1], "w", sem, k])
-        calls.append(("G", None, 0, call, accesses([p[1] for p in pairs], [p[0] for p in pairs]), 300 * len(pairs), hop))
+        calls.append(("G", None, 0, call, accesses([p[1] for p in pairs], [p[0] for p in pairs]), 300 * len(pairs), hop, 0))
 
     def issue():
-        last, before = {}, []
+        last, before, after = {}, [], [{} for c in calls]
         for i, c in enumerate(calls):
             p = {}
             for (b, m), kind in c[4]:
                 for mj, kj, j in last.get(b, []):
                     if mj & m and clash(b, kj, kind, calls[j][0] == c[0]):
-                        p[j] = calls[j][5] + calls[j][6]
+                        p[j] = calls[j][6]
                     elif mj & m and kind == "w":
-                        p.setdefault(j, calls[j][5])
+                        p.setdefault(j, 0)
             for (b, m), kind in c[4]:
                 h = last.setdefault(b, [])
                 if kind == "w":
                     h[:] = [e for e in h if e[0] & ~m]
                 h.append((m, kind, i))
             before.append(p)
-        chain = [c[5] + c[6] for c in calls]
-        after = [{} for c in calls]
-        for i in range(len(calls) - 1, -1, -1):
-            for j, d in before[i].items():
-                chain[j] = max(chain[j], d + chain[i])
-                after[j][i] = calls[i][5] + d - calls[j][5]
+            for j, d in p.items():
+                after[j][i] = d
 
-        def place(urge, links, first):
-            start, busy = {}, {q: [] for q in queue}
+        def place(urge, links, first, pace, slack):
+            end, busy = {}, {q: [] for q in queue}
             for i in sorted(range(len(calls)), key=lambda i: -urge[i]):
-                q, time = calls[i][0], calls[i][5]
-                t = max([start[j] + d for j, d in links[i].items()] + [first[i]])
+                q, time = calls[i][0], calls[i][5] * pace
+                t = max([end[j] + d for j, d in links[i].items()] + [first[i]])
                 at = 0
                 for a, b in busy[q]:
-                    if t < a and t + time <= a + SLACK:
+                    if t < a and t + time <= a + slack:
                         break
                     t = max(t, b)
                     at += 1
-                start[i] = t
+                end[i] = t + time
                 busy[q].insert(at, (t, t + time))
-            return start, [start[i] + c[5] for i, c in enumerate(calls)]
-        start, end = place(chain, before, [0] * len(calls))
-        for _ in range(TURNS):
-            start, end = place(place(end, after, [c[6] for c in calls])[1], before, [0] * len(calls))
-        for i in sorted(start, key=lambda i: (start[i], i)):
+            return end
+
+        def replay(order, pace):
+            end, free = {}, {q: 0 for q in queue}
+            for i in order:
+                q = calls[i][0]
+                end[i] = free[q] = max([free[q]] + [end[j] + d for j, d in before[i].items()]) + calls[i][5] * pace
+            return max(end[i] + calls[i][6] for i in order)
+        best = None
+        for pace, slack in PLANS:
+            urge = [c[5] * pace + c[6] for c in calls]
+            for i in range(len(calls) - 1, -1, -1):
+                for j, d in before[i].items():
+                    urge[j] = max(urge[j], calls[j][5] * pace + d + urge[i])
+            for _ in range(TURNS):
+                end = place(urge, before, [c[7] for c in calls], pace, slack)
+                order = sorted(end, key=lambda i: (end[i] - calls[i][5] * pace, i))
+                cost = sum(replay(order, p) / p for p in PACES)
+                if best is None or cost < best[0]:
+                    best = (cost, order)
+                urge = place(end, after, [c[6] for c in calls], pace, slack)
+        for i in best[1]:
             q, sem, n, call, acc = calls[i][:5]
             waits(q, acc)
             if n:
@@ -206,7 +227,7 @@ def rank_program(g, core, T, topo):
                 call(queue[q])
 
     def cycles(n, *v):
-        full = [x for x in v if x[2] > 1]
+        full = [x for x in v if isinstance(x, tuple)]
         if any(x[3] == 0 for x in full):
             return 50 + 1.3 * n
         return 0.83 * max(64, n / 2 if full and all(x[3] == 2 for x in full) else n)
@@ -216,9 +237,9 @@ def rank_program(g, core, T, topo):
 
     def ts(out, a, s1, o0, s2=None, o1=None):
         if o1 is None:
-            op("V", lambda v: v.tensor_scalar(out[0], a[0], ap(s1), None, o0), [a, s1], [out], cycles(out[2], out, a))
+            op("V", lambda v: v.tensor_scalar(out[0], a[0], ap(s1), None, o0), [a, s1], [out], cycles(out[2], out, a, s1))
         else:
-            op("V", lambda v: v.tensor_scalar(out[0], a[0], ap(s1), ap(s2), o0, o1), [a, s1, s2], [out], cycles(out[2], out, a))
+            op("V", lambda v: v.tensor_scalar(out[0], a[0], ap(s1), ap(s2), o0, o1), [a, s1, s2], [out], cycles(out[2], out, a, s1, s2))
 
     def tt(out, a, b, o):
         both = a[3] and "pb" not in (a[1][0][0][:2], b[1][0][0][:2])
@@ -234,7 +255,7 @@ def rank_program(g, core, T, topo):
         op("V", lambda v: v.memset(out[0], val), [], [out], cycles(out[2], out))
 
     def scan(out, a, b, init, o0, o1):
-        op("V", lambda v: v.tensor_tensor_scan(out[0], a[0], b[0], ap(init), o0, o1), [a, b, init], [out], cycles(out[2], out, a, b))
+        op("V", lambda v: v.tensor_tensor_scan(out[0], a[0], b[0], init, o0, o1), [a, b], [out], cycles(out[2], out, a, b))
 
     def turn(out, a):
         op("V", lambda v: v.transpose(out[0], a[0]), [a], [out], cycles(out[2]))
@@ -265,8 +286,8 @@ def rank_program(g, core, T, topo):
         out = R("pb%d" % bank, 0, n)
         op("P", lambda t: t.matmul_mx(out[0], v[0][0], v[1][0], v[2][0], v[3][0], start, stop), v, [out], 0.5 * (n + 16))
 
-    def diagonal(out, row):
-        scan(out, R("dg", 0, row[2]), row, LOW, O.add, O.max)
+    def diagonal(out, row, steps="dg"):
+        scan(out, R(steps, 0, row[2]), row, LOW, O.add, O.max)
 
     def half(n, e):
         return R(n, 160 * e, 160 * e + 160)
@@ -288,48 +309,43 @@ def rank_program(g, core, T, topo):
     def K(i, n=1):
         return R("k", i, i + n)
     RK, SG, S1, S2, HF, BK, GR, PC, PD, P1, R1 = range(1, 12)
-    RF, GF, PF, LT3, WA, WT, RA, RW, CP, I0, CK, NF = range(12)
-    WM, MK, LA, LB, G4, WH, WI, C8 = 16, 20, 24, 28, 32, 36, 40, 48
+    RF, GF, PF, LT3, WA, WT, RA, RW, CP, W4, NF = range(11)
+    WM, LA, LB, G4, WH, WI, C8 = 16, 24, 28, 32, 36, 40, 48
     iota(ci(0), [[1, 1]], 0, 1)
     iota(ci(P1), [[1, 1]], 1, 1)
     iota(K(G4, 4), [[1, 4]])
-    iota(K(C8, 8), [[1, 8]], 320)
-    iota(R("v16"), [[0, 2], [1, 8]])
-    iota(R("j16"), [[1, 16]])
-    level("one", 0, 40, -1)
+    iota(K(C8, 8), [[1, 8]], 160)
+    iota(R("v16", 0, 16), [[0, 2], [1, 8]])
+    iota(R("v16", 16, 32), [[1, 16]])
+    level("one", 0, 40, -8)
     iota(R("tgf"), [[1, 8], [0, 16]])
-    for i, low in enumerate((-TOP, -TOP, -1, -1)):
-        level("n%d" % i, 160, 193, low)
+    for i, low in ((0, -TOP), (1, -TOP), (3, -1.0)):
+        affine(R("n%d" % i, 160, 193), R("one", 0, 33), 0.0, low)
     level("wt", 8, 16, TOP)
-    level("d1", 162, 193, 0)
-    level("d2", 162, 193, 0)
-    level("cr0", 1, 160, 1)
-    level("cr0", 40, 160, 513, 40)
-    level("n3", 0, 160, 0)
-    level("at", 8, 16, 0)
-    iota(R("ixg"), [[1, 128]])
-    iota(R("ixh"), [[16, 4], [0, 2], [1, 16]])
-    iota(R("ixh", 0, 16), [[1, 16]], 112)
-    iota(R("si0"), [[1, 320]])
-    level("w8", 8, 16, 8 * TOP)
-    iota(R("hr0"), [[-1, 8], [0, 40]], 4103)
-    level("cr1", 1, 160, 1026)
-    level("cr1", 4, 160, -3070, 4)
-    iota(R("si1"), [[1, 2], [2, 160]])
-    iota(R("hr1"), [[-1, 2], [0, 40], [-2, 4]], 4103)
+    level("dk", 162, 193, 0)
+    level("at", 8, 16, -800)
+    level("eg", 0, 520, 0)
+    iota(R("ix", 0, 128), [[1, 128]])
+    iota(R("ix", 128, 256), [[16, 4], [0, 2], [1, 16]])
+    iota(R("ix", 128, 144), [[1, 16]], 112)
+    iota(R("self", 20, 40), [[16, 20]])
+    level("w8", 8, 16, TOP)
+    iota(R("hr0"), [[-1, 8], [0, 40]], 8199)
+    iota(R("sb", 0, 320), [[1, 320]], -160)
+    iota(R("sb", 320, 640), [[1, 2], [2, 160]], -160)
+    iota(R("hr1"), [[-1, 2], [0, 40], [-2, 4]], 8199)
     iota(R("ccol"), [[1, 40], [40, 8]])
     iota(R("natr"), [[1, 8], [8, 40]])
 
     fill(R("zz"), 0.0)
     fill(R("w4"), 0.0)
     fill(R("sg4"), 0.0)
-    for n, a, b in (("fa", 1, 776), ("fa", 640, 776), ("fb", 0, 776), ("fb", 1, 4), ("fb", 645, 776)):
-        out = R(n, a, b, 2)
+    for n, a, b, s in (("fa", 1, 648, 2), ("fa", 640, 648, 2), ("fb", 0, 648, 2), ("fb", 1, 4, 2), ("fb", 645, 648, 2),
+                       ("d0", 162, 193, 1), ("d1", 162, 193, 1), ("d2", 162, 193, 1), ("n3", 0, 160, 1)):
+        out = R(n, a, b, s)
         act(out, R("zz", 0, out[2]))
-    for n in ("cf", "eg", "eh"):
-        act(R(n), R("zz"))
-    fill(R("w4", 0, 64, 4), 1.0)
-    fill(R("w4", 66, 128, 4), 1.0)
+    fill(R("w4", 0, 64, 4), 8.0)
+    fill(R("w4", 66, 128, 4), 8.0)
     ts(ci(RK), ci(0), 15, O.bitwise_and)
     ts(ci(R1), ci(P1), 15, O.bitwise_and)
     ts(ci(GR), ci(0), 4, O.arith_shift_right)
@@ -343,54 +359,64 @@ def rank_program(g, core, T, topo):
     copy(K(GF), ci(GR))
     act(K(RF), ci(RK))
     act(K(NF), ci(R1))
-    act(K(PF), ci(0))
+    act(R("kb", 6, 7), ci(0))
     ts(K(WA), ci(RK), -2.0, O.mult, 4.0, O.add)
     ts(K(LT3), ci(RK), 3.0, O.is_lt)
     ts(K(RA), ci(RK), 0.25, O.mult, 0.25, O.add)
     ts(K(WT), K(WA), 1.0, O.max, K(LT3), O.mult)
     ts(K(RW), ci(RK), -1.0, O.add, K(RA), O.max)
-    ts(K(MK, 4), K(G4, 4), K(GF), O.is_equal, K(LT3), O.mult)
+    ts(R("kb", 0, 4), K(G4, 4), K(GF), O.is_equal, K(LT3), O.mult)
     ts(K(WM, 4), K(G4, 4), K(GF), O.is_equal, K(WT), O.mult)
-    ts(R("ci", 16, 32), R("v16"), K(RW), O.mult, -0.375, O.add)
+    ts(R("ci", 16, 32), R("v16", 0, 16), K(RW), O.mult, -0.375, O.add)
     ts(R("ci", 32, 48), R("ci", 16, 32), 1, O.bitwise_and)
     for at, sign in ((0, 1.0), (1, -1.0), (66, 1.0), (67, -1.0)):
-        affine(R("sg4", at, at + 61, 4), R("ci", 32, 48), -2.0 * MISS * sign, MISS * sign)
+        ts(R("sg4", at, at + 61, 4), R("ci", 32, 48), -2.0 * MISS * sign, O.mult, MISS * sign, O.add)
     for i, b in enumerate(BLOCKS):
         act(R("cs", 128 * i, 128 * i + 128), R("w4"), AF.Identity, scale=K(WM + b))
-        ts(R("cd", 128 * i, 128 * i + 128), R("sg4"), K(MK + b), O.mult)
+        ts(R("cd", 128 * i, 128 * i + 128), R("sg4"), R("kb", b, b + 1), O.mult)
     quant("s", 0, 256, "cs", 0)
     quant("d", 0, 256, "cd", 0)
-    ts(R("cf", 2, 514, 4), R("tgf"), K(GF), O.is_equal, K(WT), O.mult)
+    act(R("kb", 4, 5), K(GF))
+    act(R("kb", 5, 6), K(WT))
+    ts(R("eg", 3, 515, 4), R("tgf"), R("kb", 4, 5), O.is_equal, R("kb", 5, 6), O.mult)
     for e in range(2):
-        quant("c", 128 * e, 128 * e + 128, "cf", 2 - 2 * e)
-    ts(K(I0), ci(PD), -MISS, O.mult, TOP, O.add)
-    affine(R("d1", 161, 162), ci(PD), -MISS, 0.0)
+        quant("c", 128 * e, 128 * e + 128, "eg", 3 - 2 * e)
+    for st in range(3):
+        affine(R("d%d" % st, 161, 162), ci(PD), -2 * MISS, 0.0)
     ts(K(CP), ci(RK), 15.0, O.is_lt, KEEP, O.mult)
-    affine(K(CK), K(CP), 1.0, 511.0)
-    act(R("keep", 0, 1), K(CP))
-    ts(R("e16", 0, 16), R("j16"), K(RF), O.is_equal, -4.0 * KEEP, O.mult)
-    ts(R("e16", 16, 32), R("j16"), K(NF), O.is_equal, KEEP, O.mult)
+    affine(R("keep", 0, 1), K(CP), 3.0 / KEEP, 1.0)
+    affine(K(W4), K(CP), -3.0 / KEEP, -1.0)
+    ts(R("e16", 0, 16), R("v16", 16, 32), K(RF), O.is_equal, -4.0 * KEEP, O.mult)
+    ts(R("e16", 16, 32), R("v16", 16, 32), K(NF), O.is_equal, KEEP, O.mult)
     tt(R("d16"), R("e16", 0, 16), R("e16", 16, 32), O.add)
-    affine(R("own", 0, 20), R("one", 0, 20), 0.0, K(RF))
-    act(R("dg"), pick(R("d16"), R("own", 0, 20)))
-    for i, (src, least, unit, one) in enumerate(((BK, 2.0, 1.0, 0.0), (BK, 1.0, 1.0, 0.0), (GR, 1.0, 0.125, 1.0))):
-        ts(K(LA + i), ci(src), least, O.is_ge, unit, O.mult)
+    affine(R("own", 0, 10), R("one", 0, 10), 0.0, K(RF))
+    act(R("dg"), pick(R("d16"), R("own", 0, 10)))
+    act(R("dh"), R("dg"), scale=2.0 ** -5)
+    act(R("d4"), R("dg"), AF.Relu, scale=3.0 / KEEP, bias=1.0)
+    affine(K(PF), K(CP), 2.0 ** -5, -160.0)
+    affine(R("self", 0, 20), R("self", 20, 40), 1.0, K(RF))
+    for i, (src, least, one) in enumerate(((BK, 2.0, 0.0), (BK, 1.0, 1.0), (GR, 1.0, 1.0))):
+        ts(K(LA + i), ci(src), least, O.is_ge, 0.125, O.mult)
         ts(K(WH + i), ci(src), least, O.is_lt, 8.0 + one, O.mult)
         affine(K(WI + i), K(LA + i), K(CP), one)
         affine(K(LB + i), K(WI + i), -1.0, K(WH + i))
-    for r, (e, end) in enumerate(((2208.0, 4095.0 - 552 * 3 - 39), (513.0, 4095.0 - 8 * 39 - 1026 * 3))):
+    for r, (e, end, step, every, jump) in enumerate(((1888, 3584 - 472 * 3 + 39, -1, 40, 511), (511, 3584 + 8 * 39 - 1022 * 3, 1022, 4, -3074))):
+        wait[0] = LATE * r
         n = "cr%d" % r
-        affine(R(n, 0, 1), ci(HF), e, -4095.0)
-        affine(R(n, 160, 161), ci(HF), -e, end)
+        affine(R(n, 1, 160), R("zz", 1, 160), 1.0, step / 512)
+        affine(R(n, every, 160, every), R("zz", every, 160, every), 1.0, jump / 512)
+        affine(R(n, 0, 1), ci(HF), e / 512, -7.0)
+        affine(R(n, 160, 161), ci(HF), -e / 512, end / 512)
         affine(R(n, 161, 162), ci(PD), -MISS, 0.0)
-    ts(R("eg", 3, 515, 4), R("ixg"), K(PF), O.is_equal, 128.0, O.mult)
-    ts(R("eh", 3, 515, 4), R("ixh"), K(PF), O.is_equal)
     for e in range(2):
         diagonal(half("dn", e), half("natr", e))
     ts(R("nat", 0, 20), R("dn", 15, 320, 16), K(CP), O.subtract)
-    for k in "gh":
+    quant("v", 0, 128, "uv", 512)
+    wait[0] = 0
+    for k, at, val in (("h", 128, 1.0), ("g", 0, 128.0)):
+        ts(R("eg", 3, 515, 4), R("ix", at, at + 128), R("kb", 6, 7), O.is_equal, val, O.mult)
         for b in range(4):
-            quant(k, 128 * b, 128 * b + 128, "e" + k, 3 - b)
+            quant(k, 128 * b, 128 * b + 128, "eg", 3 - b)
 
     def stack(name, r, h, at=0):
         return R(name, at + 40 * h, at + 40 * h + 40) if r == 0 else R(name, at + h, at + 160, 4)
@@ -409,39 +435,56 @@ def rank_program(g, core, T, topo):
         at = 64 * r + SENT[name]
         return R("out", at, at + n), R("came", at, at + n)
 
+    def stage(r, st):
+        n = "n%d" % st
+        if st:
+            act(R("wg"), pick(R("wt"), R("off%d" % st, 0, 10)), AF.Abs)
+        for h in range(4):
+            if st:
+                scan(stack(n, r, h), stack("wg", r, h), stack("inc%d" % st, r, h), -LOW, O.min, O.subtract)
+            else:
+                scan(stack(n, r, h), R("one"), stack("pb0", r, h), TOP, O.add, O.subtract)
+        scan(R("mx", 0, 193), R("d%d" % st, 0, 193), R(n, 0, 193), -60000.0, O.add, O.max)
+        turn(R("tb"), R("mx", 161, 193))
+        tt(R("w8" if st == 2 else "wt", 0, 8), R("tb", 0, 8), R("tb", 16, 24), O.max)
+
     def symbols(r):
-        c = min(r, 1)
-        quant("a", 0, 160 if r else 194, "fa", 0)
-        quant("b", 0, 162 if r else 194, "fb", 0)
+        quant("a", 0, 160 if r else 162, "fa", 0)
+        quant("b", 0, 162, "fb", 0)
         for st in range(3):
             mm(2 * st, 160, "s", WINDOW[st], "a", 0)
-            mm(2 * st + 1, 162 if st else 194, "d", WINDOW[st], "a", 0, True, False)
-            mm(2 * st + 1, 162 if st else 194, "d", WINDOW[st], "b", 0, False, True)
+            mm(2 * st + 1, 162, "d", WINDOW[st], "a", 0, True, False)
+            mm(2 * st + 1, 162, "d", WINDOW[st], "b", 0, False, True)
         for e in range(2):
             mm(6 + e, 160, "c", 128 * e, "a", 0)
+        diagonal(R("dl"), R("pb2", 0, 160))
+        listed("off1", 10, "dl", 0)
+        for st in range(3):
+            act(R("d%d" % st, 0, 161), R("pb%d" % (2 * st + 1), 0, 161), scale=2.0)
+            if st:
+                affine(R("inc%d" % st), R("pb%d" % (2 * st), 0, 160), 1.0, 8.0)
+        for e in range(2):
             affine(half("dow", e), R("pb%d" % (6 + e), 0, 160), 8.0, 8.0)
             diagonal(half("df", e), half("dow", e))
         listed("offd", 20, "df", 2)
-        diagonal(R("dl"), R("pb2", 0, 160))
-        listed("off1", 10, "dl", 0)
-        affine(R("inc1"), R("pb2", 0, 160), 1.0, 1.0)
-        act(R("d1", 0, 161), R("pb3", 0, 161))
-        diagonal(R("dm"), R("pb4", 0, 160))
+        diagonal(R("dm"), R("inc2"))
         listed("off2", 10, "dm", 1)
-        affine(R("inc2"), R("pb4", 0, 160), 4096.0, 4096.0)
-        tt(R("d2", 0, 162), R("pb5", 0, 162), R("cr%d" % c, 0, 162), O.add)
-        scan(R("my2", 0, 193), R("d2", 0, 193), R("n3", 0, 193), LOW, O.add, O.max)
+        tt(R("dk", 0, 162), R("pb5", 0, 162), R("cr%d" % min(r, 1), 0, 162), O.add)
+        scan(R("my2", 0, 193), R("d2", 0, 193), R("n3", 0, 193), -60000.0, O.add, O.max)
         turn(R("ta"), R("my2", 161, 193))
-        tt(R("am", 0, 8), R("ta", 0, 8), R("ta", 16, 24), O.max)
-        ts(R("am", 8, 16), R("am", 0, 8), 0.0, O.is_ge)
-        tt(R("at", 0, 8), R("am", 8, 16), K(C8, 8), O.mult)
-        for a, b in PIECES:
-            e = a // 10
-            out = R("mate", 32 * a - 319 * e, 32 * b - 319 * e - 1, 2) if r else R("mate", 16 * a, 16 * b)
-            tt(out, pick(R("at"), R("offd", a, b)), R("si%d" % c, 16 * a, 16 * b), O.max)
-        diagonal(R("dp"), R("mate"))
+        tt(R("am", 0, 16), R("ta", 0, 16), R("ta", 16, 32), O.max)
+        ts(R("am", 16, 24), R("am", 0, 8), 1000.0, O.mult, 200.0, O.add)
+        tt(R("at", 0, 8), R("am", 16, 24), K(C8, 8), O.min)
+        diagonal(R("az"), R("am", 0, 16))
+        ts(R("am", 24, 25), R("az", 15, 16), K(CP), O.is_lt, -TOP / 4, O.mult)
+        ts(R("n2", 160, 193), R("one", 0, 33), R("am", 24, 25), O.mult, -TOP, O.add)
+        for e in range(2):
+            act(R("mate", e, 320, 2) if r else half("mate", e), pick(R("at"), R("offd", 10 * e, 10 * e + 10)))
+        for e in range(2):
+            diagonal(half("dp", e), half("mate", e), "dh")
         out, came = sent(r, "mate", 20)
-        ts(out, R("dp", 15, 320, 16), K(CP), O.subtract)
+        ts(R("acd"), R("dp", 15, 320, 16), K(PF), O.subtract)
+        tt(out, R("acd"), R("self", 0, 20), O.max)
         send("ab%d" % r, [(came, out)], HOPE)
 
     def decode(r):
@@ -454,23 +497,15 @@ def rank_program(g, core, T, topo):
 
     def times(r):
         for st in range(3):
-            n = "n%d" % st
-            if st:
-                act(R("d0"), pick(R("wt"), R("off%d" % st, 0, 10)), AF.Abs, scale=(1.0, 4096.0)[st - 1])
-            for h in range(4):
-                if st:
-                    scan(stack(n, r, h), stack("d0", r, h), stack("inc%d" % st, r, h), -LOW, O.min, O.subtract)
-                else:
-                    scan(stack(n, r, h), R("one"), stack("pb0", r, h), K(I0), O.add, O.subtract)
-            scan(R("mx", 0, 193), R(("pb1", "d1", "d2")[st], 0, 193), R(n, 0, 193), LOW, O.add, O.max)
-            turn(R("tb"), R("mx", 161, 193))
-            w = 16 if st == 2 else 8
-            tt(R("mi" if st == 2 else "wt", 0, w), R("tb", 0, w), R("tb", 16, 16 + w), O.max)
-        ts(R("w8", 0, 8), R("mi", 0, 8), 9, O.arith_shift_right, 0x1FF8, O.bitwise_and)
+            stage(r, st)
+        scan(R("my3", 0, 193), R("dk", 0, 193), R("n2", 0, 193), LOW, O.add, O.max)
+        turn(R("tc"), R("my3", 161, 193))
+        tt(R("ap"), R("tc", 0, 16), R("tc", 16, 32), O.max)
+        act(R("mi"), R("ap"), scale=512.0)
         ts(R("lx"), R("mi"), 511, O.bitwise_and)
         diagonal(R("ao"), R("lx"))
         out, came = sent(r, "first", 1)
-        ts(out, R("ao", 15, 16), -1.0, O.mult, K(CK), O.add)
+        ts(out, R("ao", 15, 16), K(CP), O.subtract, 319.0, O.min)
         send("af%d" % r, [(came, out)], HOPE)
 
     def order(r):
@@ -481,9 +516,8 @@ def rank_program(g, core, T, topo):
         for e in range(2):
             for h in range(4):
                 scan(stack("ku", r, h, 160 * e), stack("d0o", r, h, 160 * e), stack("dow", r, h, 160 * e), -LOW, O.min, O.subtract)
-            affine(half("kas", e), half("ku", e), 1.0, K(CP))
         for e in range(2):
-            diagonal(half("my", e), half("ku", e))
+            scan(half("my", e), R("d4"), half("ku", e), 0.0, O.mult, O.max)
 
         def mine(q):
             return R("my", 16 * q + 15, 16 * q + 16)
@@ -492,39 +526,36 @@ def rank_program(g, core, T, topo):
             ts(R("scn", 3180 + a, 3180 + b), R("acc", a, b), -0.5, O.mult, 159.5, O.add)
 
         def lay(a, b):
-            scatter(R("win"), R("scn", 3180 + a, 3180 + b), R("si%d" % c, 16 * a, 16 * b))
+            scatter(R("win"), R("scn", 3180 + a, 3180 + b), R("sb", 320 * c + 16 * a, 320 * c + 16 * b))
         for q in range(NS):
-            act(R("sj", 320 * (q % 2), 320 * (q % 2) + 320), R("kas"), AF.Sign, acc=R("acc", q, q + 1), scale=-1.0, bias=mine(q))
+            act(R("sj", 320 * (q % 2), 320 * (q % 2) + 320), R("ku"), AF.Sign, acc=R("acc", q, q + 1), scale=K(W4), bias=mine(q))
         for b in range(4):
             act(R("f2", 336 * b + 320, 336 * b + 336), pick(plane("f2", b), sent(r, "first", 1)[1]))
         for b in range(4):
-            mm(6 + b % 2, 320, "g", 128 * b, str(r), 0)
-            act(plane("fp", b), R("pb%d" % (6 + b % 2), 0, 320), scale=0.0078125)
+            mm(4 + b, 320, "g", 128 * b, str(r), 0)
+            act(plane("fp", b), R("pb%d" % (4 + b), 0, 320), scale=0.0078125)
         for p in range(NV + 2):
             if p < NV:
-                ts(R("fab", 320 * p, 320 * p + 320), R("ku"), R("keep", 0, 1), O.add, mine(NS + p), O.is_gt)
-            if p == AT[0]:
+                ts(R("fab", 320 * p, 320 * p + 320), R("ku"), R("keep", 0, 1), O.mult, mine(NS + p), O.is_gt)
+            if p == NV - 1:
                 places(0, EARLY)
-            if p == AT[1]:
+            if p == NV:
                 lay(0, EARLY)
-            if p == AT[2]:
-                places(EARLY, NS)
             if p >= 2:
                 a = 320 * (p - 2)
                 scan(R("scn", NS + p - 2, 3200, 20), R("fab", a, a + 160), R("fab", a + 160, a + 320), 0.0, O.add, O.add)
-        if AT[2] > NV + 1:
-            places(EARLY, NS)
+        places(EARLY, NS)
         lay(EARLY, 20)
         del strict[:]
 
     def deal(r):
         strict.extend("VS")
         for e in range(2):
-            diagonal(half("dw", e), half("win", e))
+            diagonal(half("dw", e), half("win", e), "dh")
         ll, came = sent(r, "ll", 10)
-        ts(ll, R("dw", 15, 160, 16), K(CP), O.subtract)
+        ts(ll, R("dw", 15, 160, 16), K(PF), O.subtract)
         send("al%d" % r, [(came, ll)], HOPL)
-        ts(R("kl", 0, 10), R("dw", 175, 320, 16), K(CP), O.subtract)
+        ts(R("kl", 0, 10), R("dw", 175, 320, 16), K(PF), O.subtract)
         for b in range(4):
             tt(plane("za", b), pick(plane("f2", b, 336), sent(r, "mate", 20)[1]), plane("gp", b), O.add)
             act(R("xk", b, 640, 4), pick(plane("fp", b), R("kl", 0, 10)))
@@ -547,7 +578,6 @@ def rank_program(g, core, T, topo):
         quant(str(r + 1), 160, 320, "xh", 0)
 
     quant("u", 0, 128, "uv", 0)
-    quant("v", 0, 128, "uv", 512)
     for e in range(2):
         quant("0", 160 * e, 160 * e + 160, "xt", 640 * e)
         mm(e, 160, "u", 0, "0", 160 * e)

from concourse.mybir import dt, AluOpType as O, ActivationFunctionType as AF

NS = 9
NV = 20 - NS
EARLY = 6
TOP = 8184.0
MISS = float(2 ** 13)
KEEP = float(2 ** 14)
LOW = -1.0e9
F4 = "float8_e4m3fn_x4"
BLOCKS = (0, 1, 2, 3, 0, 0, 1, 1)
WINDOW = (64, 128, 0)
LISTS = {"off1": 0, "off2": 16, "kl": 32, "offd": 48, "nat": 80, "own": 112, "keep": 128}
SENT = {"ll": 0, "first": 16, "mate": 32}
ROWS = ["hr0", "hr1", "ccol", "natr"]
WIDTH = {"bfloat16": 2, "uint16": 2, "float16": 2}
WAKE, LOAD, HOP, HOPE, HOPL, LATE = 200, 2400, 3000, 3500, 2000, 18000
PLANS = tuple((p, s) for p in (1.0, 1.1, 1.2, 1.3) for s in (10, 30, 50))
PACES = (1.0, 1.3)
TURNS = 3


def _decl():
    d = {}

    def sb(names, n, t):
        for k in names.split():
            d[k] = ("sbuf", [128, n], t)
    sb("xt fp gp za", 1280, "bfloat16")
    sb("f2", 1344, "bfloat16")
    sb("xk xh zt sj sb", 640, "bfloat16")
    sb("uv cs cd", 1024, "bfloat16")
    sb("eg zz", 520, "bfloat16")
    sb("fa fb", 648, "bfloat16")
    sb("fab", 320 * NV, "bfloat16")
    sb("w4 sg4 tgf", 128, "bfloat16")
    sb("ix", 256, "bfloat16")
    sb("dow win", 320, "bfloat16")
    sb("inc2 dg dh d4", 160, "bfloat16")
    sb("kb", 8, "bfloat16")
    for k, n in (("u", 128), ("v", 128), ("w", 512), ("h", 512), ("g", 512), ("s", 256), ("d", 256), ("c", 256), ("a", 162), ("b", 162), ("n", 320), ("z", 160)):
        d["q" + k] = ("sbuf", [128, n], F4)
        d["p" + k] = ("sbuf", [128, n], "uint8")
    for r in range(4):
        d["q%d" % r] = ("sbuf", [128, 320], F4)
        d["p%d" % r] = ("sbuf", [128, 320], "uint8")
    for r in range(3):
        d["ql%d" % r] = ("sbuf", [128, 320], F4)
        d["pl%d" % r] = ("sbuf", [128, 320], "uint8")
    sb("out came", 192, "uint16")
    sb("rows", 320 * len(ROWS), "float32")
    sb("d0o yo oprow", 320, "float32")
    sb("ku df dn my", 320, "uint16")
    sb("dm", 160, "uint16")
    sb("scn", 3200, "uint16")
    sb("dw mate dp", 320, "float16")
    sb("n0 n1 n2 n3 d0 d1 d2 mx my2", 200, "float16")
    sb("tb ta", 32, "float16")
    sb("dk cr0 cr1 my3", 200, "float32")
    sb("wg inc1 dl", 160, "float32")
    sb("one self", 40, "float32")
    sb("acc acd", 20, "float32")
    sb("tc am e16 v16", 32, "float32")
    sb("k", 56, "float32")
    sb("wt w8 at ao ap az d16", 16, "float32")
    sb("mi lx", 16, "int32")
    sb("ci", 48, "int32")
    sb("lists", 144, "uint16")
    for b in range(8):
        d["pb%d" % b] = ("psum", [128, 512], "float32")
    return d


SCRATCH = _decl()
SEMAPHORES = ["sV", "sS", "sP", "sG", "dx0", "dx1", "du", "dw", "dws", "dv", "loc", "doy", "doa"] + [k % r for r in range(3) for k in ("ax%d0", "ax%d1", "af%d", "al%d", "ab%d")]


def rank_program(g, core, T, topo):
    rank = T.rank_of(core)
    if rank is None:
        return
    nxt = T.cores[(rank + 1) % len(T.cores)]
    queue = {"V": g.vector, "S": g.scalar, "P": g.tensor, "G": g, "Y": g.sync}
    own = {"V": "sV", "S": "sS", "P": "sP", "G": "sG"}
    calls = []
    wait = [0]
    strict = []
    count = {}
    clock = {}
    known = {k: {} for k in queue}
    hist = {}

    def R(name, a=0, b=None, s=1):
        if name in LISTS:
            name, a, b = "lists", LISTS[name] + a, LISTS[name] + b
        if name in ROWS:
            at = 320 * ROWS.index(name)
            name, a, b = "rows", at + a, at + (320 if b is None else b)
        b = SCRATCH[name][1][1] if b is None else b
        m = 0
        for c in range(a, b, s):
            m |= 1 << c
        if name[:2] == "pb":
            m = 1
        return (T[name][:, a:b:s] if s > 1 else T[name][:, a:b], [(name, m)], len(range(a, b, s)), WIDTH.get(SCRATCH[name][2], 4))

    def pick(win, off):
        return (win[0].indirect(off[0]), win[1] + off[1], 16 * off[2], 0)

    def cast(v, t):
        return (v[0].bitcast(t),) + v[1:]

    def accesses(reads, writes):
        r = [a for v in reads if isinstance(v, tuple) for a in v[1]]
        return [(a, "p" if a[0][:2] == "pb" else "r") for a in r] + [(a, "w") for v in writes for a in v[1]]

    def clash(b, k0, k1, same):
        if b == "turn" or (k0 == "r" and k1 == "r"):
            return False
        return not (b[:2] == "pb" and k0 == k1 and same)

    def waits(q, acc):
        need = {}
        for (b, m), kind in acc:
            for e in hist.get(b, []):
                if e[0] & m and clash(b, e[1], kind, own.get(q) == e[2]):
                    need[e[2]] = max(need.get(e[2], 0), e[3])
        kn = known[q]
        for s in sorted(need, key=lambda s: -need[s]):
            if kn.get(s, 0) >= need[s]:
                continue
            queue[q].wait_ge(T.sem[s], need[s])
            for k, v in clock.get((s, need[s]), {}).items():
                kn[k] = max(kn.get(k, 0), v)
            kn[s] = max(kn.get(s, 0), need[s])

    def record(q, sem, n, acc):
        count[sem] = count.get(sem, 0) + n
        v = count[sem]
        clock[(sem, v)] = dict(known[q])
        for (b, m), kind in acc:
            h = hist.setdefault(b, [])
            if kind == "r":
                h[:] = [e for e in h if not (e[1] == "r" and e[2] == sem and not e[0] & ~m)]
            else:
                h[:] = [e for e in h if e[0] & ~m]
            h.append([m, kind, sem, v])

    def op(q, call, reads, writes, time):
        calls.append((q, own[q], 1, call, accesses(reads, writes) + [(("turn", 1 + (q == "S")), "w")] * (q in strict), time, WAKE, wait[0]))

    def dma(q, out, in_, reads, writes, sem):
        calls.append((q, sem, 16, lambda e: e.dma_start(out, in_), accesses(reads, writes), 60, LOAD, 0))

    def send(sem, pairs, hop):
        def call(e):
            rid, pid, _ = topo.addr(nxt)
            for out, in_ in pairs:
                e.remote_dma(out[0], in_[0], T.sem[sem], T.sem["loc"], pid, rid, topo.mask(core, nxt))
            k = len(pairs) * len(topo.engines(core, nxt))
            count["loc"] = count.get("loc", 0) + k
            count[sem] = k
            for out, in_ in pairs:
                hist.setdefault(out[1][0][0], []).append([out[1][0][1], "w", sem, k])
        calls.append(("G", None, 0, call, accesses([p[1] for p in pairs], [p[0] for p in pairs]), 300 * len(pairs), hop, 0))

    def issue():
        last, before, after = {}, [], [{} for c in calls]
        for i, c in enumerate(calls):
            p = {}
            for (b, m), kind in c[4]:
                for mj, kj, j in last.get(b, []):
                    if mj & m and clash(b, kj, kind, calls[j][0] == c[0]):
                        p[j] = calls[j][6]
                    elif mj & m and kind == "w":
                        p.setdefault(j, 0)
            for (b, m), kind in c[4]:
                h = last.setdefault(b, [])
                if kind == "w":
                    h[:] = [e for e in h if e[0] & ~m]
                h.append((m, kind, i))
            before.append(p)
            for j, d in p.items():
                after[j][i] = d

        def place(urge, links, first, pace, slack):
            end, busy = {}, {q: [] for q in queue}
            for i in sorted(range(len(calls)), key=lambda i: -urge[i]):
                q, time = calls[i][0], calls[i][5] * pace
                t = max([end[j] + d for j, d in links[i].items()] + [first[i]])
                at = 0
                for a, b in busy[q]:
                    if t < a and t + time <= a + slack:
                        break
                    t = max(t, b)
                    at += 1
                end[i] = t + time
                busy[q].insert(at, (t, t + time))
            return end

        def replay(order, pace):
            end, free = {}, {q: 0 for q in queue}
            for i in order:
                q = calls[i][0]
                end[i] = free[q] = max([free[q]] + [end[j] + d for j, d in before[i].items()]) + calls[i][5] * pace
            return max(end[i] + calls[i][6] for i in order)
        best = None
        for pace, slack in PLANS:
            urge = [c[5] * pace + c[6] for c in calls]
            for i in range(len(calls) - 1, -1, -1):
                for j, d in before[i].items():
                    urge[j] = max(urge[j], calls[j][5] * pace + d + urge[i])
            for _ in range(TURNS):
                end = place(urge, before, [c[7] for c in calls], pace, slack)
                order = sorted(end, key=lambda i: (end[i] - calls[i][5] * pace, i))
                cost = sum(replay(order, p) / p for p in PACES)
                if best is None or cost < best[0]:
                    best = (cost, order)
                urge = place(end, after, [c[6] for c in calls], pace, slack)
        for i in best[1]:
            q, sem, n, call, acc = calls[i][:5]
            waits(q, acc)
            if n:
                call(queue[q]).then_inc(T.sem[sem], n)
                record(q, sem, n, acc)
            else:
                call(queue[q])

    def cycles(n, *v):
        full = [x for x in v if isinstance(x, tuple)]
        if any(x[3] == 0 for x in full):
            return 50 + 1.3 * n
        return 0.83 * max(64, n / 2 if full and all(x[3] == 2 for x in full) else n)

    def ap(v):
        return v[0] if isinstance(v, tuple) else v

    def ts(out, a, s1, o0, s2=None, o1=None):
        if o1 is None:
            op("V", lambda v: v.tensor_scalar(out[0], a[0], ap(s1), None, o0), [a, s1], [out], cycles(out[2], out, a, s1))
        else:
            op("V", lambda v: v.tensor_scalar(out[0], a[0], ap(s1), ap(s2), o0, o1), [a, s1, s2], [out], cycles(out[2], out, a, s1, s2))

    def tt(out, a, b, o):
        both = a[3] and "pb" not in (a[1][0][0][:2], b[1][0][0][:2])
        op("V", lambda v: v.tensor_tensor(out[0], a[0], b[0], o), [a, b], [out], cycles(2 * out[2]) if both else cycles(out[2], a))

    def copy(out, a):
        op("V", lambda v: v.tensor_copy(out[0], a[0]), [a], [out], cycles(out[2], out, a))

    def scatter(win, off, a):
        op("V", lambda v: v.tensor_copy(win[0].indirect(off[0]), a[0]), [a, off], [win], 50 + 3.2 * a[2])

    def fill(out, val):
        op("V", lambda v: v.memset(out[0], val), [], [out], cycles(out[2], out))

    def scan(out, a, b, init, o0, o1):
        op("V", lambda v: v.tensor_tensor_scan(out[0], a[0], b[0], init, o0, o1), [a, b], [out], cycles(out[2], out, a, b))

    def turn(out, a):
        op("V", lambda v: v.transpose(out[0], a[0]), [a], [out], cycles(out[2]))

    def act(out, a, f=AF.Copy, acc=None, **kw):
        more = {k: ap(v) for k, v in kw.items()}
        if acc:
            more["accum_out"] = acc[0]
        op("S", lambda s: s.activation(out[0], a[0], f, **more), [a] + list(kw.values()), [out] + ([acc] if acc else []),
           (cycles(out[2]) if a[3] else 65 + 1.3 * out[2]) + (20 if acc else 0))

    def affine(out, a, scale, bias):
        act(out, a, AF.Identity, scale=scale, bias=bias)

    def iota(out, pat, base=0, cm=0):
        more = {} if SCRATCH[out[1][0][0]][2] == "int32" else {"allow_small_or_imprecise_dtypes": True}
        op("G", lambda e: e.iota(out[0], pat, base, cm, **more), [], [out], 130 + 1.66 * out[2])

    def level(name, a, b, val, s=1):
        iota(R(name, a, b, s), [[0, len(range(a, b, s))]], int(val))

    def quant(k, a, b, tile, lo):
        q, p, t = R("q" + k, a, b), R("p" + k, a, b), R(tile, lo, lo + 4 * (b - a))
        op("V", lambda v: v.quantize_mx(q[0], p[0], t[0]), [t], [q, p], 12 + 0.22 * t[2])

    def mm(bank, n, k, a, m, b, start=True, stop=True):
        v = [R("q" + k, a, a + 128), R("p" + k, a, a + 128), R("q" + m, b, b + n), R("p" + m, b, b + n)]
        out = R("pb%d" % bank, 0, n)
        op("P", lambda t: t.matmul_mx(out[0], v[0][0], v[1][0], v[2][0], v[3][0], start, stop), v, [out], 0.5 * (n + 16))

    def diagonal(out, row, steps="dg"):
        scan(out, R(steps, 0, row[2]), row, LOW, O.add, O.max)

    def half(n, e):
        return R(n, 160 * e, 160 * e + 160)

    def plane(n, b, w=320):
        a = b * (SCRATCH[n][1][1] // 4)
        return R(n, a, a + w)

    for e in range(2):
        dma("Y", T.xt[:, 640 * e:640 * e + 640], T.x[:, 640 * e:640 * e + 640], [], [R("xt", 640 * e, 640 * e + 640)], "dx%d" % e)
    dma("S", T.uv[:, 0:512], T.u[:], [], [R("uv", 0, 512)], "du")
    dma("Y", T.qw[:].bitcast(dt.uint8), T.wc[:], [R("xt")], [R("qw")], "dw")
    dma("Y", T.pw[:], T.ws[:], [R("xt")], [R("pw")], "dws")
    dma("Y", T.uv[:, 512:1024], T.v[:], [R("xt")], [R("uv", 512, 1024)], "dv")

    def ci(i):
        return R("ci", i, i + 1)

    def K(i, n=1):
        return R("k", i, i + n)
    RK, SG, S1, S2, HF, BK, GR, PC, PD, P1, R1 = range(1, 12)
    RF, GF, PF, LT3, WA, WT, RA, RW, CP, W4, NF = range(11)
    WM, LA, LB, G4, WH, WI, C8 = 16, 24, 28, 32, 36, 40, 48
    iota(ci(0), [[1, 1]], 0, 1)
    iota(ci(P1), [[1, 1]], 1, 1)
    iota(K(G4, 4), [[1, 4]])
    iota(K(C8, 8), [[1, 8]], 160)
    iota(R("v16", 0, 16), [[0, 2], [1, 8]])
    iota(R("v16", 16, 32), [[1, 16]])
    level("one", 0, 40, -8)
    iota(R("tgf"), [[1, 8], [0, 16]])
    for i, low in ((0, -TOP), (1, -TOP), (3, -1.0)):
        affine(R("n%d" % i, 160, 193), R("one", 0, 33), 0.0, low)
    level("wt", 8, 16, TOP)
    level("dk", 162, 193, 0)
    level("at", 8, 16, -800)
    level("eg", 0, 520, 0)
    iota(R("ix", 0, 128), [[1, 128]])
    iota(R("ix", 128, 256), [[16, 4], [0, 2], [1, 16]])
    iota(R("ix", 128, 144), [[1, 16]], 112)
    iota(R("self", 20, 40), [[16, 20]])
    level("w8", 8, 16, TOP)
    iota(R("hr0"), [[-1, 8], [0, 40]], 8199)
    iota(R("sb", 0, 320), [[1, 320]], -160)
    iota(R("sb", 320, 640), [[1, 2], [2, 160]], -160)
    iota(R("hr1"), [[-1, 2], [0, 40], [-2, 4]], 8199)
    iota(R("ccol"), [[1, 40], [40, 8]])
    iota(R("natr"), [[1, 8], [8, 40]])

    fill(R("zz"), 0.0)
    fill(R("w4"), 0.0)
    fill(R("sg4"), 0.0)
    for n, a, b, s in (("fa", 1, 648, 2), ("fa", 640, 648, 2), ("fb", 0, 648, 2), ("fb", 1, 4, 2), ("fb", 645, 648, 2),
                       ("d0", 162, 193, 1), ("d1", 162, 193, 1), ("d2", 162, 193, 1), ("n3", 0, 160, 1)):
        out = R(n, a, b, s)
        act(out, R("zz", 0, out[2]))
    fill(R("w4", 0, 64, 4), 8.0)
    fill(R("w4", 66, 128, 4), 8.0)
    ts(ci(RK), ci(0), 15, O.bitwise_and)
    ts(ci(R1), ci(P1), 15, O.bitwise_and)
    ts(ci(GR), ci(0), 4, O.arith_shift_right)
    ts(ci(SG), ci(0), 7, O.bitwise_and)
    ts(ci(S1), ci(0), 7, O.bitwise_and, 1, O.arith_shift_right)
    ts(ci(S2), ci(0), 7, O.bitwise_and, 2, O.arith_shift_right)
    ts(ci(HF), ci(0), 16, O.bitwise_and, 4, O.arith_shift_right)
    ts(ci(BK), ci(0), 5, O.arith_shift_right)
    tt(ci(PC), ci(SG), ci(S1), O.subtract)
    tt(ci(PD), ci(PC), ci(S2), O.subtract)
    copy(K(GF), ci(GR))
    act(K(RF), ci(RK))
    act(K(NF), ci(R1))
    act(R("kb", 6, 7), ci(0))
    ts(K(WA), ci(RK), -2.0, O.mult, 4.0, O.add)
    ts(K(LT3), ci(RK), 3.0, O.is_lt)
    ts(K(RA), ci(RK), 0.25, O.mult, 0.25, O.add)
    ts(K(WT), K(WA), 1.0, O.max, K(LT3), O.mult)
    ts(K(RW), ci(RK), -1.0, O.add, K(RA), O.max)
    ts(R("kb", 0, 4), K(G4, 4), K(GF), O.is_equal, K(LT3), O.mult)
    ts(K(WM, 4), K(G4, 4), K(GF), O.is_equal, K(WT), O.mult)
    ts(R("ci", 16, 32), R("v16", 0, 16), K(RW), O.mult, -0.375, O.add)
    ts(R("ci", 32, 48), R("ci", 16, 32), 1, O.bitwise_and)
    for at, sign in ((0, 1.0), (1, -1.0), (66, 1.0), (67, -1.0)):
        ts(R("sg4", at, at + 61, 4), R("ci", 32, 48), -2.0 * MISS * sign, O.mult, MISS * sign, O.add)
    for i, b in enumerate(BLOCKS):
        act(R("cs", 128 * i, 128 * i + 128), R("w4"), AF.Identity, scale=K(WM + b))
        ts(R("cd", 128 * i, 128 * i + 128), R("sg4"), R("kb", b, b + 1), O.mult)
    quant("s", 0, 256, "cs", 0)
    quant("d", 0, 256, "cd", 0)
    act(R("kb", 4, 5), K(GF))
    act(R("kb", 5, 6), K(WT))
    ts(R("eg", 3, 515, 4), R("tgf"), R("kb", 4, 5), O.is_equal, R("kb", 5, 6), O.mult)
    for e in range(2):
        quant("c", 128 * e, 128 * e + 128, "eg", 3 - 2 * e)
    for st in range(3):
        affine(R("d%d" % st, 161, 162), ci(PD), -2 * MISS, 0.0)
    ts(K(CP), ci(RK), 15.0, O.is_lt, KEEP, O.mult)
    affine(R("keep", 0, 1), K(CP), 3.0 / KEEP, 1.0)
    affine(K(W4), K(CP), -3.0 / KEEP, -1.0)
    ts(R("e16", 0, 16), R("v16", 16, 32), K(RF), O.is_equal, -4.0 * KEEP, O.mult)
    ts(R("e16", 16, 32), R("v16", 16, 32), K(NF), O.is_equal, KEEP, O.mult)
    tt(R("d16"), R("e16", 0, 16), R("e16", 16, 32), O.add)
    affine(R("own", 0, 10), R("one", 0, 10), 0.0, K(RF))
    act(R("dg"), pick(R("d16"), R("own", 0, 10)))
    act(R("dh"), R("dg"), scale=2.0 ** -5)
    act(R("d4"), R("dg"), AF.Relu, scale=3.0 / KEEP, bias=1.0)
    affine(K(PF), K(CP), 2.0 ** -5, -160.0)
    affine(R("self", 0, 20), R("self", 20, 40), 1.0, K(RF))
    for i, (src, least, one) in enumerate(((BK, 2.0, 0.0), (BK, 1.0, 1.0), (GR, 1.0, 1.0))):
        ts(K(LA + i), ci(src), least, O.is_ge, 0.125, O.mult)
        ts(K(WH + i), ci(src), least, O.is_lt, 8.0 + one, O.mult)
        affine(K(WI + i), K(LA + i), K(CP), one)
        affine(K(LB + i), K(WI + i), -1.0, K(WH + i))
    for r, (e, end, step, every, jump) in enumerate(((1888, 3584 - 472 * 3 + 39, -1, 40, 511), (511, 3584 + 8 * 39 - 1022 * 3, 1022, 4, -3074))):
        wait[0] = LATE * r
        n = "cr%d" % r
        affine(R(n, 1, 160), R("zz", 1, 160), 1.0, step / 512)
        affine(R(n, every, 160, every), R("zz", every, 160, every), 1.0, jump / 512)
        affine(R(n, 0, 1), ci(HF), e / 512, -7.0)
        affine(R(n, 160, 161), ci(HF), -e / 512, end / 512)
        affine(R(n, 161, 162), ci(PD), -MISS, 0.0)
    for e in range(2):
        diagonal(half("dn", e), half("natr", e))
    ts(R("nat", 0, 20), R("dn", 15, 320, 16), K(CP), O.subtract)
    quant("v", 0, 128, "uv", 512)
    wait[0] = 0
    for k, at, val in (("h", 128, 1.0), ("g", 0, 128.0)):
        ts(R("eg", 3, 515, 4), R("ix", at, at + 128), R("kb", 6, 7), O.is_equal, val, O.mult)
        for b in range(4):
            quant(k, 128 * b, 128 * b + 128, "eg", 3 - b)

    def stack(name, r, h, at=0):
        return R(name, at + 40 * h, at + 40 * h + 40) if r == 0 else R(name, at + h, at + 160, 4)

    def flags(bank, at, step):
        for n, a in (("fa", at), ("fb", at + 5)):
            ts(R(n, a, a + 160 * step - 1, step), R("pb%d" % bank, 0, 160), 0.0, O.is_gt)

    def listed(off, n, row, i):
        ts(R(off, 0, n), R(row, 15, 16 * n, 16), K(LA + i), O.mult, K(LB + i), O.add)

    def state(r, e):
        send("ax%d%d" % (r, e), [(cast(half("ql%d" % r, e), dt.uint8), cast(half("q%d" % r, e), dt.uint8)), (half("pl%d" % r, e), half("p%d" % r, e))], HOP)

    def sent(r, name, n):
        at = 64 * r + SENT[name]
        return R("out", at, at + n), R("came", at, at + n)

    def stage(r, st):
        n = "n%d" % st
        if st:
            act(R("wg"), pick(R("wt"), R("off%d" % st, 0, 10)), AF.Abs)
        for h in range(4):
            if st:
                scan(stack(n, r, h), stack("wg", r, h), stack("inc%d" % st, r, h), -LOW, O.min, O.subtract)
            else:
                scan(stack(n, r, h), R("one"), stack("pb0", r, h), TOP, O.add, O.subtract)
        scan(R("mx", 0, 193), R("d%d" % st, 0, 193), R(n, 0, 193), -60000.0, O.add, O.max)
        turn(R("tb"), R("mx", 161, 193))
        tt(R("w8" if st == 2 else "wt", 0, 8), R("tb", 0, 8), R("tb", 16, 24), O.max)

    def symbols(r):
        quant("a", 0, 160 if r else 162, "fa", 0)
        quant("b", 0, 162, "fb", 0)
        for st in range(3):
            mm(2 * st, 160, "s", WINDOW[st], "a", 0)
            mm(2 * st + 1, 162, "d", WINDOW[st], "a", 0, True, False)
            mm(2 * st + 1, 162, "d", WINDOW[st], "b", 0, False, True)
        for e in range(2):
            mm(6 + e, 160, "c", 128 * e, "a", 0)
        diagonal(R("dl"), R("pb2", 0, 160))
        listed("off1", 10, "dl", 0)
        for st in range(3):
            act(R("d%d" % st, 0, 161), R("pb%d" % (2 * st + 1), 0, 161), scale=2.0)
            if st:
                affine(R("inc%d" % st), R("pb%d" % (2 * st), 0, 160), 1.0, 8.0)
        for e in range(2):
            affine(half("dow", e), R("pb%d" % (6 + e), 0, 160), 8.0, 8.0)
            diagonal(half("df", e), half("dow", e))
        listed("offd", 20, "df", 2)
        diagonal(R("dm"), R("inc2"))
        listed("off2", 10, "dm", 1)
        tt(R("dk", 0, 162), R("pb5", 0, 162), R("cr%d" % min(r, 1), 0, 162), O.add)
        scan(R("my2", 0, 193), R("d2", 0, 193), R("n3", 0, 193), -60000.0, O.add, O.max)
        turn(R("ta"), R("my2", 161, 193))
        tt(R("am", 0, 16), R("ta", 0, 16), R("ta", 16, 32), O.max)
        ts(R("am", 16, 24), R("am", 0, 8), 1000.0, O.mult, 200.0, O.add)
        tt(R("at", 0, 8), R("am", 16, 24), K(C8, 8), O.min)
        diagonal(R("az"), R("am", 0, 16))
        ts(R("am", 24, 25), R("az", 15, 16), K(CP), O.is_lt, -TOP / 4, O.mult)
        ts(R("n2", 160, 193), R("one", 0, 33), R("am", 24, 25), O.mult, -TOP, O.add)
        for e in range(2):
            act(R("mate", e, 320, 2) if r else half("mate", e), pick(R("at"), R("offd", 10 * e, 10 * e + 10)))
        for e in range(2):
            diagonal(half("dp", e), half("mate", e), "dh")
        out, came = sent(r, "mate", 20)
        ts(R("acd"), R("dp", 15, 320, 16), K(PF), O.subtract)
        tt(out, R("acd"), R("self", 0, 20), O.max)
        send("ab%d" % r, [(came, out)], HOPE)

    def decode(r):
        for e in range(2):
            for i in range(8):
                k, dst, b, sc = ("g", "gp", i - 4, 2.0 ** -8) if i >= 4 else ("h", "f2", i, 0.5)
                bank, at = 2 + 2 * e + i % 2, b * (SCRATCH[dst][1][1] // 4) + 160 * e
                mm(bank, 160, k, 128 * b, "l%d" % r, 160 * e)
                act(R(dst, at, at + 160), R("pb%d" % bank, 0, 160), scale=sc)

    def times(r):
        for st in range(3):
            stage(r, st)
        scan(R("my3", 0, 193), R("dk", 0, 193), R("n2", 0, 193), LOW, O.add, O.max)
        turn(R("tc"), R("my3", 161, 193))
        tt(R("ap"), R("tc", 0, 16), R("tc", 16, 32), O.max)
        act(R("mi"), R("ap"), scale=512.0)
        ts(R("lx"), R("mi"), 511, O.bitwise_and)
        diagonal(R("ao"), R("lx"))
        out, came = sent(r, "first", 1)
        ts(out, R("ao", 15, 16), K(CP), O.subtract, 319.0, O.min)
        send("af%d" % r, [(came, out)], HOPE)

    def order(r):
        c = min(r, 1)
        strict.extend("VS")
        for e in range(2):
            tt(half("d0o", e), pick(R("w8"), R("offd", 10 * e, 10 * e + 10)), half("hr%d" % c, e), O.add)
        for e in range(2):
            for h in range(4):
                scan(stack("ku", r, h, 160 * e), stack("d0o", r, h, 160 * e), stack("dow", r, h, 160 * e), -LOW, O.min, O.subtract)
        for e in range(2):
            scan(half("my", e), R("d4"), half("ku", e), 0.0, O.mult, O.max)

        def mine(q):
            return R("my", 16 * q + 15, 16 * q + 16)

        def places(a, b):
            ts(R("scn", 3180 + a, 3180 + b), R("acc", a, b), -0.5, O.mult, 159.5, O.add)

        def lay(a, b):
            scatter(R("win"), R("scn", 3180 + a, 3180 + b), R("sb", 320 * c + 16 * a, 320 * c + 16 * b))
        for q in range(NS):
            act(R("sj", 320 * (q % 2), 320 * (q % 2) + 320), R("ku"), AF.Sign, acc=R("acc", q, q + 1), scale=K(W4), bias=mine(q))
        for b in range(4):
            act(R("f2", 336 * b + 320, 336 * b + 336), pick(plane("f2", b), sent(r, "first", 1)[1]))
        for b in range(4):
            mm(4 + b, 320, "g", 128 * b, str(r), 0)
            act(plane("fp", b), R("pb%d" % (4 + b), 0, 320), scale=0.0078125)
        for p in range(NV + 2):
            if p < NV:
                ts(R("fab", 320 * p, 320 * p + 320), R("ku"), R("keep", 0, 1), O.mult, mine(NS + p), O.is_gt)
            if p == NV - 1:
                places(0, EARLY)
            if p == NV:
                lay(0, EARLY)
            if p >= 2:
                a = 320 * (p - 2)
                scan(R("scn", NS + p - 2, 3200, 20), R("fab", a, a + 160), R("fab", a + 160, a + 320), 0.0, O.add, O.add)
        places(EARLY, NS)
        lay(EARLY, 20)
        del strict[:]

    def deal(r):
        strict.extend("VS")
        for e in range(2):
            diagonal(half("dw", e), half("win", e), "dh")
        ll, came = sent(r, "ll", 10)
        ts(ll, R("dw", 15, 160, 16), K(PF), O.subtract)
        send("al%d" % r, [(came, ll)], HOPL)
        ts(R("kl", 0, 10), R("dw", 175, 320, 16), K(PF), O.subtract)
        for b in range(4):
            tt(plane("za", b), pick(plane("f2", b, 336), sent(r, "mate", 20)[1]), plane("gp", b), O.add)
            act(R("xk", b, 640, 4), pick(plane("fp", b), R("kl", 0, 10)))
        for b in range(4):
            (copy if b // 2 else act)(R("zt", b, 640, 4), pick(plane("za", b), came))
        quant(str(r + 1), 0, 160, "xk", 0)
        quant("z", 0, 160, "zt", 0)
        del strict[:]

    def arrive(r):
        for b in range(4):
            mm(2 + b, 160, "w", 128 * b, "z", 0, True, False)
            mm(2 + b, 160, "g", 128 * b, "z", 0, False, True)
        for b in range(4):
            out, pb = R("xh", b, 640, 4), R("pb%d" % (2 + b), 0, 160)
            if b % 2:
                ts(out, pb, 0.0078125, O.mult)
            else:
                act(out, pb, scale=0.0078125)
        quant(str(r + 1), 160, 320, "xh", 0)

    quant("u", 0, 128, "uv", 0)
    for e in range(2):
        quant("0", 160 * e, 160 * e + 160, "xt", 640 * e)
        mm(e, 160, "u", 0, "0", 160 * e)
        flags(e, 2 * e, 4)
        state(0, e)
    for r in range(3):
        symbols(r)
        decode(r)
        times(r)
        order(r)
        deal(r)
        if r < 2:
            state(r + 1, 0)
            mm(0, 160, "u", 0, str(r + 1), 0)
            flags(0, 0, 2)
            arrive(r)
            state(r + 1, 1)
            mm(1, 160, "u", 0, str(r + 1), 160)
            flags(1, 320, 2)
    mm(0, 160, "v", 0, "3", 0)
    for h in range(8):
        act(R("yo", 40 * h, 40 * h + 20), R("pb0", h, 160, 8))
    for e, at in enumerate((sent(2, "ll", 10)[0], R("kl", 0, 10))):
        act(half("oprow", e), pick(R("ccol"), at))
    for k in range(8):
        dma("Y", T.op[k:k + 1, :], T.oprow[16 * k:16 * k + 1, :], [R("oprow")], [], "doy")
    arrive(2)
    for e in range(2):
        mm(6 + e, 160, "v", 0, "3", 160)
    act(R("pn"), pick(R("p3"), R("nat", 0, 20)))
    copy(cast(R("qn"), dt.uint32), pick(cast(R("q3"), dt.uint32), R("nat", 0, 20)))
    dma("Y", T.oc[:], T.qn[:].bitcast(dt.uint8), [R("qn")], [], "doy")
    for h in range(8):
        (act if h % 2 else copy)(R("yo", 40 * h + 20, 40 * h + 40), R("pb%d" % (6 + h % 2), h, 160, 8))
    for k in range(4):
        dma("Y", T.osc[4 * k:4 * k + 4, :], T.pn[32 * k:32 * k + 4, :], [R("pn")], [], "doy")
    dma("S", T.y[:], T.yo[:], [R("yo")], [], "doa")
    issue()
    for s in sorted(count):
        if known["G"].get(s, 0) < count[s]:
            g.wait_ge(T.sem[s], count[s])
